import numpy as np
import ml_dtypes


def mxq(x, axis, fmt="e4m3"):
    dtype, down = {"e4m3": (ml_dtypes.float8_e4m3fn, 7), "e5m2": (ml_dtypes.float8_e5m2, 14)}[fmt]
    v = np.moveaxis(np.asarray(x, np.float32).astype(ml_dtypes.bfloat16).astype(np.float64), axis, -1)
    blocks = v.reshape(v.shape[:-1] + (-1, 32))
    amax = np.abs(blocks).max(-1, keepdims=True)
    byte = np.maximum(np.where(amax > 0, np.frexp(amax)[1] - 1 + 127, 0) - down, 1)
    scale = np.exp2(byte - 127.0)
    codes = (blocks / scale).astype(np.float32).astype(dtype).astype(np.float64)
    return np.moveaxis((codes * scale).reshape(v.shape), -1, axis)


WIDE = False


def mx_kscale(k):
    if not WIDE:
        return np.ones(k)
    levels = np.array([10, -10, 5, -5, 0])
    if k % 512:
        return np.exp2(np.random.permutation(np.resize(levels, k // 32))).repeat(32)
    a = np.empty((k // 512, 16))
    for p in range(k // 512):
        a[p, :8] = np.random.permutation(np.resize(levels, 8))
        for g in range(8):
            far = levels[np.abs(levels - a[p, g]) >= 10]
            a[p, g + 8] = far[np.random.randint(len(far))]
    return np.exp2(a.ravel()).repeat(32)


def f64(x):
    return np.asarray(x).astype(np.float64)


def striped(idx):
    return np.tile(idx.reshape(-1, 16).T, (8, 1)).astype(np.uint16)


def unstriped(offs):
    return offs[:16].T.reshape(-1).astype(np.int64)


E2M1 = np.array([0.0, 0.5, 1.0, 1.5, 2.0, 3.0, 4.0, 6.0, -0.0, -0.5, -1.0, -1.5, -2.0, -3.0, -4.0, -6.0])


def pack_weight(w, fmt):
    k, n = w.shape
    w = f64(np.asarray(w, np.float32).astype(ml_dtypes.bfloat16)).reshape(k // 32, 32, n)
    amax = np.abs(w).max(1)
    if fmt == "e4m3":
        byte = np.frexp(amax)[1] - 1 + 127 - 7
    else:
        mant, ex = np.frexp(amax / 6.0)
        byte = np.where(mant > 0.5, ex, ex - 1) + 127
    byte = np.clip(np.where(amax > 0, byte, 1), 1, 254)
    scaled = (w * np.exp2(127.0 - byte)[:, None, :]).reshape(k, n).astype(np.float32)
    by_word = np.ascontiguousarray(scaled.reshape(k // 512, 128, 4, n).transpose(0, 1, 3, 2))
    if fmt == "e4m3":
        words = by_word.astype(ml_dtypes.float8_e4m3fn).view(np.uint8)
    else:
        c = by_word.astype(ml_dtypes.float4_e2m1fn).view(np.uint8) & 0xF
        words = (c[..., 0::2] | (c[..., 1::2] << 4)).reshape(k // 512, 128, 2 * n)
    return np.ascontiguousarray(words), np.ascontiguousarray(byte.astype(np.uint8).reshape(k // 512, 16, n))


def unpack_weight(words, scales, fmt):
    g, _, n = scales.shape
    words = np.ascontiguousarray(words).reshape(g, 128, n, -1)
    if fmt == "e4m3":
        vals = words.view(ml_dtypes.float8_e4m3fn).astype(np.float64)
    else:
        nib = np.empty((g, 128, n, 4), np.uint8)
        nib[..., 0::2] = words & 0xF
        nib[..., 1::2] = words >> 4
        vals = E2M1[nib]
    vals = vals * np.repeat(np.exp2(scales.astype(np.float64) - 127.0), 8, axis=1)[..., None]
    return vals.transpose(0, 1, 3, 2).reshape(g * 512, n)


def gelu(v):
    return 0.5 * v * (1.0 + np.tanh(np.sqrt(2.0 / np.pi) * (v + 0.044715 * v**3)))


K, H, N, T, S = 1536, 1024, 512, 2048, 1024

def setup_inputs():
    n = np.random.standard_normal
    s = mx_kscale(K)[:, None]
    u = mx_kscale(H)[:, None]
    tab_words, tab_scales = pack_weight(n((K, T)) * s, "e4m3")
    w1 = n((K, H)) / np.sqrt(K) / s * u.T
    cub = np.random.uniform(0.05, 0.25, H) / u[:, 0] ** 2
    w4_words, w4_scales = pack_weight(n((H, N)) / np.sqrt(H) / u, "e2m1")
    return {
        "tab_words": tab_words, "tab_scales": tab_scales,
        "offs": striped(np.random.permutation(T)[:S]),
        "gT": n((N, T)).astype(np.float32),
        "w1": w1.astype(np.float32),
        "cub": cub.astype(np.float32),
        "w4_words": w4_words, "w4_scales": w4_scales,
        "step": np.random.uniform(0.3, 0.9, N).astype(np.float32),
    }

def reference(tab_words, tab_scales, offs, gT, w1, cub, w4_words, w4_scales, step):
    v = unpack_weight(tab_words, tab_scales, "e4m3")[:, unstriped(offs)]
    h = mxq(f64(w1), 0, "e4m3").T @ v
    z = h + f64(cub)[:, None] * (h * h * h)
    w4 = unpack_weight(w4_words, w4_scales, "e2m1")
    y = w4.T @ mxq(z, 0, "e4m3")
    g = f64(gT)[:, unstriped(offs)]
    new = g + f64(step)[:, None] * y
    out = f64(gT).copy()
    out[:, unstriped(offs)] = new
    return out

@@ -1,0 +1,203 @@
+from contextlib import ExitStack
+
+import concourse.mybir as mybir
+
+K, H, N, T, S = 1536, 1024, 512, 2048, 1024
+FLOPS = 2 * K * H * S + 2 * H * N * S
+
+F32 = mybir.dt.float32
+BF16 = mybir.dt.bfloat16
+I32 = mybir.dt.int32
+U32 = mybir.dt.uint32
+U16 = mybir.dt.uint16
+U8 = mybir.dt.uint8
+FP8X4 = mybir.dt.float8_e4m3fn_x4
+FP4X4 = mybir.dt.float4_e2m1fn_x4
+ACT = mybir.ActivationFunctionType
+ALU = mybir.AluOpType
+P = 128
+QW = 256
+NB = 8
+ZI = 4
+
+
+def tile_list_oven_tray_refresh_kernel(tc, tab_words, tab_scales, offs, gT, w1, cub, w4_words, w4_scales, step, out):
+    nc = tc.nc
+    with ExitStack() as ctx:
+        keep = ctx.enter_context(tc.tile_pool(name="keep", bufs=1))
+        ring = ctx.enter_context(tc.tile_pool(name="ring", bufs=3))
+        psum = ctx.enter_context(tc.psum_pool(name="psum", bufs=1))
+
+        offsets = keep.tile([P, S // 16], U16, name="offsets")
+        nc.sync.dma_start(offsets[:], offs)
+
+        tscale = keep.tile([P, T], U8, name="tscale", align_bytes=64)
+        nc.vector.memset(tscale[:].bitcast(I32), 0)
+        for Q in range(4):
+            nc.scalar.dma_start(tscale[32 * Q : 32 * Q + 12, :].bitcast(I32), tab_scales[:, 4 * Q : 4 * Q + 4, :].bitcast(I32))
+        w4s = keep.tile([P, 2, N], U8, name="w4s", align_bytes=64)
+        nc.vector.memset(w4s[:].rearrange("p b n -> p (b n)").bitcast(I32), 0)
+
+        cub_sb = keep.tile([P, 2, 4], F32, name="cub_sb")
+        step_sb = keep.tile([P, 4], F32, name="step_sb")
+        nc.scalar.dma_start(cub_sb[:], cub.rearrange("(b p t) -> p b t", b=2, t=4))
+        with nc.allow_non_contiguous_dma(reason="one step value a partition"):
+            nc.scalar.dma_start(step_sb[:], step.rearrange("(i p) -> p i", p=P))
+
+        twords = [keep.tile([P, T], U32, name="twords%d" % a, align_bytes=64) for a in range(3)]
+        state = [keep.tile([P, T], F32, name="state%d" % i, align_bytes=64) for i in range(4)]
+        wraw = {}
+        w4w = keep.tile([P, 2, 2 * N], U8, name="w4w", align_bytes=64)
+        for item in [("t", 0), ("w", 0, 0), ("w", 1, 0), ("t", 1), ("w", 2, 0), ("t", 2), ("w", 0, 1), ("w", 1, 1), ("w", 2, 1), ("w4",), ("g", 0), ("g", 1), ("g", 2), ("g", 3)]:
+            if item[0] == "w":
+                a, b = item[1], item[2]
+                wraw[a, b] = keep.tile([P, 4, 512], F32, name="wraw%d%d" % (a, b), align_bytes=64)
+                nc.sync.dma_start(wraw[a, b][:], w1[512 * a : 512 * a + 512, 512 * b : 512 * b + 512].rearrange("(p j) c -> p j c", j=4))
+            elif item[0] == "t":
+                a = item[1]
+                nc.sync.dma_start(twords[a][:].bitcast(I32), tab_words[a].rearrange("p t i -> p (t i)").bitcast(I32))
+            elif item[0] == "g":
+                i = item[1]
+                nc.sync.dma_start(state[i][:], gT[P * i : P * i + P, :])
+            else:
+                nc.sync.dma_start(w4w[:].bitcast(I32), w4_words.rearrange("b p c -> p b c").bitcast(I32))
+                for Q in range(4):
+                    nc.sync.dma_start(w4s[32 * Q : 32 * Q + 4, :, :].bitcast(I32), w4_scales[:, 4 * Q : 4 * Q + 4, :].rearrange("b r n -> r b n").bitcast(I32))
+
+        vwords = [keep.tile([P, S], U32, name="vwords%d" % a, align_bytes=64) for a in range(3)]
+        vscale = keep.tile([P, S], U8, name="vscale", align_bytes=64)
+        picked = [keep.tile([P, S], F32, name="picked%d" % i, align_bytes=64) for i in range(4)]
+        wb, wcodes, wscale, zcodes, zscale = {}, {}, {}, {}, {}
+        used = []
+
+        def new_bank(shape):
+            n = len(used)
+            used.append(n)
+            return psum.tile(shape, F32, name="bank%d" % n, tag="bank%d" % (n % NB))
+
+        def gather_scales():
+            nc.vector.tensor_copy(vscale[:], tscale[:].indirect(offsets[:]))
+
+        def gather_words(a, lo=0, hi=4):
+            nc.vector.tensor_copy(vwords[a][:, QW * lo : QW * hi], twords[a][:].indirect(offsets[:, 16 * lo : 16 * hi]))
+
+        def gather_state(i, lo=0, hi=4):
+            nc.vector.tensor_copy(picked[i][:, QW * lo : QW * hi], state[i][:].indirect(offsets[:, 16 * lo : 16 * hi]))
+
+        def cast(a, b, eng="s"):
+            wb[a, b] = ring.tile([P, 2048], BF16, name="wb", tag="wb", align_bytes=64)
+            dst = wb[a, b][:].rearrange("p (t m j) -> p m j t", t=4, j=4)
+            src = wraw[a, b][:].rearrange("p j (m t) -> p m j t", t=4)
+            if eng == "s":
+                nc.scalar.activation(dst, src, ACT.Copy)
+            else:
+                nc.vector.tensor_copy(dst, src)
+
+        def quant_w(a, b):
+            wcodes[a, b] = keep.tile([P, 512], U32, name="wcodes%d%d" % (a, b), align_bytes=64)
+            wscale[a, b] = keep.tile([P, 512], U8, name="wscale%d%d" % (a, b), align_bytes=64)
+            nc.vector.quantize_mx(out=wcodes[a, b][:].bitcast(FP8X4), scales=wscale[a, b][:], in_=wb[a, b][:])
+
+        def unit(q, b):
+            sq = ring.tile([P, 4, QW], F32, name="sq", tag="sq", align_bytes=64)
+            fac = ring.tile([P, 4, QW], F32, name="fac", tag="fac", align_bytes=64)
+            zb = ring.tile([P, 4 * QW], BF16, name="zb", tag="zb", align_bytes=64)
+            banks = []
+            for u in range(2):
+                bank = new_bank([P, 4, P])
+                banks.append(bank)
+                cols = slice(QW * q + P * u, QW * q + P * u + P)
+                for t in range(4):
+                    for a in range(3):
+                        nc.tensor.matmul_mx(
+                            out=bank[:, t, :],
+                            lhsT=wcodes[a, b][:, P * t : P * t + P].bitcast(FP8X4),
+                            lhsT_scale=wscale[a, b][:, P * t : P * t + P],
+                            rhs=vwords[a][:, cols].bitcast(FP8X4),
+                            rhs_scale=vscale[4 * a : P, cols],
+                            start=(a == 0),
+                            stop=(a == 2),
+                        )
+                nc.scalar.activation(sq[:, :, P * u : P * u + P], bank[:], ACT.Square)
+            for t in range(4):
+                nc.scalar.activation(fac[:, t, :], sq[:, t, :], ACT.Copy, bias=1.0, scale=cub_sb[:, b, t : t + 1])
+            for u in range(2):
+                nc.vector.tensor_tensor(
+                    zb[:, 512 * u : 512 * u + 512].rearrange("p (c i t) -> p c t i", i=ZI, t=4),
+                    banks[u][:].rearrange("p t (c i) -> p c t i", i=ZI),
+                    fac[:, :, P * u : P * u + P].rearrange("p t (c i) -> p c t i", i=ZI),
+                    ALU.mult,
+                )
+            zcodes[q, b] = keep.tile([P, QW], U32, name="zcodes%d%d" % (q, b), align_bytes=64)
+            zscale[q, b] = keep.tile([P, QW], U8, name="zscale%d%d" % (q, b), align_bytes=64)
+            nc.vector.quantize_mx(out=zcodes[q, b][:].bitcast(FP8X4), scales=zscale[q, b][:], in_=zb[:])
+
+        moved = [keep.tile([P, S], F32, name="moved%d" % i, align_bytes=64) for i in range(4)]
+
+        def drive(q):
+            for pair in range(2):
+                bank = new_bank([P, 2, QW])
+                for e in range(2):
+                    i = 2 * pair + e
+                    for u in range(2):
+                        for b in range(2):
+                            nc.tensor.matmul_mx(
+                                out=bank[:, e, P * u : P * u + P],
+                                lhsT=w4w[:, b, 2 * P * i : 2 * P * i + 2 * P].bitcast(FP4X4),
+                                lhsT_scale=w4s[:, b, P * i : P * i + P],
+                                rhs=zcodes[q, b][:, P * u : P * u + P].bitcast(FP8X4),
+                                rhs_scale=zscale[q, b][:, P * u : P * u + P],
+                                start=(b == 0),
+                                stop=(b == 1),
+                            )
+                for e in range(2):
+                    i = 2 * pair + e
+                    nc.scalar.activation(moved[i][:, QW * q : QW * q + QW], bank[:, e, :], ACT.Copy, scale=step_sb[:, i : i + 1])
+
+        def put(lo, hi):
+            for i in range(4):
+                nc.vector.tensor_tensor(
+                    state[i][:].indirect(offsets[:, 16 * lo : 16 * hi]),
+                    picked[i][:, QW * lo : QW * hi],
+                    moved[i][:, QW * lo : QW * hi],
+                    ALU.add,
+                )
+                if hi == 4:
+                    nc.sync.dma_start(out[P * i : P * i + P, :], state[i][:])
+
+        gather_words(0)
+        cast(0, 0)
+        gather_scales()
+        quant_w(0, 0)
+        cast(1, 0)
+        gather_words(1)
+        quant_w(1, 0)
+        cast(2, 0)
+        quant_w(2, 0)
+        gather_words(2, 0, 2)
+        gather_words(2, 2, 4)
+        unit(0, 0)
+        cast(0, 1, "s")
+        quant_w(0, 1)
+        unit(1, 0)
+        cast(1, 1, "v")
+        quant_w(1, 1)
+        cast(2, 1, "v")
+        quant_w(2, 1)
+        unit(0, 1)
+        drive(0)
+        unit(1, 1)
+        unit(2, 0)
+        for i in range(4):
+            gather_state(i, 0, 2)
+        put(0, 1)
+        unit(2, 1)
+        unit(3, 0)
+        unit(3, 1)
+        drive(1)
+        for i in range(4):
+            gather_state(i, 2, 4)
+        put(1, 2)
+        drive(2)
+        drive(3)
+        put(2, 4)

@@ -15,189 +15,196 @@ FP8X4 = mybir.dt.float8_e4m3fn_x4
 FP4X4 = mybir.dt.float4_e2m1fn_x4
 ACT = mybir.ActivationFunctionType
 ALU = mybir.AluOpType
+
 P = 128
-QW = 256
-NB = 8
-ZI = 4
+PACK = 4
+PASS = P * PACK
+K_PASSES = K // PASS
+R_PASSES = H // PASS
+N_TILES = N // P
+QUADRANT = 32
+QUARTERS = 4
+QUARTER = S // QUARTERS
+LIST_COLS = QUARTER // 16
+RUN = 2
+RING = 3
+VECTOR_CAST_PASS = 1
 
 
 def tile_list_oven_tray_refresh_kernel(tc, tab_words, tab_scales, offs, gT, w1, cub, w4_words, w4_scales, step, out):
     nc = tc.nc
     with ExitStack() as ctx:
         keep = ctx.enter_context(tc.tile_pool(name="keep", bufs=1))
-        ring = ctx.enter_context(tc.tile_pool(name="ring", bufs=3))
+        ring = ctx.enter_context(tc.tile_pool(name="ring", bufs=RING))
         psum = ctx.enter_context(tc.psum_pool(name="psum", bufs=1))
 
         offsets = keep.tile([P, S // 16], U16, name="offsets")
+        tab_s = keep.tile([P, T], U8, name="tab_s", align_bytes=64)
+        nc.gpsimd.memset(tab_s[:].bitcast(I32), 0)
+        w4_s = keep.tile([P, R_PASSES, N], U8, name="w4_s", align_bytes=64)
+        nc.vector.memset(w4_s[:].rearrange("p b n -> p (b n)").bitcast(I32), 0)
+        cub_sb = keep.tile([P, R_PASSES, PACK], F32, name="cub_sb")
+        step_sb = keep.tile([P, N_TILES], F32, name="step_sb")
+        tab_w = [keep.tile([P, T], U32, name="tab_w%d" % a, align_bytes=64) for a in range(K_PASSES)]
+        state = [keep.tile([P, T], F32, name="state%d" % i, align_bytes=64) for i in range(N_TILES)]
+        w4_w = keep.tile([P, R_PASSES, 2 * N], U8, name="w4_w", align_bytes=64)
+        w1_raw = {}
+
+        def load_table(a):
+            nc.sync.dma_start(tab_w[a][:].bitcast(I32), tab_words[a].rearrange("p t i -> p (t i)").bitcast(I32))
+
+        def load_w1(a, b):
+            w1_raw[a, b] = keep.tile([P, PACK, PASS], F32, name="w1_raw%d%d" % (a, b), align_bytes=64)
+            rows = w1[PASS * a : PASS * (a + 1), PASS * b : PASS * (b + 1)]
+            nc.sync.dma_start(w1_raw[a, b][:], rows.rearrange("(p j) c -> p j c", j=PACK))
+
+        def load_state(i):
+            nc.sync.dma_start(state[i][:], gT[P * i : P * (i + 1), :])
+
+        load_table(0)
         nc.sync.dma_start(offsets[:], offs)
-
-        tscale = keep.tile([P, T], U8, name="tscale", align_bytes=64)
-        nc.vector.memset(tscale[:].bitcast(I32), 0)
-        for Q in range(4):
-            nc.scalar.dma_start(tscale[32 * Q : 32 * Q + 12, :].bitcast(I32), tab_scales[:, 4 * Q : 4 * Q + 4, :].bitcast(I32))
-        w4s = keep.tile([P, 2, N], U8, name="w4s", align_bytes=64)
-        nc.vector.memset(w4s[:].rearrange("p b n -> p (b n)").bitcast(I32), 0)
-
-        cub_sb = keep.tile([P, 2, 4], F32, name="cub_sb")
-        step_sb = keep.tile([P, 4], F32, name="step_sb")
-        nc.scalar.dma_start(cub_sb[:], cub.rearrange("(b p t) -> p b t", b=2, t=4))
+        load_w1(0, 0)
+        for Q in range(P // QUADRANT):
+            nc.sync.dma_start(
+                tab_s[QUADRANT * Q : QUADRANT * Q + 4 * K_PASSES, :].bitcast(I32),
+                tab_scales[:, 4 * Q : 4 * Q + 4, :].bitcast(I32),
+            )
+        for a in range(1, K_PASSES):
+            load_table(a)
+            load_w1(a, 0)
+        nc.sync.dma_start(cub_sb[:], cub.rearrange("(b p t) -> p b t", b=R_PASSES, t=PACK))
+        load_w1(0, 1)
+        load_state(0)
+        for a in range(1, K_PASSES):
+            load_w1(a, 1)
+        for i in range(1, N_TILES - 1):
+            load_state(i)
+        nc.sync.dma_start(w4_w[:].bitcast(I32), w4_words.rearrange("b p c -> p b c").bitcast(I32))
+        for Q in range(P // QUADRANT):
+            nc.sync.dma_start(
+                w4_s[QUADRANT * Q : QUADRANT * Q + 4, :, :].bitcast(I32),
+                w4_scales[:, 4 * Q : 4 * Q + 4, :].rearrange("b s n -> s b n").bitcast(I32),
+            )
         with nc.allow_non_contiguous_dma(reason="one step value a partition"):
-            nc.scalar.dma_start(step_sb[:], step.rearrange("(i p) -> p i", p=P))
+            nc.sync.dma_start(step_sb[:], step.rearrange("(i p) -> p i", p=P))
+        load_state(N_TILES - 1)
 
-        twords = [keep.tile([P, T], U32, name="twords%d" % a, align_bytes=64) for a in range(3)]
-        state = [keep.tile([P, T], F32, name="state%d" % i, align_bytes=64) for i in range(4)]
-        wraw = {}
-        w4w = keep.tile([P, 2, 2 * N], U8, name="w4w", align_bytes=64)
-        for item in [("t", 0), ("w", 0, 0), ("w", 1, 0), ("t", 1), ("w", 2, 0), ("t", 2), ("w", 0, 1), ("w", 1, 1), ("w", 2, 1), ("w4",), ("g", 0), ("g", 1), ("g", 2), ("g", 3)]:
-            if item[0] == "w":
-                a, b = item[1], item[2]
-                wraw[a, b] = keep.tile([P, 4, 512], F32, name="wraw%d%d" % (a, b), align_bytes=64)
-                nc.sync.dma_start(wraw[a, b][:], w1[512 * a : 512 * a + 512, 512 * b : 512 * b + 512].rearrange("(p j) c -> p j c", j=4))
-            elif item[0] == "t":
-                a = item[1]
-                nc.sync.dma_start(twords[a][:].bitcast(I32), tab_words[a].rearrange("p t i -> p (t i)").bitcast(I32))
-            elif item[0] == "g":
-                i = item[1]
-                nc.sync.dma_start(state[i][:], gT[P * i : P * i + P, :])
-            else:
-                nc.sync.dma_start(w4w[:].bitcast(I32), w4_words.rearrange("b p c -> p b c").bitcast(I32))
-                for Q in range(4):
-                    nc.sync.dma_start(w4s[32 * Q : 32 * Q + 4, :, :].bitcast(I32), w4_scales[:, 4 * Q : 4 * Q + 4, :].rearrange("b r n -> r b n").bitcast(I32))
+        v_w = [keep.tile([P, S], U32, name="v_w%d" % a, align_bytes=64) for a in range(K_PASSES)]
+        v_s = keep.tile([P, S], U8, name="v_s", align_bytes=64)
+        picked = [keep.tile([P, S], F32, name="picked%d" % i, align_bytes=64) for i in range(N_TILES)]
+        w1_w, w1_s, z_bf, z_w, z_s = {}, {}, {}, {}, {}
 
-        vwords = [keep.tile([P, S], U32, name="vwords%d" % a, align_bytes=64) for a in range(3)]
-        vscale = keep.tile([P, S], U8, name="vscale", align_bytes=64)
-        picked = [keep.tile([P, S], F32, name="picked%d" % i, align_bytes=64) for i in range(4)]
-        wb, wcodes, wscale, zcodes, zscale = {}, {}, {}, {}, {}
-        used = []
+        def gather_words(a):
+            nc.vector.tensor_copy(v_w[a][:], tab_w[a][:].indirect(offsets[:]))
 
-        def new_bank(shape):
-            n = len(used)
-            used.append(n)
-            return psum.tile(shape, F32, name="bank%d" % n, tag="bank%d" % (n % NB))
-
-        def gather_scales():
-            nc.vector.tensor_copy(vscale[:], tscale[:].indirect(offsets[:]))
-
-        def gather_words(a, lo=0, hi=4):
-            nc.vector.tensor_copy(vwords[a][:, QW * lo : QW * hi], twords[a][:].indirect(offsets[:, 16 * lo : 16 * hi]))
-
-        def gather_state(i, lo=0, hi=4):
-            nc.vector.tensor_copy(picked[i][:, QW * lo : QW * hi], state[i][:].indirect(offsets[:, 16 * lo : 16 * hi]))
-
-        def cast(a, b, eng="s"):
-            wb[a, b] = ring.tile([P, 2048], BF16, name="wb", tag="wb", align_bytes=64)
-            dst = wb[a, b][:].rearrange("p (t m j) -> p m j t", t=4, j=4)
-            src = wraw[a, b][:].rearrange("p j (m t) -> p m j t", t=4)
-            if eng == "s":
-                nc.scalar.activation(dst, src, ACT.Copy)
-            else:
+        def quantise_w1(a, b):
+            w1_bf = ring.tile([P, PACK * PASS], BF16, name="w1_bf", tag="w1_bf", align_bytes=64)
+            dst = w1_bf[:].rearrange("p (t m j) -> p m j t", t=PACK, j=PACK)
+            src = w1_raw[a, b][:].rearrange("p j (m t) -> p m j t", t=PACK)
+            if (a, b) == (VECTOR_CAST_PASS, 1):
                 nc.vector.tensor_copy(dst, src)
+            else:
+                nc.scalar.activation(dst, src, ACT.Copy)
+            w1_w[a, b] = keep.tile([P, PASS], U32, name="w1_w%d%d" % (a, b), align_bytes=64)
+            w1_s[a, b] = keep.tile([P, PASS], U8, name="w1_s%d%d" % (a, b), align_bytes=64)
+            nc.vector.quantize_mx(out=w1_w[a, b][:].bitcast(FP8X4), scales=w1_s[a, b][:], in_=w1_bf[:])
 
-        def quant_w(a, b):
-            wcodes[a, b] = keep.tile([P, 512], U32, name="wcodes%d%d" % (a, b), align_bytes=64)
-            wscale[a, b] = keep.tile([P, 512], U8, name="wscale%d%d" % (a, b), align_bytes=64)
-            nc.vector.quantize_mx(out=wcodes[a, b][:].bitcast(FP8X4), scales=wscale[a, b][:], in_=wb[a, b][:])
-
-        def unit(q, b):
-            sq = ring.tile([P, 4, QW], F32, name="sq", tag="sq", align_bytes=64)
-            fac = ring.tile([P, 4, QW], F32, name="fac", tag="fac", align_bytes=64)
-            zb = ring.tile([P, 4 * QW], BF16, name="zb", tag="zb", align_bytes=64)
-            banks = []
+        def modes(q, b, pair):
+            square = ring.tile([P, PACK, QUARTER], F32, name="square", tag="square", align_bytes=64)
+            factor = ring.tile([P, PACK, QUARTER], F32, name="factor", tag="factor", align_bytes=64)
+            if b == 0:
+                z_bf[q] = keep.tile([P, R_PASSES * PACK * QUARTER], BF16, name="z_bf%d" % q, align_bytes=64)
+            h_banks = []
             for u in range(2):
-                bank = new_bank([P, 4, P])
-                banks.append(bank)
-                cols = slice(QW * q + P * u, QW * q + P * u + P)
-                for t in range(4):
-                    for a in range(3):
+                h_bank = psum.tile([P, PACK, P], F32, name="h_bank", tag="bank%d" % (2 * pair + u))
+                h_banks.append(h_bank)
+                entries = slice(QUARTER * q + P * u, QUARTER * q + P * (u + 1))
+                for t in range(PACK):
+                    for a in range(K_PASSES):
                         nc.tensor.matmul_mx(
-                            out=bank[:, t, :],
-                            lhsT=wcodes[a, b][:, P * t : P * t + P].bitcast(FP8X4),
-                            lhsT_scale=wscale[a, b][:, P * t : P * t + P],
-                            rhs=vwords[a][:, cols].bitcast(FP8X4),
-                            rhs_scale=vscale[4 * a : P, cols],
+                            out=h_bank[:, t, :],
+                            lhsT=w1_w[a, b][:, P * t : P * (t + 1)].bitcast(FP8X4),
+                            lhsT_scale=w1_s[a, b][:, P * t : P * (t + 1)],
+                            rhs=v_w[a][:, entries].bitcast(FP8X4),
+                            rhs_scale=v_s[4 * a : P, entries],
                             start=(a == 0),
-                            stop=(a == 2),
+                            stop=(a == K_PASSES - 1),
                         )
-                nc.scalar.activation(sq[:, :, P * u : P * u + P], bank[:], ACT.Square)
-            for t in range(4):
-                nc.scalar.activation(fac[:, t, :], sq[:, t, :], ACT.Copy, bias=1.0, scale=cub_sb[:, b, t : t + 1])
+                nc.scalar.activation(square[:, :, P * u : P * (u + 1)], h_bank[:], ACT.Square)
+            for t in range(PACK):
+                nc.scalar.activation(factor[:, t, :], square[:, t, :], ACT.Copy, bias=1.0, scale=cub_sb[:, b, t : t + 1])
             for u in range(2):
+                first = PACK * (QUARTER * b + P * u)
                 nc.vector.tensor_tensor(
-                    zb[:, 512 * u : 512 * u + 512].rearrange("p (c i t) -> p c t i", i=ZI, t=4),
-                    banks[u][:].rearrange("p t (c i) -> p c t i", i=ZI),
-                    fac[:, :, P * u : P * u + P].rearrange("p t (c i) -> p c t i", i=ZI),
+                    z_bf[q][:, first : first + PACK * P].rearrange("p (c i t) -> p c t i", i=RUN, t=PACK),
+                    h_banks[u][:].rearrange("p t (c i) -> p c t i", i=RUN),
+                    factor[:, :, P * u : P * (u + 1)].rearrange("p t (c i) -> p c t i", i=RUN),
                     ALU.mult,
                 )
-            zcodes[q, b] = keep.tile([P, QW], U32, name="zcodes%d%d" % (q, b), align_bytes=64)
-            zscale[q, b] = keep.tile([P, QW], U8, name="zscale%d%d" % (q, b), align_bytes=64)
-            nc.vector.quantize_mx(out=zcodes[q, b][:].bitcast(FP8X4), scales=zscale[q, b][:], in_=zb[:])
+            if b == R_PASSES - 1:
+                z_w[q] = keep.tile([P, R_PASSES * QUARTER], U32, name="z_w%d" % q, align_bytes=64)
+                z_s[q] = keep.tile([P, R_PASSES * QUARTER], U8, name="z_s%d" % q, align_bytes=64)
+                nc.vector.quantize_mx(out=z_w[q][:].bitcast(FP8X4), scales=z_s[q][:], in_=z_bf[q][:])
 
-        moved = [keep.tile([P, S], F32, name="moved%d" % i, align_bytes=64) for i in range(4)]
+        moved = [keep.tile([P, S], F32, name="moved%d" % i, align_bytes=64) for i in range(N_TILES)]
 
-        def drive(q):
-            for pair in range(2):
-                bank = new_bank([P, 2, QW])
+        def drive(q, pair):
+            for u in range(2):
+                y_bank = psum.tile([P, 2, QUARTER], F32, name="y_bank", tag="bank%d" % (2 * pair + u))
                 for e in range(2):
-                    i = 2 * pair + e
-                    for u in range(2):
-                        for b in range(2):
+                    i = 2 * u + e
+                    for c in range(0, QUARTER, P):
+                        for b in range(R_PASSES):
+                            z_cols = slice(QUARTER * b + c, QUARTER * b + c + P)
                             nc.tensor.matmul_mx(
-                                out=bank[:, e, P * u : P * u + P],
-                                lhsT=w4w[:, b, 2 * P * i : 2 * P * i + 2 * P].bitcast(FP4X4),
-                                lhsT_scale=w4s[:, b, P * i : P * i + P],
-                                rhs=zcodes[q, b][:, P * u : P * u + P].bitcast(FP8X4),
-                                rhs_scale=zscale[q, b][:, P * u : P * u + P],
+                                out=y_bank[:, e, c : c + P],
+                                lhsT=w4_w[:, b, 2 * P * i : 2 * P * (i + 1)].bitcast(FP4X4),
+                                lhsT_scale=w4_s[:, b, P * i : P * (i + 1)],
+                                rhs=z_w[q][:, z_cols].bitcast(FP8X4),
+                                rhs_scale=z_s[q][:, z_cols],
                                 start=(b == 0),
-                                stop=(b == 1),
+                                stop=(b == R_PASSES - 1),
                             )
                 for e in range(2):
-                    i = 2 * pair + e
-                    nc.scalar.activation(moved[i][:, QW * q : QW * q + QW], bank[:, e, :], ACT.Copy, scale=step_sb[:, i : i + 1])
+                    i = 2 * u + e
+                    nc.scalar.activation(
+                        moved[i][:, QUARTER * q : QUARTER * (q + 1)], y_bank[:, e, :], ACT.Copy, scale=step_sb[:, i : i + 1]
+                    )
 
         def put(lo, hi):
-            for i in range(4):
+            for i in range(N_TILES):
                 nc.vector.tensor_tensor(
-                    state[i][:].indirect(offsets[:, 16 * lo : 16 * hi]),
-                    picked[i][:, QW * lo : QW * hi],
-                    moved[i][:, QW * lo : QW * hi],
+                    state[i][:].indirect(offsets[:, LIST_COLS * lo : LIST_COLS * hi]),
+                    picked[i][:, QUARTER * lo : QUARTER * hi],
+                    moved[i][:, QUARTER * lo : QUARTER * hi],
                     ALU.add,
                 )
-                if hi == 4:
-                    nc.sync.dma_start(out[P * i : P * i + P, :], state[i][:])
+                if hi == QUARTERS:
+                    nc.sync.dma_start(out[P * i : P * (i + 1), :], state[i][:])
 
         gather_words(0)
-        cast(0, 0)
-        gather_scales()
-        quant_w(0, 0)
-        cast(1, 0)
-        gather_words(1)
-        quant_w(1, 0)
-        cast(2, 0)
-        quant_w(2, 0)
-        gather_words(2, 0, 2)
-        gather_words(2, 2, 4)
-        unit(0, 0)
-        cast(0, 1, "s")
-        quant_w(0, 1)
-        unit(1, 0)
-        cast(1, 1, "v")
-        quant_w(1, 1)
-        cast(2, 1, "v")
-        quant_w(2, 1)
-        unit(0, 1)
-        drive(0)
-        unit(1, 1)
-        unit(2, 0)
-        for i in range(4):
-            gather_state(i, 0, 2)
+        nc.vector.tensor_copy(v_s[:], tab_s[:].indirect(offsets[:]))
+        for a in range(K_PASSES):
+            quantise_w1(a, 0)
+            if a + 1 < K_PASSES:
+                gather_words(a + 1)
+        for a in range(K_PASSES):
+            quantise_w1(a, 1)
+
+        modes(0, 0, 0)
+        modes(0, 1, 1)
+        drive(0, 2)
+        modes(1, 0, 3)
+        modes(1, 1, 0)
+        for i in range(N_TILES):
+            nc.vector.tensor_copy(picked[i][:], state[i][:].indirect(offsets[:]))
         put(0, 1)
-        unit(2, 1)
-        unit(3, 0)
-        unit(3, 1)
-        drive(1)
-        for i in range(4):
-            gather_state(i, 2, 4)
+        modes(2, 0, 1)
+        modes(2, 1, 2)
+        modes(3, 0, 3)
+        modes(3, 1, 0)
+        drive(1, 1)
         put(1, 2)
-        drive(2)
-        drive(3)
-        put(2, 4)
+        drive(2, 2)
+        drive(3, 3)
+        put(2, QUARTERS)

@@ -173,11 +173,12 @@ def tile_list_oven_tray_refresh_kernel(tc, tab_words, tab_scales, offs, gT, w1, 
 
         def put(lo, hi):
             for i in range(N_TILES):
-                nc.vector.tensor_tensor(
+                for q in range(lo, hi):
+                    cols = slice(QUARTER * q, QUARTER * (q + 1))
+                    nc.gpsimd.tensor_tensor(moved[i][:, cols], picked[i][:, cols], moved[i][:, cols], ALU.add)
+                nc.vector.tensor_copy(
                     state[i][:].indirect(offsets[:, LIST_COLS * lo : LIST_COLS * hi]),
-                    picked[i][:, QUARTER * lo : QUARTER * hi],
                     moved[i][:, QUARTER * lo : QUARTER * hi],
-                    ALU.add,
                 )
                 if hi == QUARTERS:
                     nc.sync.dma_start(out[P * i : P * (i + 1), :], state[i][:])

@@ -28,7 +28,8 @@ QUARTER = S // QUARTERS
 LIST_COLS = QUARTER // 16
 RUN = 2
 RING = 3
-VECTOR_CAST_PASS = 1
+CAST_ENGINE = "AAVVVV"
+PRODUCT_ENGINE = "GVGVGGGG"
 
 
 def tile_list_oven_tray_refresh_kernel(tc, tab_words, tab_scales, offs, gT, w1, cub, w4_words, w4_scales, step, out):
@@ -61,48 +62,67 @@ def tile_list_oven_tray_refresh_kernel(tc, tab_words, tab_scales, offs, gT, w1, 
         def load_state(i):
             nc.sync.dma_start(state[i][:], gT[P * i : P * (i + 1), :])
 
-        load_table(0)
-        nc.sync.dma_start(offsets[:], offs)
-        load_w1(0, 0)
-        for Q in range(P // QUADRANT):
-            nc.sync.dma_start(
-                tab_s[QUADRANT * Q : QUADRANT * Q + 4 * K_PASSES, :].bitcast(I32),
-                tab_scales[:, 4 * Q : 4 * Q + 4, :].bitcast(I32),
-            )
-        for a in range(1, K_PASSES):
-            load_table(a)
-            load_w1(a, 0)
-        nc.sync.dma_start(cub_sb[:], cub.rearrange("(b p t) -> p b t", b=R_PASSES, t=PACK))
-        load_w1(0, 1)
-        load_state(0)
-        for a in range(1, K_PASSES):
-            load_w1(a, 1)
-        for i in range(1, N_TILES - 1):
-            load_state(i)
-        nc.sync.dma_start(w4_w[:].bitcast(I32), w4_words.rearrange("b p c -> p b c").bitcast(I32))
-        for Q in range(P // QUADRANT):
+        def load_scale_rows():
+            for Q in range(P // QUADRANT):
+                nc.sync.dma_start(
+                    tab_s[QUADRANT * Q : QUADRANT * Q + 4 * K_PASSES, :].bitcast(I32),
+                    tab_scales[:, 4 * Q : 4 * Q + 4, :].bitcast(I32),
+                )
+
+        def load_w4_scales(Q):
             nc.sync.dma_start(
                 w4_s[QUADRANT * Q : QUADRANT * Q + 4, :, :].bitcast(I32),
                 w4_scales[:, 4 * Q : 4 * Q + 4, :].rearrange("b s n -> s b n").bitcast(I32),
             )
+
+        nc.sync.dma_start(offsets[:], offs)
+        load_table(0)
+        load_w1(0, 0)
+        load_scale_rows()
+        load_w1(1, 0)
+        load_w4_scales(0)
+        load_w4_scales(1)
+        load_table(1)
+        load_w4_scales(2)
+        load_w4_scales(3)
+        load_w1(2, 0)
         with nc.allow_non_contiguous_dma(reason="one step value a partition"):
             nc.sync.dma_start(step_sb[:], step.rearrange("(i p) -> p i", p=P))
-        load_state(N_TILES - 1)
+        nc.sync.dma_start(cub_sb[:], cub.rearrange("(b p t) -> p b t", b=R_PASSES, t=PACK))
+        load_table(2)
+        load_w1(0, 1)
+        load_w1(1, 1)
+        load_state(0)
+        load_w1(2, 1)
+        load_state(1)
+        nc.sync.dma_start(w4_w[:].bitcast(I32), w4_words.rearrange("b p c -> p b c").bitcast(I32))
+        load_state(2)
+        load_state(3)
 
         v_w = [keep.tile([P, S], U32, name="v_w%d" % a, align_bytes=64) for a in range(K_PASSES)]
         v_s = keep.tile([P, S], U8, name="v_s", align_bytes=64)
         picked = [keep.tile([P, S], F32, name="picked%d" % i, align_bytes=64) for i in range(N_TILES)]
         w1_w, w1_s, z_bf, z_w, z_s = {}, {}, {}, {}, {}
 
-        def gather_words(a):
-            nc.vector.tensor_copy(v_w[a][:], tab_w[a][:].indirect(offsets[:]))
+        def gather_words(a, lo, hi):
+            nc.vector.tensor_copy(
+                v_w[a][:, QUARTER * lo : QUARTER * hi], tab_w[a][:].indirect(offsets[:, LIST_COLS * lo : LIST_COLS * hi])
+            )
+
+        def gather_state(i, lo, hi):
+            nc.vector.tensor_copy(
+                picked[i][:, QUARTER * lo : QUARTER * hi], state[i][:].indirect(offsets[:, LIST_COLS * lo : LIST_COLS * hi])
+            )
 
         def quantise_w1(a, b):
             w1_bf = ring.tile([P, PACK * PASS], BF16, name="w1_bf", tag="w1_bf", align_bytes=64)
             dst = w1_bf[:].rearrange("p (t m j) -> p m j t", t=PACK, j=PACK)
             src = w1_raw[a, b][:].rearrange("p j (m t) -> p m j t", t=PACK)
-            if (a, b) == (VECTOR_CAST_PASS, 1):
+            if CAST_ENGINE[3 * b + a] == "V":
                 nc.vector.tensor_copy(dst, src)
+            elif CAST_ENGINE[3 * b + a] == "G":
+                for m in range(0, P, P // 2):
+                    nc.gpsimd.tensor_scalar(dst[:, m : m + P // 2], src[:, m : m + P // 2], 1.0, 0.0, ALU.mult, ALU.add)
             else:
                 nc.scalar.activation(dst, src, ACT.Copy)
             w1_w[a, b] = keep.tile([P, PASS], U32, name="w1_w%d%d" % (a, b), align_bytes=64)
@@ -110,7 +130,9 @@ def tile_list_oven_tray_refresh_kernel(tc, tab_words, tab_scales, offs, gT, w1, 
             nc.vector.quantize_mx(out=w1_w[a, b][:].bitcast(FP8X4), scales=w1_s[a, b][:], in_=w1_bf[:])
 
         def modes(q, b, pair):
-            square = ring.tile([P, PACK, QUARTER], F32, name="square", tag="square", align_bytes=64)
+            on_gpsimd = PRODUCT_ENGINE[2 * q + b] == "G"
+            if on_gpsimd:
+                h_sb = ring.tile([P, 2, P, PACK], F32, name="h_sb", tag="h_sb", align_bytes=64)
             factor = ring.tile([P, PACK, QUARTER], F32, name="factor", tag="factor", align_bytes=64)
             if b == 0:
                 z_bf[q] = keep.tile([P, R_PASSES * PACK * QUARTER], BF16, name="z_bf%d" % q, align_bytes=64)
@@ -130,11 +152,23 @@ def tile_list_oven_tray_refresh_kernel(tc, tab_words, tab_scales, offs, gT, w1, 
                             start=(a == 0),
                             stop=(a == K_PASSES - 1),
                         )
-                nc.scalar.activation(square[:, :, P * u : P * (u + 1)], h_bank[:], ACT.Square)
+                nc.scalar.activation(factor[:, :, P * u : P * (u + 1)], h_bank[:], ACT.Square)
+                if on_gpsimd:
+                    nc.scalar.copy(h_sb[:, u], h_bank[:].rearrange("p t j -> p j t"))
             for t in range(PACK):
-                nc.scalar.activation(factor[:, t, :], square[:, t, :], ACT.Copy, bias=1.0, scale=cub_sb[:, b, t : t + 1])
+                nc.scalar.activation(factor[:, t, :], factor[:, t, :], ACT.Copy, bias=1.0, scale=cub_sb[:, b, t : t + 1])
             for u in range(2):
                 first = PACK * (QUARTER * b + P * u)
+                if on_gpsimd:
+                    for c in range(0, P, P // 2):
+                        w = P // 2
+                        nc.gpsimd.tensor_tensor(
+                            z_bf[q][:, first + PACK * c : first + PACK * (c + w)].rearrange("p (j t) -> p j t", t=PACK),
+                            h_sb[:, u, c : c + w],
+                            factor[:, :, P * u + c : P * u + c + w].rearrange("p t j -> p j t"),
+                            ALU.mult,
+                        )
+                    continue
                 nc.vector.tensor_tensor(
                     z_bf[q][:, first : first + PACK * P].rearrange("p (c i t) -> p c t i", i=RUN, t=PACK),
                     h_banks[u][:].rearrange("p t (c i) -> p c t i", i=RUN),
@@ -171,8 +205,18 @@ def tile_list_oven_tray_refresh_kernel(tc, tab_words, tab_scales, offs, gT, w1, 
                         moved[i][:, QUARTER * q : QUARTER * (q + 1)], y_bank[:, e, :], ACT.Copy, scale=step_sb[:, i : i + 1]
                     )
 
-        def put(lo, hi):
-            for i in range(N_TILES):
+        def put(lo, hi, tiles, fused):
+            for i in tiles:
+                if fused:
+                    nc.vector.tensor_tensor(
+                        state[i][:].indirect(offsets[:, LIST_COLS * lo : LIST_COLS * hi]),
+                        picked[i][:, QUARTER * lo : QUARTER * hi],
+                        moved[i][:, QUARTER * lo : QUARTER * hi],
+                        ALU.add,
+                    )
+                    if hi == QUARTERS:
+                        nc.sync.dma_start(out[P * i : P * (i + 1), :], state[i][:])
+                    continue
                 for q in range(lo, hi):
                     cols = slice(QUARTER * q, QUARTER * (q + 1))
                     nc.gpsimd.tensor_tensor(moved[i][:, cols], picked[i][:, cols], moved[i][:, cols], ALU.add)
@@ -183,29 +227,35 @@ def tile_list_oven_tray_refresh_kernel(tc, tab_words, tab_scales, offs, gT, w1, 
                 if hi == QUARTERS:
                     nc.sync.dma_start(out[P * i : P * (i + 1), :], state[i][:])
 
-        gather_words(0)
+        gather_words(0, 0, 4)
         nc.vector.tensor_copy(v_s[:], tab_s[:].indirect(offsets[:]))
-        for a in range(K_PASSES):
-            quantise_w1(a, 0)
-            if a + 1 < K_PASSES:
-                gather_words(a + 1)
-        for a in range(K_PASSES):
-            quantise_w1(a, 1)
-
+        quantise_w1(0, 0)
+        quantise_w1(1, 0)
+        gather_words(1, 0, 4)
+        quantise_w1(2, 0)
+        gather_words(2, 0, 1)
+        gather_words(2, 1, 4)
+        quantise_w1(0, 1)
+        quantise_w1(1, 1)
+        quantise_w1(2, 1)
         modes(0, 0, 0)
-        modes(0, 1, 1)
-        drive(0, 2)
-        modes(1, 0, 3)
+        modes(1, 0, 1)
+        modes(2, 0, 2)
+        modes(0, 1, 3)
         modes(1, 1, 0)
-        for i in range(N_TILES):
-            nc.vector.tensor_copy(picked[i][:], state[i][:].indirect(offsets[:]))
-        put(0, 1)
-        modes(2, 0, 1)
+        drive(0, 1)
+        gather_state(0, 0, 4)
+        gather_state(1, 0, 4)
+        gather_state(2, 0, 4)
+        gather_state(3, 0, 4)
+        put(0, 1, [0, 1, 2, 3], False)
         modes(2, 1, 2)
-        modes(3, 0, 3)
+        drive(1, 2)
+        put(1, 2, [0, 1, 2, 3], False)
+        modes(3, 0, 1)
         modes(3, 1, 0)
-        drive(1, 1)
-        put(1, 2)
-        drive(2, 2)
+        drive(2, 1)
         drive(3, 3)
-        put(2, QUARTERS)
+        put(2, 3, [0, 1], False)
+        put(3, 4, [0, 1], True)
+        put(2, 4, [2, 3], True)

@@ -27,6 +27,7 @@ QUARTERS = 4
 QUARTER = S // QUARTERS
 LIST_COLS = QUARTER // 16
 RUN = 2
+LINE = 4
 RING = 3
 CAST_ENGINE = "AAVVVV"
 PRODUCT_ENGINE = "GVGVGGGG"
@@ -132,7 +133,7 @@ def tile_list_oven_tray_refresh_kernel(tc, tab_words, tab_scales, offs, gT, w1, 
         def modes(q, b, pair):
             on_gpsimd = PRODUCT_ENGINE[2 * q + b] == "G"
             if on_gpsimd:
-                h_sb = ring.tile([P, 2, P, PACK], F32, name="h_sb", tag="h_sb", align_bytes=64)
+                h_sb = ring.tile([P, PACK, QUARTER], F32, name="h_sb", tag="h_sb", align_bytes=64)
             factor = ring.tile([P, PACK, QUARTER], F32, name="factor", tag="factor", align_bytes=64)
             if b == 0:
                 z_bf[q] = keep.tile([P, R_PASSES * PACK * QUARTER], BF16, name="z_bf%d" % q, align_bytes=64)
@@ -154,7 +155,7 @@ def tile_list_oven_tray_refresh_kernel(tc, tab_words, tab_scales, offs, gT, w1, 
                         )
                 nc.scalar.activation(factor[:, :, P * u : P * (u + 1)], h_bank[:], ACT.Square)
                 if on_gpsimd:
-                    nc.scalar.copy(h_sb[:, u], h_bank[:].rearrange("p t j -> p j t"))
+                    nc.scalar.copy(h_sb[:, :, P * u : P * (u + 1)], h_bank[:])
             for t in range(PACK):
                 nc.scalar.activation(factor[:, t, :], factor[:, t, :], ACT.Copy, bias=1.0, scale=cub_sb[:, b, t : t + 1])
             for u in range(2):
@@ -163,9 +164,9 @@ def tile_list_oven_tray_refresh_kernel(tc, tab_words, tab_scales, offs, gT, w1, 
                     for c in range(0, P, P // 2):
                         w = P // 2
                         nc.gpsimd.tensor_tensor(
-                            z_bf[q][:, first + PACK * c : first + PACK * (c + w)].rearrange("p (j t) -> p j t", t=PACK),
-                            h_sb[:, u, c : c + w],
-                            factor[:, :, P * u + c : P * u + c + w].rearrange("p t j -> p j t"),
+                            z_bf[q][:, first + PACK * c : first + PACK * (c + w)].rearrange("p (c i t) -> p c t i", i=LINE, t=PACK),
+                            h_sb[:, :, P * u + c : P * u + c + w].rearrange("p t (c i) -> p c t i", i=LINE),
+                            factor[:, :, P * u + c : P * u + c + w].rearrange("p t (c i) -> p c t i", i=LINE),
                             ALU.mult,
                         )
                     continue

@@ -29,7 +29,7 @@ LIST_COLS = QUARTER // 16
 RUN = 2
 LINE = 4
 RING = 3
-CAST_ENGINE = "AAVVVV"
+CAST_ENGINE = "AAAVVV"
 PRODUCT_ENGINE = "GVGVGGGG"
 
 
@@ -83,12 +83,10 @@ def tile_list_oven_tray_refresh_kernel(tc, tab_words, tab_scales, offs, gT, w1, 
         load_w1(1, 0)
         load_w4_scales(0)
         load_w4_scales(1)
-        load_table(1)
+        load_w1(2, 0)
         load_w4_scales(2)
         load_w4_scales(3)
-        load_w1(2, 0)
-        with nc.allow_non_contiguous_dma(reason="one step value a partition"):
-            nc.sync.dma_start(step_sb[:], step.rearrange("(i p) -> p i", p=P))
+        load_table(1)
         nc.sync.dma_start(cub_sb[:], cub.rearrange("(b p t) -> p b t", b=R_PASSES, t=PACK))
         load_table(2)
         load_w1(0, 1)
@@ -99,6 +97,8 @@ def tile_list_oven_tray_refresh_kernel(tc, tab_words, tab_scales, offs, gT, w1, 
         nc.sync.dma_start(w4_w[:].bitcast(I32), w4_words.rearrange("b p c -> p b c").bitcast(I32))
         load_state(2)
         load_state(3)
+        with nc.allow_non_contiguous_dma(reason="one step value a partition"):
+            nc.sync.dma_start(step_sb[:], step.rearrange("(i p) -> p i", p=P))
 
         v_w = [keep.tile([P, S], U32, name="v_w%d" % a, align_bytes=64) for a in range(K_PASSES)]
         v_s = keep.tile([P, S], U8, name="v_s", align_bytes=64)
@@ -116,7 +116,10 @@ def tile_list_oven_tray_refresh_kernel(tc, tab_words, tab_scales, offs, gT, w1, 
             )
 
         def quantise_w1(a, b):
-            w1_bf = ring.tile([P, PACK * PASS], BF16, name="w1_bf", tag="w1_bf", align_bytes=64)
+            if (a, b) == (K_PASSES - 1, R_PASSES - 1):
+                w1_bf = keep.tile([P, PACK * PASS], BF16, name="w1_bf_last", tag="slot0", align_bytes=64)
+            else:
+                w1_bf = ring.tile([P, PACK * PASS], BF16, name="w1_bf", tag="w1_bf", align_bytes=64)
             dst = w1_bf[:].rearrange("p (t m j) -> p m j t", t=PACK, j=PACK)
             src = w1_raw[a, b][:].rearrange("p j (m t) -> p m j t", t=PACK)
             if CAST_ENGINE[3 * b + a] == "V":
@@ -133,10 +136,17 @@ def tile_list_oven_tray_refresh_kernel(tc, tab_words, tab_scales, offs, gT, w1, 
         def modes(q, b, pair):
             on_gpsimd = PRODUCT_ENGINE[2 * q + b] == "G"
             if on_gpsimd:
-                h_sb = ring.tile([P, PACK, QUARTER], F32, name="h_sb", tag="h_sb", align_bytes=64)
-            factor = ring.tile([P, PACK, QUARTER], F32, name="factor", tag="factor", align_bytes=64)
+                if (q, b) in ((0, 0), (3, 0)):
+                    h_sb = keep.tile([P, PACK * QUARTER], F32, name="h_held", tag="slot%d" % (1 if q == 0 else 2), align_bytes=64)
+                else:
+                    h_sb = ring.tile([P, PACK * QUARTER], F32, name="h_sb", tag="h_sb", align_bytes=64)
+            flat = ring.tile([P, PACK * QUARTER], F32, name="factor", tag="factor", bufs=4, align_bytes=64)
+            if on_gpsimd:
+                factor = flat[:].rearrange("p (c t i) -> p t c i", t=PACK, i=LINE)
+            else:
+                factor = flat[:].rearrange("p (t c i) -> p t c i", t=PACK, i=LINE)
             if b == 0:
-                z_bf[q] = keep.tile([P, R_PASSES * PACK * QUARTER], BF16, name="z_bf%d" % q, align_bytes=64)
+                z_bf[q] = keep.tile([P, R_PASSES * PACK * QUARTER], BF16, name="z_bf%d" % q, tag="slot%d" % [0, 1, 0, 0][q], align_bytes=64)
             h_banks = []
             for u in range(2):
                 h_bank = psum.tile([P, PACK, P], F32, name="h_bank", tag="bank%d" % (2 * pair + u))
@@ -153,27 +163,33 @@ def tile_list_oven_tray_refresh_kernel(tc, tab_words, tab_scales, offs, gT, w1, 
                             start=(a == 0),
                             stop=(a == K_PASSES - 1),
                         )
-                nc.scalar.activation(factor[:, :, P * u : P * (u + 1)], h_bank[:], ACT.Square)
+                lines = slice(P // LINE * u, P // LINE * (u + 1))
+                h_lines = h_bank[:].rearrange("p t (c i) -> p t c i", i=LINE)
                 if on_gpsimd:
-                    nc.scalar.copy(h_sb[:, :, P * u : P * (u + 1)], h_bank[:])
+                    h_lines = h_bank[:].rearrange("p t (c i) -> p c t i", i=LINE)
+                    part = slice(PACK * P * u, PACK * P * (u + 1))
+                    nc.scalar.activation(flat[:, part].rearrange("p (c t i) -> p c t i", t=PACK, i=LINE), h_lines, ACT.Square)
+                    nc.scalar.copy(h_sb[:, part].rearrange("p (c t i) -> p c t i", t=PACK, i=LINE), h_lines)
+                else:
+                    nc.scalar.activation(factor[:, :, lines], h_lines, ACT.Square)
             for t in range(PACK):
-                nc.scalar.activation(factor[:, t, :], factor[:, t, :], ACT.Copy, bias=1.0, scale=cub_sb[:, b, t : t + 1])
+                nc.scalar.activation(factor[:, t], factor[:, t], ACT.Copy, bias=1.0, scale=cub_sb[:, b, t : t + 1])
             for u in range(2):
                 first = PACK * (QUARTER * b + P * u)
                 if on_gpsimd:
-                    for c in range(0, P, P // 2):
-                        w = P // 2
+                    for c in range(0, P, P // 1):
+                        w = P // 1
                         nc.gpsimd.tensor_tensor(
                             z_bf[q][:, first + PACK * c : first + PACK * (c + w)].rearrange("p (c i t) -> p c t i", i=LINE, t=PACK),
-                            h_sb[:, :, P * u + c : P * u + c + w].rearrange("p t (c i) -> p c t i", i=LINE),
-                            factor[:, :, P * u + c : P * u + c + w].rearrange("p t (c i) -> p c t i", i=LINE),
+                            h_sb[:, PACK * (P * u + c) : PACK * (P * u + c + w)].rearrange("p (c t i) -> p c t i", t=PACK, i=LINE),
+                            flat[:, PACK * (P * u + c) : PACK * (P * u + c + w)].rearrange("p (c t i) -> p c t i", t=PACK, i=LINE),
                             ALU.mult,
                         )
                     continue
                 nc.vector.tensor_tensor(
                     z_bf[q][:, first : first + PACK * P].rearrange("p (c i t) -> p c t i", i=RUN, t=PACK),
                     h_banks[u][:].rearrange("p t (c i) -> p c t i", i=RUN),
-                    factor[:, :, P * u : P * (u + 1)].rearrange("p t (c i) -> p c t i", i=RUN),
+                    flat[:].rearrange("p (t j) -> p t j", t=PACK)[:, :, P * u : P * (u + 1)].rearrange("p t (c i) -> p c t i", i=RUN),
                     ALU.mult,
                 )
             if b == R_PASSES - 1:
@@ -207,6 +223,8 @@ def tile_list_oven_tray_refresh_kernel(tc, tab_words, tab_scales, offs, gT, w1, 
                     )
 
         def put(lo, hi, tiles, fused):
+            if not fused:
+                fresh = keep.tile([P, N_TILES - 1, QUARTER], F32, name="fresh%d" % lo, tag="slot%d" % [1, 2, 0][lo], align_bytes=64)
             for i in tiles:
                 if fused:
                     nc.vector.tensor_tensor(
@@ -220,10 +238,11 @@ def tile_list_oven_tray_refresh_kernel(tc, tab_words, tab_scales, offs, gT, w1, 
                     continue
                 for q in range(lo, hi):
                     cols = slice(QUARTER * q, QUARTER * (q + 1))
-                    nc.gpsimd.tensor_tensor(moved[i][:, cols], picked[i][:, cols], moved[i][:, cols], ALU.add)
+                    new = moved[i][:, cols] if i < [1, 3, 1][q] else fresh[:, i - 1]
+                    nc.gpsimd.tensor_tensor(new, picked[i][:, cols], moved[i][:, cols], ALU.add)
                 nc.vector.tensor_copy(
                     state[i][:].indirect(offsets[:, LIST_COLS * lo : LIST_COLS * hi]),
-                    moved[i][:, QUARTER * lo : QUARTER * hi],
+                    new,
                 )
                 if hi == QUARTERS:
                     nc.sync.dma_start(out[P * i : P * (i + 1), :], state[i][:])
@@ -232,8 +251,8 @@ def tile_list_oven_tray_refresh_kernel(tc, tab_words, tab_scales, offs, gT, w1, 
         nc.vector.tensor_copy(v_s[:], tab_s[:].indirect(offsets[:]))
         quantise_w1(0, 0)
         quantise_w1(1, 0)
-        gather_words(1, 0, 4)
         quantise_w1(2, 0)
+        gather_words(1, 0, 4)
         gather_words(2, 0, 1)
         gather_words(2, 1, 4)
         quantise_w1(0, 1)
@@ -252,8 +271,8 @@ def tile_list_oven_tray_refresh_kernel(tc, tab_words, tab_scales, offs, gT, w1, 
         put(0, 1, [0, 1, 2, 3], False)
         modes(2, 1, 2)
         drive(1, 2)
-        put(1, 2, [0, 1, 2, 3], False)
         modes(3, 0, 1)
+        put(1, 2, [0, 1, 2, 3], False)
         modes(3, 1, 0)
         drive(2, 1)
         drive(3, 3)

@@ -29,8 +29,8 @@ LIST_COLS = QUARTER // 16
 RUN = 2
 LINE = 4
 RING = 3
-CAST_ENGINE = "AAAVVV"
-PRODUCT_ENGINE = "GVGVGGGG"
+FACTOR_RING = 4
+VECTOR_PRODUCTS = ((0, 1), (1, 1))
 
 
 def tile_list_oven_tray_refresh_kernel(tc, tab_words, tab_scales, offs, gT, w1, cub, w4_words, w4_scales, step, out):
@@ -63,29 +63,25 @@ def tile_list_oven_tray_refresh_kernel(tc, tab_words, tab_scales, offs, gT, w1, 
         def load_state(i):
             nc.sync.dma_start(state[i][:], gT[P * i : P * (i + 1), :])
 
-        def load_scale_rows():
-            for Q in range(P // QUADRANT):
+        def load_w4_scales(quadrants):
+            for Q in quadrants:
                 nc.sync.dma_start(
-                    tab_s[QUADRANT * Q : QUADRANT * Q + 4 * K_PASSES, :].bitcast(I32),
-                    tab_scales[:, 4 * Q : 4 * Q + 4, :].bitcast(I32),
+                    w4_s[QUADRANT * Q : QUADRANT * Q + 4, :, :].bitcast(I32),
+                    w4_scales[:, 4 * Q : 4 * Q + 4, :].rearrange("b s n -> s b n").bitcast(I32),
                 )
-
-        def load_w4_scales(Q):
-            nc.sync.dma_start(
-                w4_s[QUADRANT * Q : QUADRANT * Q + 4, :, :].bitcast(I32),
-                w4_scales[:, 4 * Q : 4 * Q + 4, :].rearrange("b s n -> s b n").bitcast(I32),
-            )
 
         nc.sync.dma_start(offsets[:], offs)
         load_table(0)
         load_w1(0, 0)
-        load_scale_rows()
+        for Q in range(P // QUADRANT):
+            nc.sync.dma_start(
+                tab_s[QUADRANT * Q : QUADRANT * Q + 4 * K_PASSES, :].bitcast(I32),
+                tab_scales[:, 4 * Q : 4 * Q + 4, :].bitcast(I32),
+            )
         load_w1(1, 0)
-        load_w4_scales(0)
-        load_w4_scales(1)
+        load_w4_scales((0, 1))
         load_w1(2, 0)
-        load_w4_scales(2)
-        load_w4_scales(3)
+        load_w4_scales((2, 3))
         load_table(1)
         nc.sync.dma_start(cub_sb[:], cub.rearrange("(b p t) -> p b t", b=R_PASSES, t=PACK))
         load_table(2)
@@ -93,27 +89,26 @@ def tile_list_oven_tray_refresh_kernel(tc, tab_words, tab_scales, offs, gT, w1, 
         load_w1(1, 1)
         load_state(0)
         load_w1(2, 1)
-        load_state(1)
+        for i in range(1, N_TILES):
+            load_state(i)
         nc.sync.dma_start(w4_w[:].bitcast(I32), w4_words.rearrange("b p c -> p b c").bitcast(I32))
-        load_state(2)
-        load_state(3)
         with nc.allow_non_contiguous_dma(reason="one step value a partition"):
             nc.sync.dma_start(step_sb[:], step.rearrange("(i p) -> p i", p=P))
 
         v_w = [keep.tile([P, S], U32, name="v_w%d" % a, align_bytes=64) for a in range(K_PASSES)]
         v_s = keep.tile([P, S], U8, name="v_s", align_bytes=64)
-        picked = [keep.tile([P, S], F32, name="picked%d" % i, align_bytes=64) for i in range(N_TILES)]
+        picked = keep.tile([P, N_TILES, S], F32, name="picked", align_bytes=64)
         w1_w, w1_s, z_bf, z_w, z_s = {}, {}, {}, {}, {}
 
-        def gather_words(a, lo, hi):
-            nc.vector.tensor_copy(
-                v_w[a][:, QUARTER * lo : QUARTER * hi], tab_w[a][:].indirect(offsets[:, LIST_COLS * lo : LIST_COLS * hi])
-            )
+        z_slot = {0: "slot0", 1: "slot1", 2: "slot0", 3: "slot0"}
+        h_slot = {(0, 0): "slot1", (3, 0): "slot2"}
+        sum_slot = {0: "slot1", 1: "slot2", 2: "slot0"}
 
-        def gather_state(i, lo, hi):
-            nc.vector.tensor_copy(
-                picked[i][:, QUARTER * lo : QUARTER * hi], state[i][:].indirect(offsets[:, LIST_COLS * lo : LIST_COLS * hi])
-            )
+        def listed(lo, hi):
+            return offsets[:, LIST_COLS * lo : LIST_COLS * hi]
+
+        def gather_words(a, lo, hi):
+            nc.vector.tensor_copy(v_w[a][:, QUARTER * lo : QUARTER * hi], tab_w[a][:].indirect(listed(lo, hi)))
 
         def quantise_w1(a, b):
             if (a, b) == (K_PASSES - 1, R_PASSES - 1):
@@ -122,31 +117,30 @@ def tile_list_oven_tray_refresh_kernel(tc, tab_words, tab_scales, offs, gT, w1, 
                 w1_bf = ring.tile([P, PACK * PASS], BF16, name="w1_bf", tag="w1_bf", align_bytes=64)
             dst = w1_bf[:].rearrange("p (t m j) -> p m j t", t=PACK, j=PACK)
             src = w1_raw[a, b][:].rearrange("p j (m t) -> p m j t", t=PACK)
-            if CAST_ENGINE[3 * b + a] == "V":
-                nc.vector.tensor_copy(dst, src)
-            elif CAST_ENGINE[3 * b + a] == "G":
-                for m in range(0, P, P // 2):
-                    nc.gpsimd.tensor_scalar(dst[:, m : m + P // 2], src[:, m : m + P // 2], 1.0, 0.0, ALU.mult, ALU.add)
-            else:
+            if b == 0:
                 nc.scalar.activation(dst, src, ACT.Copy)
+            else:
+                nc.vector.tensor_copy(dst, src)
             w1_w[a, b] = keep.tile([P, PASS], U32, name="w1_w%d%d" % (a, b), align_bytes=64)
             w1_s[a, b] = keep.tile([P, PASS], U8, name="w1_s%d%d" % (a, b), align_bytes=64)
             nc.vector.quantize_mx(out=w1_w[a, b][:].bitcast(FP8X4), scales=w1_s[a, b][:], in_=w1_bf[:])
 
+        def by_line(ap):
+            return ap.rearrange("p (c t i) -> p c t i", t=PACK, i=LINE)
+
         def modes(q, b, pair):
-            on_gpsimd = PRODUCT_ENGINE[2 * q + b] == "G"
-            if on_gpsimd:
-                if (q, b) in ((0, 0), (3, 0)):
-                    h_sb = keep.tile([P, PACK * QUARTER], F32, name="h_held", tag="slot%d" % (1 if q == 0 else 2), align_bytes=64)
-                else:
-                    h_sb = ring.tile([P, PACK * QUARTER], F32, name="h_sb", tag="h_sb", align_bytes=64)
-            flat = ring.tile([P, PACK * QUARTER], F32, name="factor", tag="factor", bufs=4, align_bytes=64)
-            if on_gpsimd:
-                factor = flat[:].rearrange("p (c t i) -> p t c i", t=PACK, i=LINE)
+            on_vector = (q, b) in VECTOR_PRODUCTS
+            if (q, b) in h_slot:
+                h_sb = keep.tile([P, PACK * QUARTER], F32, name="h_held", tag=h_slot[q, b], align_bytes=64)
+            elif not on_vector:
+                h_sb = ring.tile([P, PACK * QUARTER], F32, name="h_sb", tag="h_sb", align_bytes=64)
+            factor = ring.tile([P, PACK * QUARTER], F32, name="factor", tag="factor", bufs=FACTOR_RING, align_bytes=64)
+            if on_vector:
+                planes = factor[:].rearrange("p (t j) -> p t j", t=PACK)
             else:
-                factor = flat[:].rearrange("p (t c i) -> p t c i", t=PACK, i=LINE)
+                planes = by_line(factor[:]).rearrange("p c t i -> p t c i")
             if b == 0:
-                z_bf[q] = keep.tile([P, R_PASSES * PACK * QUARTER], BF16, name="z_bf%d" % q, tag="slot%d" % [0, 1, 0, 0][q], align_bytes=64)
+                z_bf[q] = keep.tile([P, R_PASSES * PACK * QUARTER], BF16, name="z_bf%d" % q, tag=z_slot[q], align_bytes=64)
             h_banks = []
             for u in range(2):
                 h_bank = psum.tile([P, PACK, P], F32, name="h_bank", tag="bank%d" % (2 * pair + u))
@@ -163,41 +157,34 @@ def tile_list_oven_tray_refresh_kernel(tc, tab_words, tab_scales, offs, gT, w1, 
                             start=(a == 0),
                             stop=(a == K_PASSES - 1),
                         )
-                lines = slice(P // LINE * u, P // LINE * (u + 1))
-                h_lines = h_bank[:].rearrange("p t (c i) -> p t c i", i=LINE)
-                if on_gpsimd:
+                if on_vector:
+                    nc.scalar.activation(planes[:, :, P * u : P * (u + 1)], h_bank[:], ACT.Square)
+                else:
                     h_lines = h_bank[:].rearrange("p t (c i) -> p c t i", i=LINE)
                     part = slice(PACK * P * u, PACK * P * (u + 1))
-                    nc.scalar.activation(flat[:, part].rearrange("p (c t i) -> p c t i", t=PACK, i=LINE), h_lines, ACT.Square)
-                    nc.scalar.copy(h_sb[:, part].rearrange("p (c t i) -> p c t i", t=PACK, i=LINE), h_lines)
-                else:
-                    nc.scalar.activation(factor[:, :, lines], h_lines, ACT.Square)
+                    nc.scalar.activation(by_line(factor[:, part]), h_lines, ACT.Square)
+                    nc.scalar.copy(by_line(h_sb[:, part]), h_lines)
             for t in range(PACK):
-                nc.scalar.activation(factor[:, t], factor[:, t], ACT.Copy, bias=1.0, scale=cub_sb[:, b, t : t + 1])
-            for u in range(2):
-                first = PACK * (QUARTER * b + P * u)
-                if on_gpsimd:
-                    for c in range(0, P, P // 1):
-                        w = P // 1
-                        nc.gpsimd.tensor_tensor(
-                            z_bf[q][:, first + PACK * c : first + PACK * (c + w)].rearrange("p (c i t) -> p c t i", i=LINE, t=PACK),
-                            h_sb[:, PACK * (P * u + c) : PACK * (P * u + c + w)].rearrange("p (c t i) -> p c t i", t=PACK, i=LINE),
-                            flat[:, PACK * (P * u + c) : PACK * (P * u + c + w)].rearrange("p (c t i) -> p c t i", t=PACK, i=LINE),
-                            ALU.mult,
-                        )
-                    continue
-                nc.vector.tensor_tensor(
-                    z_bf[q][:, first : first + PACK * P].rearrange("p (c i t) -> p c t i", i=RUN, t=PACK),
-                    h_banks[u][:].rearrange("p t (c i) -> p c t i", i=RUN),
-                    flat[:].rearrange("p (t j) -> p t j", t=PACK)[:, :, P * u : P * (u + 1)].rearrange("p t (c i) -> p c t i", i=RUN),
-                    ALU.mult,
+                nc.scalar.activation(planes[:, t], planes[:, t], ACT.Copy, bias=1.0, scale=cub_sb[:, b, t : t + 1])
+            z_half = z_bf[q][:, PACK * QUARTER * b : PACK * QUARTER * (b + 1)]
+            if on_vector:
+                for u in range(2):
+                    nc.vector.tensor_tensor(
+                        z_half[:, PACK * P * u : PACK * P * (u + 1)].rearrange("p (c i t) -> p c t i", i=RUN, t=PACK),
+                        h_banks[u][:].rearrange("p t (c i) -> p c t i", i=RUN),
+                        planes[:, :, P * u : P * (u + 1)].rearrange("p t (c i) -> p c t i", i=RUN),
+                        ALU.mult,
+                    )
+            else:
+                nc.gpsimd.tensor_tensor(
+                    z_half.rearrange("p (c i t) -> p c t i", i=LINE, t=PACK), by_line(h_sb[:]), by_line(factor[:]), ALU.mult
                 )
             if b == R_PASSES - 1:
                 z_w[q] = keep.tile([P, R_PASSES * QUARTER], U32, name="z_w%d" % q, align_bytes=64)
                 z_s[q] = keep.tile([P, R_PASSES * QUARTER], U8, name="z_s%d" % q, align_bytes=64)
                 nc.vector.quantize_mx(out=z_w[q][:].bitcast(FP8X4), scales=z_s[q][:], in_=z_bf[q][:])
 
-        moved = [keep.tile([P, S], F32, name="moved%d" % i, align_bytes=64) for i in range(N_TILES)]
+        moved = keep.tile([P, N_TILES, S], F32, name="moved", align_bytes=64)
 
         def drive(q, pair):
             for u in range(2):
@@ -219,63 +206,50 @@ def tile_list_oven_tray_refresh_kernel(tc, tab_words, tab_scales, offs, gT, w1, 
                 for e in range(2):
                     i = 2 * u + e
                     nc.scalar.activation(
-                        moved[i][:, QUARTER * q : QUARTER * (q + 1)], y_bank[:, e, :], ACT.Copy, scale=step_sb[:, i : i + 1]
+                        moved[:, i, QUARTER * q : QUARTER * (q + 1)], y_bank[:, e, :], ACT.Copy, scale=step_sb[:, i : i + 1]
                     )
 
-        def put(lo, hi, tiles, fused):
-            if not fused:
-                fresh = keep.tile([P, N_TILES - 1, QUARTER], F32, name="fresh%d" % lo, tag="slot%d" % [1, 2, 0][lo], align_bytes=64)
+        def put_summed(q, free, tiles):
+            cols = slice(QUARTER * q, QUARTER * (q + 1))
+            held = keep.tile([P, N_TILES - 1, QUARTER], F32, name="held%d" % q, tag=sum_slot[q], align_bytes=64)
+            nc.gpsimd.tensor_tensor(moved[:, 0:free, cols], picked[:, 0:free, cols], moved[:, 0:free, cols], ALU.add)
+            for i in range(free):
+                nc.vector.tensor_copy(state[i][:].indirect(listed(q, q + 1)), moved[:, i, cols])
+            nc.gpsimd.tensor_tensor(held[:, 0 : tiles - free], picked[:, free:tiles, cols], moved[:, free:tiles, cols], ALU.add)
+            for i in range(free, tiles):
+                nc.vector.tensor_copy(state[i][:].indirect(listed(q, q + 1)), held[:, i - free])
+
+        def put_last(lo, tiles):
+            cols = slice(QUARTER * lo, S)
             for i in tiles:
-                if fused:
-                    nc.vector.tensor_tensor(
-                        state[i][:].indirect(offsets[:, LIST_COLS * lo : LIST_COLS * hi]),
-                        picked[i][:, QUARTER * lo : QUARTER * hi],
-                        moved[i][:, QUARTER * lo : QUARTER * hi],
-                        ALU.add,
-                    )
-                    if hi == QUARTERS:
-                        nc.sync.dma_start(out[P * i : P * (i + 1), :], state[i][:])
-                    continue
-                for q in range(lo, hi):
-                    cols = slice(QUARTER * q, QUARTER * (q + 1))
-                    new = moved[i][:, cols] if i < [1, 3, 1][q] else fresh[:, i - 1]
-                    nc.gpsimd.tensor_tensor(new, picked[i][:, cols], moved[i][:, cols], ALU.add)
-                nc.vector.tensor_copy(
-                    state[i][:].indirect(offsets[:, LIST_COLS * lo : LIST_COLS * hi]),
-                    new,
-                )
-                if hi == QUARTERS:
-                    nc.sync.dma_start(out[P * i : P * (i + 1), :], state[i][:])
+                nc.vector.tensor_tensor(state[i][:].indirect(listed(lo, QUARTERS)), picked[:, i, cols], moved[:, i, cols], ALU.add)
+                nc.sync.dma_start(out[P * i : P * (i + 1), :], state[i][:])
 
-        gather_words(0, 0, 4)
+        gather_words(0, 0, QUARTERS)
         nc.vector.tensor_copy(v_s[:], tab_s[:].indirect(offsets[:]))
-        quantise_w1(0, 0)
-        quantise_w1(1, 0)
-        quantise_w1(2, 0)
-        gather_words(1, 0, 4)
+        for a in range(K_PASSES):
+            quantise_w1(a, 0)
+        gather_words(1, 0, QUARTERS)
         gather_words(2, 0, 1)
-        gather_words(2, 1, 4)
-        quantise_w1(0, 1)
-        quantise_w1(1, 1)
-        quantise_w1(2, 1)
-        modes(0, 0, 0)
-        modes(1, 0, 1)
-        modes(2, 0, 2)
+        gather_words(2, 1, QUARTERS)
+        for a in range(K_PASSES):
+            quantise_w1(a, 1)
+
+        for q in range(QUARTERS - 1):
+            modes(q, 0, q)
         modes(0, 1, 3)
         modes(1, 1, 0)
-        drive(0, 1)
-        gather_state(0, 0, 4)
-        gather_state(1, 0, 4)
-        gather_state(2, 0, 4)
-        gather_state(3, 0, 4)
-        put(0, 1, [0, 1, 2, 3], False)
-        modes(2, 1, 2)
-        drive(1, 2)
+        drive(0, 2)
+        for i in range(N_TILES):
+            nc.vector.tensor_copy(picked[:, i], state[i][:].indirect(offsets[:]))
+        put_summed(0, 1, N_TILES)
+        modes(2, 1, 3)
+        drive(1, 0)
         modes(3, 0, 1)
-        put(1, 2, [0, 1, 2, 3], False)
-        modes(3, 1, 0)
+        put_summed(1, N_TILES - 1, N_TILES)
+        modes(3, 1, 2)
         drive(2, 1)
         drive(3, 3)
-        put(2, 3, [0, 1], False)
-        put(3, 4, [0, 1], True)
-        put(2, 4, [2, 3], True)
+        put_summed(2, 1, 2)
+        put_last(3, (0, 1))
+        put_last(2, (2, 3))

@@ -63,26 +63,22 @@ def tile_list_oven_tray_refresh_kernel(tc, tab_words, tab_scales, offs, gT, w1, 
         def load_state(i):
             nc.sync.dma_start(state[i][:], gT[P * i : P * (i + 1), :])
 
-        def load_w4_scales(quadrants):
-            for Q in quadrants:
-                nc.sync.dma_start(
-                    w4_s[QUADRANT * Q : QUADRANT * Q + 4, :, :].bitcast(I32),
-                    w4_scales[:, 4 * Q : 4 * Q + 4, :].rearrange("b s n -> s b n").bitcast(I32),
-                )
-
-        nc.sync.dma_start(offsets[:], offs)
-        load_table(0)
         load_w1(0, 0)
+        load_w1(1, 0)
         for Q in range(P // QUADRANT):
             nc.sync.dma_start(
                 tab_s[QUADRANT * Q : QUADRANT * Q + 4 * K_PASSES, :].bitcast(I32),
                 tab_scales[:, 4 * Q : 4 * Q + 4, :].bitcast(I32),
             )
-        load_w1(1, 0)
-        load_w4_scales((0, 1))
+        nc.sync.dma_start(offsets[:], offs)
         load_w1(2, 0)
-        load_w4_scales((2, 3))
+        load_table(0)
         load_table(1)
+        for Q in range(P // QUADRANT):
+            nc.sync.dma_start(
+                w4_s[QUADRANT * Q : QUADRANT * Q + 4, :, :].bitcast(I32),
+                w4_scales[:, 4 * Q : 4 * Q + 4, :].rearrange("b s n -> s b n").bitcast(I32),
+            )
         nc.sync.dma_start(cub_sb[:], cub.rearrange("(b p t) -> p b t", b=R_PASSES, t=PACK))
         load_table(2)
         load_w1(0, 1)
@@ -225,11 +221,11 @@ def tile_list_oven_tray_refresh_kernel(tc, tab_words, tab_scales, offs, gT, w1, 
                 nc.vector.tensor_tensor(state[i][:].indirect(listed(lo, QUARTERS)), picked[:, i, cols], moved[:, i, cols], ALU.add)
                 nc.sync.dma_start(out[P * i : P * (i + 1), :], state[i][:])
 
-        gather_words(0, 0, QUARTERS)
         nc.vector.tensor_copy(v_s[:], tab_s[:].indirect(offsets[:]))
         for a in range(K_PASSES):
             quantise_w1(a, 0)
-        gather_words(1, 0, QUARTERS)
+        for a in range(K_PASSES - 1):
+            gather_words(a, 0, QUARTERS)
         gather_words(2, 0, 1)
         gather_words(2, 1, QUARTERS)
         for a in range(K_PASSES):

@@ -45,7 +45,7 @@ def tile_list_oven_tray_refresh_kernel(tc, tab_words, tab_scales, offs, gT, w1, 
         nc.gpsimd.memset(tab_s[:].bitcast(I32), 0)
         w4_s = keep.tile([P, R_PASSES, N], U8, name="w4_s", align_bytes=64)
         nc.vector.memset(w4_s[:].rearrange("p b n -> p (b n)").bitcast(I32), 0)
-        cub_sb = keep.tile([P, R_PASSES, PACK], F32, name="cub_sb")
+        cub_sb = [keep.tile([P, PACK], F32, name="cub_sb%d" % b) for b in range(R_PASSES)]
         step_sb = keep.tile([P, N_TILES], F32, name="step_sb")
         tab_w = [keep.tile([P, T], U32, name="tab_w%d" % a, align_bytes=64) for a in range(K_PASSES)]
         state = [keep.tile([P, T], F32, name="state%d" % i, align_bytes=64) for i in range(N_TILES)]
@@ -56,9 +56,12 @@ def tile_list_oven_tray_refresh_kernel(tc, tab_words, tab_scales, offs, gT, w1, 
             nc.sync.dma_start(tab_w[a][:].bitcast(I32), tab_words[a].rearrange("p t i -> p (t i)").bitcast(I32))
 
         def load_w1(a, b):
-            w1_raw[a, b] = keep.tile([P, PACK, PASS], F32, name="w1_raw%d%d" % (a, b), align_bytes=64)
+            w1_raw[a, b] = keep.tile([P, PACK, PASS], F32, name="w1_raw%d%d" % (a, b), tag="raw%d%d" % (a, b), align_bytes=64)
             rows = w1[PASS * a : PASS * (a + 1), PASS * b : PASS * (b + 1)]
             nc.sync.dma_start(w1_raw[a, b][:], rows.rearrange("(p j) c -> p j c", j=PACK))
+
+        def load_cub(b):
+            nc.sync.dma_start(cub_sb[b][:], cub[PASS * b : PASS * (b + 1)].rearrange("(p t) -> p t", t=PACK))
 
         def load_state(i):
             nc.sync.dma_start(state[i][:], gT[P * i : P * (i + 1), :])
@@ -79,26 +82,26 @@ def tile_list_oven_tray_refresh_kernel(tc, tab_words, tab_scales, offs, gT, w1, 
                 w4_s[QUADRANT * Q : QUADRANT * Q + 4, :, :].bitcast(I32),
                 w4_scales[:, 4 * Q : 4 * Q + 4, :].rearrange("b s n -> s b n").bitcast(I32),
             )
-        nc.sync.dma_start(cub_sb[:], cub.rearrange("(b p t) -> p b t", b=R_PASSES, t=PACK))
-        load_table(2)
-        load_w1(0, 1)
-        load_w1(1, 1)
-        load_state(0)
-        load_w1(2, 1)
-        for i in range(1, N_TILES):
-            load_state(i)
-        nc.sync.dma_start(w4_w[:].bitcast(I32), w4_words.rearrange("b p c -> p b c").bitcast(I32))
+        load_cub(0)
         with nc.allow_non_contiguous_dma(reason="one step value a partition"):
             nc.sync.dma_start(step_sb[:], step.rearrange("(i p) -> p i", p=P))
+        load_table(2)
+        for a in range(K_PASSES):
+            load_w1(a, 1)
+        for i in range(N_TILES - 1, 0, -1):
+            load_state(i)
+        load_cub(1)
+        nc.sync.dma_start(w4_w[:].bitcast(I32), w4_words.rearrange("b p c -> p b c").bitcast(I32))
+        load_state(0)
 
         v_w = [keep.tile([P, S], U32, name="v_w%d" % a, align_bytes=64) for a in range(K_PASSES)]
         v_s = keep.tile([P, S], U8, name="v_s", align_bytes=64)
-        picked = keep.tile([P, N_TILES, S], F32, name="picked", align_bytes=64)
+        arena = keep.tile([P, S + N_TILES * S], F32, name="arena", align_bytes=64)
+        picked = arena[:, S:].rearrange("p (i s) -> p i s", i=N_TILES)
         w1_w, w1_s, z_bf, z_w, z_s = {}, {}, {}, {}, {}
 
-        z_slot = {0: "slot0", 1: "slot1", 2: "slot0", 3: "slot0"}
-        h_slot = {(0, 0): "slot1", (3, 0): "slot2"}
-        sum_slot = {0: "slot1", 1: "slot2", 2: "slot0"}
+        work_slot = {(0, 0): "raw00", (1, 0): "raw10", (0, 1): "raw20", (1, 1): "raw01", (2, 0): "raw20", (2, 1): "raw01", (3, 0): "raw20", (3, 1): "raw01"}
+        HALF = PACK * QUARTER
 
         def listed(lo, hi):
             return offsets[:, LIST_COLS * lo : LIST_COLS * hi]
@@ -108,10 +111,10 @@ def tile_list_oven_tray_refresh_kernel(tc, tab_words, tab_scales, offs, gT, w1, 
 
         def quantise_w1(a, b):
             if (a, b) == (K_PASSES - 1, R_PASSES - 1):
-                w1_bf = keep.tile([P, PACK * PASS], BF16, name="w1_bf_last", tag="slot0", align_bytes=64)
+                w1_bf = arena[:, 0:S].bitcast(BF16)
             else:
-                w1_bf = ring.tile([P, PACK * PASS], BF16, name="w1_bf", tag="w1_bf", align_bytes=64)
-            dst = w1_bf[:].rearrange("p (t m j) -> p m j t", t=PACK, j=PACK)
+                w1_bf = ring.tile([P, PACK * PASS], BF16, name="w1_bf", tag="w1_bf", align_bytes=64)[:]
+            dst = w1_bf.rearrange("p (t m j) -> p m j t", t=PACK, j=PACK)
             src = w1_raw[a, b][:].rearrange("p j (m t) -> p m j t", t=PACK)
             if b == 0:
                 nc.scalar.activation(dst, src, ACT.Copy)
@@ -119,77 +122,66 @@ def tile_list_oven_tray_refresh_kernel(tc, tab_words, tab_scales, offs, gT, w1, 
                 nc.vector.tensor_copy(dst, src)
             w1_w[a, b] = keep.tile([P, PASS], U32, name="w1_w%d%d" % (a, b), align_bytes=64)
             w1_s[a, b] = keep.tile([P, PASS], U8, name="w1_s%d%d" % (a, b), align_bytes=64)
-            nc.vector.quantize_mx(out=w1_w[a, b][:].bitcast(FP8X4), scales=w1_s[a, b][:], in_=w1_bf[:])
+            nc.vector.quantize_mx(out=w1_w[a, b][:].bitcast(FP8X4), scales=w1_s[a, b][:], in_=w1_bf)
 
         def by_line(ap):
             return ap.rearrange("p (c t i) -> p c t i", t=PACK, i=LINE)
 
+        z_order = {}
+
         def modes(q, b, pair):
-            on_vector = (q, b) in VECTOR_PRODUCTS
-            if (q, b) in h_slot:
-                h_sb = keep.tile([P, PACK * QUARTER], F32, name="h_held", tag=h_slot[q, b], align_bytes=64)
-            elif not on_vector:
-                h_sb = ring.tile([P, PACK * QUARTER], F32, name="h_sb", tag="h_sb", align_bytes=64)
-            factor = ring.tile([P, PACK * QUARTER], F32, name="factor", tag="factor", bufs=FACTOR_RING, align_bytes=64)
-            if on_vector:
-                planes = factor[:].rearrange("p (t j) -> p t j", t=PACK)
-            else:
-                planes = by_line(factor[:]).rearrange("p c t i -> p t c i")
-            if b == 0:
-                z_bf[q] = keep.tile([P, R_PASSES * PACK * QUARTER], BF16, name="z_bf%d" % q, tag=z_slot[q], align_bytes=64)
-            h_banks = []
+            work = keep.tile([P, 2 * HALF], F32, name="work%d%d" % (q, b), tag=work_slot[q, b], align_bytes=64)
+            h_sb, factor = work[:, 0:HALF], work[:, HALF : 2 * HALF]
+            planes = by_line(factor).rearrange("p c t i -> p t c i")
+            if (q, b) == (0, 0):
+                ring3 = arena[:, 0 : 3 * HALF // 2].bitcast(BF16)
+                z_bf[0], z_order[0] = ring3[:, HALF : 3 * HALF], (0, 1)
+                z_bf[1], z_order[1] = ring3[:, 0 : 2 * HALF], (0, 1)
+            elif b == 0 and q > 1:
+                z_tile = keep.tile([P, 2 * HALF], BF16, name="z%d" % q, tag="slotB" if q == 2 else "slotC", align_bytes=64)
+                z_bf[q], z_order[q] = z_tile[:], (0, 1)
             for u in range(2):
                 h_bank = psum.tile([P, PACK, P], F32, name="h_bank", tag="bank%d" % (2 * pair + u))
-                h_banks.append(h_bank)
                 entries = slice(QUARTER * q + P * u, QUARTER * q + P * (u + 1))
-                for t in range(PACK):
-                    for a in range(K_PASSES):
+                for a in range(K_PASSES):
+                    for t in range(PACK):
                         nc.tensor.matmul_mx(
                             out=h_bank[:, t, :],
                             lhsT=w1_w[a, b][:, P * t : P * (t + 1)].bitcast(FP8X4),
                             lhsT_scale=w1_s[a, b][:, P * t : P * (t + 1)],
                             rhs=v_w[a][:, entries].bitcast(FP8X4),
                             rhs_scale=v_s[4 * a : P, entries],
-                            start=(a == 0),
-                            stop=(a == K_PASSES - 1),
+                            start=(a == 0 and t == 0),
+                            stop=(a == K_PASSES - 1 and t == PACK - 1),
                         )
-                if on_vector:
-                    nc.scalar.activation(planes[:, :, P * u : P * (u + 1)], h_bank[:], ACT.Square)
-                else:
-                    h_lines = h_bank[:].rearrange("p t (c i) -> p c t i", i=LINE)
-                    part = slice(PACK * P * u, PACK * P * (u + 1))
-                    nc.scalar.activation(by_line(factor[:, part]), h_lines, ACT.Square)
-                    nc.scalar.copy(by_line(h_sb[:, part]), h_lines)
+                h_lines = h_bank[:].rearrange("p t (c i) -> p c t i", i=LINE)
+                part = slice(PACK * P * u, PACK * P * (u + 1))
+                nc.scalar.activation(by_line(factor[:, part]), h_lines, ACT.Square)
+                nc.scalar.copy(by_line(h_sb[:, part]), h_lines)
             for t in range(PACK):
-                nc.scalar.activation(planes[:, t], planes[:, t], ACT.Copy, bias=1.0, scale=cub_sb[:, b, t : t + 1])
-            z_half = z_bf[q][:, PACK * QUARTER * b : PACK * QUARTER * (b + 1)]
-            if on_vector:
-                for u in range(2):
-                    nc.vector.tensor_tensor(
-                        z_half[:, PACK * P * u : PACK * P * (u + 1)].rearrange("p (c i t) -> p c t i", i=RUN, t=PACK),
-                        h_banks[u][:].rearrange("p t (c i) -> p c t i", i=RUN),
-                        planes[:, :, P * u : P * (u + 1)].rearrange("p t (c i) -> p c t i", i=RUN),
-                        ALU.mult,
-                    )
-            else:
-                nc.gpsimd.tensor_tensor(
-                    z_half.rearrange("p (c i t) -> p c t i", i=LINE, t=PACK), by_line(h_sb[:]), by_line(factor[:]), ALU.mult
-                )
+                if (q, b) == (0, 1):
+                    nc.gpsimd.tensor_scalar(planes[:, t], planes[:, t], cub_sb[b][:, t : t + 1], 1.0, ALU.mult, ALU.add)
+                else:
+                    nc.scalar.activation(planes[:, t], planes[:, t], ACT.Copy, bias=1.0, scale=cub_sb[b][:, t : t + 1])
+            place = z_order[q][b]
+            z_half = z_bf[q][:, HALF * place : HALF * (place + 1)]
+            nc.gpsimd.tensor_tensor(z_half.rearrange("p (c i t) -> p c t i", i=LINE, t=PACK), by_line(h_sb), by_line(factor), ALU.mult)
             if b == R_PASSES - 1:
                 z_w[q] = keep.tile([P, R_PASSES * QUARTER], U32, name="z_w%d" % q, align_bytes=64)
                 z_s[q] = keep.tile([P, R_PASSES * QUARTER], U8, name="z_s%d" % q, align_bytes=64)
-                nc.vector.quantize_mx(out=z_w[q][:].bitcast(FP8X4), scales=z_s[q][:], in_=z_bf[q][:])
+                nc.vector.quantize_mx(out=z_w[q][:].bitcast(FP8X4), scales=z_s[q][:], in_=z_bf[q])
 
         moved = keep.tile([P, N_TILES, S], F32, name="moved", align_bytes=64)
+        moved_at = {(q, i): moved[:, i, QUARTER * q : QUARTER * (q + 1)] for q in range(QUARTERS) for i in range(N_TILES)}
 
         def drive(q, pair):
-            for u in range(2):
+            for u in (1, 0):
                 y_bank = psum.tile([P, 2, QUARTER], F32, name="y_bank", tag="bank%d" % (2 * pair + u))
                 for e in range(2):
                     i = 2 * u + e
                     for c in range(0, QUARTER, P):
                         for b in range(R_PASSES):
-                            z_cols = slice(QUARTER * b + c, QUARTER * b + c + P)
+                            z_cols = slice(QUARTER * z_order[q][b] + c, QUARTER * z_order[q][b] + c + P)
                             nc.tensor.matmul_mx(
                                 out=y_bank[:, e, c : c + P],
                                 lhsT=w4_w[:, b, 2 * P * i : 2 * P * (i + 1)].bitcast(FP4X4),
@@ -199,27 +191,26 @@ def tile_list_oven_tray_refresh_kernel(tc, tab_words, tab_scales, offs, gT, w1, 
                                 start=(b == 0),
                                 stop=(b == R_PASSES - 1),
                             )
-                for e in range(2):
+                for e in (1, 0):
                     i = 2 * u + e
-                    nc.scalar.activation(
-                        moved[:, i, QUARTER * q : QUARTER * (q + 1)], y_bank[:, e, :], ACT.Copy, scale=step_sb[:, i : i + 1]
-                    )
+                    nc.scalar.activation(moved_at[q, i], y_bank[:, e, :], ACT.Copy, scale=step_sb[:, i : i + 1])
 
-        def put_summed(q, free, tiles):
+        def put_summed(q, tiles, slot):
             cols = slice(QUARTER * q, QUARTER * (q + 1))
-            held = keep.tile([P, N_TILES - 1, QUARTER], F32, name="held%d" % q, tag=sum_slot[q], align_bytes=64)
-            nc.gpsimd.tensor_tensor(moved[:, 0:free, cols], picked[:, 0:free, cols], moved[:, 0:free, cols], ALU.add)
-            for i in range(free):
-                nc.vector.tensor_copy(state[i][:].indirect(listed(q, q + 1)), moved[:, i, cols])
-            nc.gpsimd.tensor_tensor(held[:, 0 : tiles - free], picked[:, free:tiles, cols], moved[:, free:tiles, cols], ALU.add)
-            for i in range(free, tiles):
-                nc.vector.tensor_copy(state[i][:].indirect(listed(q, q + 1)), held[:, i - free])
+            n = tiles.stop - tiles.start
+            if slot == "arena":
+                new = arena[:, 0 : n * QUARTER].rearrange("p (e j) -> p e j", e=n)
+            else:
+                new = keep.tile([P, n, QUARTER], F32, name="new%d%d" % (q, tiles.start), tag=slot, align_bytes=64)[:]
+            nc.gpsimd.tensor_tensor(new, picked[:, tiles, cols], moved[:, tiles, cols], ALU.add)
+            for e in reversed(range(n)):
+                nc.vector.tensor_copy(state[tiles.start + e][:].indirect(listed(q, q + 1)), new[:, e])
 
-        def put_last(lo, tiles):
-            cols = slice(QUARTER * lo, S)
-            for i in tiles:
-                nc.vector.tensor_tensor(state[i][:].indirect(listed(lo, QUARTERS)), picked[:, i, cols], moved[:, i, cols], ALU.add)
-                nc.sync.dma_start(out[P * i : P * (i + 1), :], state[i][:])
+        def put_fused(lo, hi, i, values):
+            nc.vector.tensor_tensor(state[i][:].indirect(listed(lo, hi)), picked[:, i, QUARTER * lo : QUARTER * hi], values, ALU.add)
+
+        def store(i):
+            nc.sync.dma_start(out[P * i : P * (i + 1), :], state[i][:])
 
         nc.vector.tensor_copy(v_s[:], tab_s[:].indirect(offsets[:]))
         for a in range(K_PASSES):
@@ -230,22 +221,34 @@ def tile_list_oven_tray_refresh_kernel(tc, tab_words, tab_scales, offs, gT, w1, 
         gather_words(2, 1, QUARTERS)
         for a in range(K_PASSES):
             quantise_w1(a, 1)
-
-        for q in range(QUARTERS - 1):
-            modes(q, 0, q)
-        modes(0, 1, 3)
-        modes(1, 1, 0)
-        drive(0, 2)
-        for i in range(N_TILES):
+        for i in range(N_TILES - 1, 0, -1):
             nc.vector.tensor_copy(picked[:, i], state[i][:].indirect(offsets[:]))
-        put_summed(0, 1, N_TILES)
-        modes(2, 1, 3)
-        drive(1, 0)
-        modes(3, 0, 1)
-        put_summed(1, N_TILES - 1, N_TILES)
+
+        modes(0, 0, 0)
+        modes(1, 0, 1)
+        modes(0, 1, 2)
+        nc.vector.tensor_copy(picked[:, 0], state[0][:].indirect(offsets[:]))
+        modes(1, 1, 3)
+        drive(0, 1)
+        put_summed(0, slice(3, 4), "slotB")
+        put_summed(0, slice(0, 3), "arena")
+        modes(2, 0, 2)
+        modes(2, 1, 1)
+        drive(1, 1)
+        put_summed(1, slice(3, 4), "slotC")
+        put_summed(1, slice(0, 3), "slotB")
+        modes(3, 0, 3)
         modes(3, 1, 2)
-        drive(2, 1)
-        drive(3, 3)
-        put_summed(2, 1, 2)
-        put_last(3, (0, 1))
-        put_last(2, (2, 3))
+        late = keep.tile([P, N_TILES * QUARTER], F32, name="late", tag="raw01", align_bytes=64)
+        for i in range(N_TILES - 1):
+            moved_at[2, i] = late[:, QUARTER * (2 - i) : QUARTER * (3 - i)]
+        moved_at[3, 0] = late[:, QUARTER * 3 : QUARTER * 4]
+        drive(2, 2)
+        for i in range(N_TILES - 1, 0, -1):
+            put_fused(2, 3, i, moved_at[2, i])
+        drive(3, 0)
+        for i in range(N_TILES - 1, 0, -1):
+            put_fused(3, 4, i, moved_at[3, i])
+            store(i)
+        put_fused(2, 4, 0, late[:, QUARTER * 2 : QUARTER * 4])
+        store(0)

@@ -66,41 +66,42 @@ def tile_list_oven_tray_refresh_kernel(tc, tab_words, tab_scales, offs, gT, w1, 
         def load_state(i):
             nc.sync.dma_start(state[i][:], gT[P * i : P * (i + 1), :])
 
+        nc.sync.dma_start(offsets[:], offs)
+        load_table(0)
         load_w1(0, 0)
-        load_w1(1, 0)
         for Q in range(P // QUADRANT):
             nc.sync.dma_start(
                 tab_s[QUADRANT * Q : QUADRANT * Q + 4 * K_PASSES, :].bitcast(I32),
                 tab_scales[:, 4 * Q : 4 * Q + 4, :].bitcast(I32),
             )
-        nc.sync.dma_start(offsets[:], offs)
-        load_w1(2, 0)
-        load_table(0)
         load_table(1)
+        load_w1(1, 0)
+        load_w1(2, 0)
+        load_cub(0)
+        load_table(2)
+        for a in range(K_PASSES):
+            load_w1(a, 1)
+        load_state(3)
+        load_state(2)
+        load_cub(1)
+        load_state(1)
+        nc.sync.dma_start(w4_w[:].bitcast(I32), w4_words.rearrange("b p c -> p b c").bitcast(I32))
         for Q in range(P // QUADRANT):
             nc.sync.dma_start(
                 w4_s[QUADRANT * Q : QUADRANT * Q + 4, :, :].bitcast(I32),
                 w4_scales[:, 4 * Q : 4 * Q + 4, :].rearrange("b s n -> s b n").bitcast(I32),
             )
-        load_cub(0)
+        load_state(0)
         with nc.allow_non_contiguous_dma(reason="one step value a partition"):
             nc.sync.dma_start(step_sb[:], step.rearrange("(i p) -> p i", p=P))
-        load_table(2)
-        for a in range(K_PASSES):
-            load_w1(a, 1)
-        for i in range(N_TILES - 1, 0, -1):
-            load_state(i)
-        load_cub(1)
-        nc.sync.dma_start(w4_w[:].bitcast(I32), w4_words.rearrange("b p c -> p b c").bitcast(I32))
-        load_state(0)
 
         v_w = [keep.tile([P, S], U32, name="v_w%d" % a, align_bytes=64) for a in range(K_PASSES)]
         v_s = keep.tile([P, S], U8, name="v_s", align_bytes=64)
-        arena = keep.tile([P, S + N_TILES * S], F32, name="arena", align_bytes=64)
-        picked = arena[:, S:].rearrange("p (i s) -> p i s", i=N_TILES)
+        arena = keep.tile([P, 2 * S - QUARTER + N_TILES * S], F32, name="arena", align_bytes=64)
+        picked = arena[:, 2 * S - QUARTER :].rearrange("p (i s) -> p i s", i=N_TILES)
         w1_w, w1_s, z_bf, z_w, z_s = {}, {}, {}, {}, {}
 
-        work_slot = {(0, 0): "raw00", (1, 0): "raw10", (0, 1): "raw20", (1, 1): "raw01", (2, 0): "raw20", (2, 1): "raw01", (3, 0): "raw20", (3, 1): "raw01"}
+        work_slot = {(0, 0): "raw00", (1, 0): "raw10", (2, 0): "raw20", (2, 1): "raw01", (3, 0): "raw11", (3, 1): "raw01"}
         HALF = PACK * QUARTER
 
         def listed(lo, hi):
@@ -111,12 +112,15 @@ def tile_list_oven_tray_refresh_kernel(tc, tab_words, tab_scales, offs, gT, w1, 
 
         def quantise_w1(a, b):
             if (a, b) == (K_PASSES - 1, R_PASSES - 1):
-                w1_bf = arena[:, 0:S].bitcast(BF16)
+                w1_bf = arena[:, S : 2 * S].bitcast(BF16)
             else:
                 w1_bf = ring.tile([P, PACK * PASS], BF16, name="w1_bf", tag="w1_bf", align_bytes=64)[:]
             dst = w1_bf.rearrange("p (t m j) -> p m j t", t=PACK, j=PACK)
             src = w1_raw[a, b][:].rearrange("p j (m t) -> p m j t", t=PACK)
-            if b == 0:
+            if (a, b) == (K_PASSES - 1, 0):
+                nc.scalar.activation(dst[:, 0 : P // 2], src[:, 0 : P // 2], ACT.Copy)
+                nc.vector.tensor_copy(dst[:, P // 2 : P], src[:, P // 2 : P])
+            elif b == 0:
                 nc.scalar.activation(dst, src, ACT.Copy)
             else:
                 nc.vector.tensor_copy(dst, src)
@@ -130,18 +134,34 @@ def tile_list_oven_tray_refresh_kernel(tc, tab_words, tab_scales, offs, gT, w1, 
         z_order = {}
 
         def modes(q, b, pair):
-            work = keep.tile([P, 2 * HALF], F32, name="work%d%d" % (q, b), tag=work_slot[q, b], align_bytes=64)
-            h_sb, factor = work[:, 0:HALF], work[:, HALF : 2 * HALF]
-            planes = by_line(factor).rearrange("p c t i -> p t c i")
+            on_vector = (q, b) in VECTOR_PRODUCTS
+            if on_vector:
+                square = keep.tile([P, PACK, QUARTER], F32, name="square", tag="square", align_bytes=64)
+                planes = keep.tile([P, PACK, QUARTER], F32, name="factor%d" % q, align_bytes=64)
+            else:
+                work = keep.tile([P, 2 * HALF], F32, name="work%d%d" % (q, b), tag=work_slot[q, b], align_bytes=64)
+                h_sb, factor = work[:, 0:HALF], work[:, HALF : 2 * HALF]
+                planes = by_line(factor).rearrange("p c t i -> p t c i")
+                square = planes
+                squares = factor
+                if q == 2:
+                    squares = keep.tile([P, HALF], F32, name="square", tag=("square", "raw11")[b], align_bytes=64)[:]
+                    square = by_line(squares).rearrange("p c t i -> p t c i")
+                if (q, b) == (2, 1):
+                    h_sb = keep.tile([P, HALF], F32, name="h21", tag="slotB", align_bytes=64)[:]
+            h_banks = []
             if (q, b) == (0, 0):
-                ring3 = arena[:, 0 : 3 * HALF // 2].bitcast(BF16)
-                z_bf[0], z_order[0] = ring3[:, HALF : 3 * HALF], (0, 1)
-                z_bf[1], z_order[1] = ring3[:, 0 : 2 * HALF], (0, 1)
-            elif b == 0 and q > 1:
-                z_tile = keep.tile([P, 2 * HALF], BF16, name="z%d" % q, tag="slotB" if q == 2 else "slotC", align_bytes=64)
+                ring3 = arena[:, 0 : 2 * S].bitcast(BF16)
+                z_bf[0], z_order[0] = ring3[:, HALF : 3 * HALF], (1, 0)
+                z_bf[1], z_order[1] = ring3[:, 2 * HALF : 4 * HALF], (1, 0)
+            elif (q, b) == (2, 0):
+                z_bf[q], z_order[q] = arena[:, 0:S].bitcast(BF16), (1, 0)
+            elif (q, b) == (3, 0):
+                z_tile = keep.tile([P, 2 * HALF], BF16, name="z%d" % q, tag="slotB", align_bytes=64)
                 z_bf[q], z_order[q] = z_tile[:], (0, 1)
             for u in range(2):
                 h_bank = psum.tile([P, PACK, P], F32, name="h_bank", tag="bank%d" % (2 * pair + u))
+                h_banks.append(h_bank)
                 entries = slice(QUARTER * q + P * u, QUARTER * q + P * (u + 1))
                 for a in range(K_PASSES):
                     for t in range(PACK):
@@ -154,18 +174,27 @@ def tile_list_oven_tray_refresh_kernel(tc, tab_words, tab_scales, offs, gT, w1, 
                             start=(a == 0 and t == 0),
                             stop=(a == K_PASSES - 1 and t == PACK - 1),
                         )
+                if on_vector:
+                    nc.scalar.activation(square[:, :, P * u : P * (u + 1)], h_bank[:], ACT.Square)
+                    continue
                 h_lines = h_bank[:].rearrange("p t (c i) -> p c t i", i=LINE)
                 part = slice(PACK * P * u, PACK * P * (u + 1))
-                nc.scalar.activation(by_line(factor[:, part]), h_lines, ACT.Square)
+                nc.scalar.activation(by_line(squares[:, part]), h_lines, ACT.Square)
                 nc.scalar.copy(by_line(h_sb[:, part]), h_lines)
             for t in range(PACK):
-                if (q, b) == (0, 1):
-                    nc.gpsimd.tensor_scalar(planes[:, t], planes[:, t], cub_sb[b][:, t : t + 1], 1.0, ALU.mult, ALU.add)
-                else:
-                    nc.scalar.activation(planes[:, t], planes[:, t], ACT.Copy, bias=1.0, scale=cub_sb[b][:, t : t + 1])
+                nc.scalar.activation(planes[:, t], square[:, t], ACT.Copy, bias=1.0, scale=cub_sb[b][:, t : t + 1])
             place = z_order[q][b]
             z_half = z_bf[q][:, HALF * place : HALF * (place + 1)]
-            nc.gpsimd.tensor_tensor(z_half.rearrange("p (c i t) -> p c t i", i=LINE, t=PACK), by_line(h_sb), by_line(factor), ALU.mult)
+            if on_vector:
+                for u in range(2):
+                    nc.vector.tensor_tensor(
+                        z_half[:, PACK * P * u : PACK * P * (u + 1)].rearrange("p (c i t) -> p c t i", i=RUN, t=PACK),
+                        h_banks[u][:].rearrange("p t (c i) -> p c t i", i=RUN),
+                        planes[:, :, P * u : P * (u + 1)].rearrange("p t (c i) -> p c t i", i=RUN),
+                        ALU.mult,
+                    )
+            else:
+                nc.gpsimd.tensor_tensor(z_half.rearrange("p (c i t) -> p c t i", i=LINE, t=PACK), by_line(h_sb), by_line(factor), ALU.mult)
             if b == R_PASSES - 1:
                 z_w[q] = keep.tile([P, R_PASSES * QUARTER], U32, name="z_w%d" % q, align_bytes=64)
                 z_s[q] = keep.tile([P, R_PASSES * QUARTER], U8, name="z_s%d" % q, align_bytes=64)
@@ -198,11 +227,11 @@ def tile_list_oven_tray_refresh_kernel(tc, tab_words, tab_scales, offs, gT, w1, 
         def put_summed(q, tiles, slot):
             cols = slice(QUARTER * q, QUARTER * (q + 1))
             n = tiles.stop - tiles.start
-            if slot == "arena":
-                new = arena[:, 0 : n * QUARTER].rearrange("p (e j) -> p e j", e=n)
+            if isinstance(slot, int):
+                new = arena[:, slot : slot + n * QUARTER].rearrange("p (e j) -> p e j", e=n)
             else:
                 new = keep.tile([P, n, QUARTER], F32, name="new%d%d" % (q, tiles.start), tag=slot, align_bytes=64)[:]
-            nc.gpsimd.tensor_tensor(new, picked[:, tiles, cols], moved[:, tiles, cols], ALU.add)
+            nc.gpsimd.tensor_tensor(new, picked[:, tiles, cols], first[:, tiles] if q == 0 else moved[:, tiles, cols], ALU.add)
             for e in reversed(range(n)):
                 nc.vector.tensor_copy(state[tiles.start + e][:].indirect(listed(q, q + 1)), new[:, e])
 
@@ -212,11 +241,12 @@ def tile_list_oven_tray_refresh_kernel(tc, tab_words, tab_scales, offs, gT, w1, 
         def store(i):
             nc.sync.dma_start(out[P * i : P * (i + 1), :], state[i][:])
 
+        gather_words(0, 0, QUARTERS)
         nc.vector.tensor_copy(v_s[:], tab_s[:].indirect(offsets[:]))
-        for a in range(K_PASSES):
-            quantise_w1(a, 0)
-        for a in range(K_PASSES - 1):
-            gather_words(a, 0, QUARTERS)
+        quantise_w1(0, 0)
+        gather_words(1, 0, QUARTERS)
+        quantise_w1(1, 0)
+        quantise_w1(2, 0)
         gather_words(2, 0, 1)
         gather_words(2, 1, QUARTERS)
         for a in range(K_PASSES):
@@ -227,28 +257,32 @@ def tile_list_oven_tray_refresh_kernel(tc, tab_words, tab_scales, offs, gT, w1, 
         modes(0, 0, 0)
         modes(1, 0, 1)
         modes(0, 1, 2)
-        nc.vector.tensor_copy(picked[:, 0], state[0][:].indirect(offsets[:]))
+        modes(2, 0, 0)
         modes(1, 1, 3)
+        nc.vector.tensor_copy(picked[:, 0], state[0][:].indirect(offsets[:]))
+        first = keep.tile([P, N_TILES, QUARTER], F32, name="first", tag="square", align_bytes=64)
+        for i in range(N_TILES):
+            moved_at[0, i] = first[:, i]
         drive(0, 1)
-        put_summed(0, slice(3, 4), "slotB")
-        put_summed(0, slice(0, 3), "arena")
-        modes(2, 0, 2)
+        put_summed(0, slice(2, 4), S)
+        put_summed(0, slice(1, 2), S + 2 * QUARTER)
         modes(2, 1, 1)
+        put_summed(0, slice(0, 1), "slotB")
         drive(1, 1)
-        put_summed(1, slice(3, 4), "slotC")
-        put_summed(1, slice(0, 3), "slotB")
-        modes(3, 0, 3)
-        modes(3, 1, 2)
-        late = keep.tile([P, N_TILES * QUARTER], F32, name="late", tag="raw01", align_bytes=64)
-        for i in range(N_TILES - 1):
-            moved_at[2, i] = late[:, QUARTER * (2 - i) : QUARTER * (3 - i)]
-        moved_at[3, 0] = late[:, QUARTER * 3 : QUARTER * 4]
-        drive(2, 2)
+        put_summed(1, slice(2, 4), 0)
+        put_summed(1, slice(0, 2), 2 * QUARTER)
+        modes(3, 0, 2)
+        modes(3, 1, 3)
+        late = keep.tile([P, (N_TILES + 1) * QUARTER], F32, name="late", tag="raw01", align_bytes=64)
+        for i in range(N_TILES):
+            moved_at[2, i] = late[:, QUARTER * (3 - i) : QUARTER * (4 - i)]
+        moved_at[3, 0] = late[:, QUARTER * 4 : QUARTER * 5]
+        drive(2, 3)
         for i in range(N_TILES - 1, 0, -1):
             put_fused(2, 3, i, moved_at[2, i])
         drive(3, 0)
         for i in range(N_TILES - 1, 0, -1):
             put_fused(3, 4, i, moved_at[3, i])
             store(i)
-        put_fused(2, 4, 0, late[:, QUARTER * 2 : QUARTER * 4])
+        put_fused(2, 4, 0, late[:, QUARTER * 3 : QUARTER * 5])
         store(0)

@@ -77,6 +77,11 @@ def tile_list_oven_tray_refresh_kernel(tc, tab_words, tab_scales, offs, gT, w1, 
         load_table(1)
         load_w1(1, 0)
         load_w1(2, 0)
+        for Q in range(P // QUADRANT):
+            nc.sync.dma_start(
+                w4_s[QUADRANT * Q : QUADRANT * Q + 4, :, :].bitcast(I32),
+                w4_scales[:, 4 * Q : 4 * Q + 4, :].rearrange("b s n -> s b n").bitcast(I32),
+            )
         load_cub(0)
         load_table(2)
         for a in range(K_PASSES):
@@ -84,24 +89,27 @@ def tile_list_oven_tray_refresh_kernel(tc, tab_words, tab_scales, offs, gT, w1, 
         load_state(3)
         load_state(2)
         load_cub(1)
-        load_state(1)
         nc.sync.dma_start(w4_w[:].bitcast(I32), w4_words.rearrange("b p c -> p b c").bitcast(I32))
-        for Q in range(P // QUADRANT):
-            nc.sync.dma_start(
-                w4_s[QUADRANT * Q : QUADRANT * Q + 4, :, :].bitcast(I32),
-                w4_scales[:, 4 * Q : 4 * Q + 4, :].rearrange("b s n -> s b n").bitcast(I32),
-            )
-        load_state(0)
         with nc.allow_non_contiguous_dma(reason="one step value a partition"):
             nc.sync.dma_start(step_sb[:], step.rearrange("(i p) -> p i", p=P))
+        load_state(1)
+        load_state(0)
 
         v_w = [keep.tile([P, S], U32, name="v_w%d" % a, align_bytes=64) for a in range(K_PASSES)]
         v_s = keep.tile([P, S], U8, name="v_s", align_bytes=64)
-        arena = keep.tile([P, 2 * S - QUARTER + N_TILES * S], F32, name="arena", align_bytes=64)
-        picked = arena[:, 2 * S - QUARTER :].rearrange("p (i s) -> p i s", i=N_TILES)
+        ZH = 2 * QUARTER
+        Z1, Z2, Z0 = S - QUARTER, S - QUARTER + 2 * ZH, S - QUARTER + 3 * ZH
+        P1 = Z0 + ZH
+        arena = keep.tile([P, P1 + 3 * S], F32, name="arena", align_bytes=64)
+        lower = arena[:, 0 : 2 * P1].rearrange("p (i s) -> p i s", i=2)[:, :, 0:S]
+        upper = arena[:, P1 + S :].rearrange("p (i s) -> p i s", i=2)
+
+        def picked(lo, hi, cols):
+            return lower[:, lo:hi, cols] if lo < 2 else upper[:, lo - 2 : hi - 2, cols]
+
         w1_w, w1_s, z_bf, z_w, z_s = {}, {}, {}, {}, {}
 
-        work_slot = {(0, 0): "raw00", (1, 0): "raw10", (2, 0): "raw20", (2, 1): "raw01", (3, 0): "raw11", (3, 1): "raw01"}
+        work_slot = {(0, 0): "raw00", (1, 0): "raw10", (2, 0): "raw20", (2, 1): "raw01", (3, 0): "raw11", (3, 1): "raw21"}
         HALF = PACK * QUARTER
 
         def listed(lo, hi):
@@ -112,7 +120,7 @@ def tile_list_oven_tray_refresh_kernel(tc, tab_words, tab_scales, offs, gT, w1, 
 
         def quantise_w1(a, b):
             if (a, b) == (K_PASSES - 1, R_PASSES - 1):
-                w1_bf = arena[:, S : 2 * S].bitcast(BF16)
+                w1_bf = arena[:, Z2 - QUARTER : Z2 - QUARTER + S].bitcast(BF16)
             else:
                 w1_bf = ring.tile([P, PACK * PASS], BF16, name="w1_bf", tag="w1_bf", align_bytes=64)[:]
             dst = w1_bf.rearrange("p (t m j) -> p m j t", t=PACK, j=PACK)
@@ -136,29 +144,32 @@ def tile_list_oven_tray_refresh_kernel(tc, tab_words, tab_scales, offs, gT, w1, 
         def modes(q, b, pair):
             on_vector = (q, b) in VECTOR_PRODUCTS
             if on_vector:
-                square = keep.tile([P, PACK, QUARTER], F32, name="square", tag="square", align_bytes=64)
-                planes = keep.tile([P, PACK, QUARTER], F32, name="factor%d" % q, align_bytes=64)
+                if q == 0:
+                    square = keep.tile([P, PACK, QUARTER], F32, name="square", tag="square", align_bytes=64)[:]
+                else:
+                    square = keep.tile([P, PACK, QUARTER], F32, name="square11", tag="square2", align_bytes=64)[:]
+                planes = keep.tile([P, PACK, QUARTER], F32, name="factor%d" % q, tag="factor%d" % q, align_bytes=64)
             else:
                 work = keep.tile([P, 2 * HALF], F32, name="work%d%d" % (q, b), tag=work_slot[q, b], align_bytes=64)
                 h_sb, factor = work[:, 0:HALF], work[:, HALF : 2 * HALF]
                 planes = by_line(factor).rearrange("p c t i -> p t c i")
                 square = planes
                 squares = factor
-                if q == 2:
-                    squares = keep.tile([P, HALF], F32, name="square", tag=("square", "raw11")[b], align_bytes=64)[:]
-                    square = by_line(squares).rearrange("p c t i -> p t c i")
+                if (q, b) == (2, 0):
+                    factor = keep.tile([P, HALF], F32, name="factor20", tag="square", align_bytes=64)[:]
+                    squares = keep.tile([P, HALF], F32, name="square20", tag="square2", align_bytes=64)[:]
+                    planes = by_line(factor).rearrange("p c t i -> p t c i")
                 if (q, b) == (2, 1):
-                    h_sb = keep.tile([P, HALF], F32, name="h21", tag="slotB", align_bytes=64)[:]
+                    h_sb, squares = both[:, 0:HALF], both[:, HALF : 2 * HALF]
+                square = by_line(squares).rearrange("p c t i -> p t c i")
             h_banks = []
             if (q, b) == (0, 0):
-                ring3 = arena[:, 0 : 2 * S].bitcast(BF16)
-                z_bf[0], z_order[0] = ring3[:, HALF : 3 * HALF], (1, 0)
-                z_bf[1], z_order[1] = ring3[:, 2 * HALF : 4 * HALF], (1, 0)
+                z_bf[0], z_order[0] = arena[:, Z0 : Z0 + S].bitcast(BF16), (0, 1)
+                z_bf[1], z_order[1] = arena[:, Z1 : Z1 + S].bitcast(BF16), (1, 0)
             elif (q, b) == (2, 0):
-                z_bf[q], z_order[q] = arena[:, 0:S].bitcast(BF16), (1, 0)
+                z_bf[q], z_order[q] = arena[:, Z2 : Z2 + S].bitcast(BF16), (1, 0)
             elif (q, b) == (3, 0):
-                z_tile = keep.tile([P, 2 * HALF], BF16, name="z%d" % q, tag="slotB", align_bytes=64)
-                z_bf[q], z_order[q] = z_tile[:], (0, 1)
+                z_bf[q], z_order[q] = arena[:, Z2 - ZH : Z2 + ZH].bitcast(BF16), (1, 0)
             for u in range(2):
                 h_bank = psum.tile([P, PACK, P], F32, name="h_bank", tag="bank%d" % (2 * pair + u))
                 h_banks.append(h_bank)
@@ -227,16 +238,13 @@ def tile_list_oven_tray_refresh_kernel(tc, tab_words, tab_scales, offs, gT, w1, 
         def put_summed(q, tiles, slot):
             cols = slice(QUARTER * q, QUARTER * (q + 1))
             n = tiles.stop - tiles.start
-            if isinstance(slot, int):
-                new = arena[:, slot : slot + n * QUARTER].rearrange("p (e j) -> p e j", e=n)
-            else:
-                new = keep.tile([P, n, QUARTER], F32, name="new%d%d" % (q, tiles.start), tag=slot, align_bytes=64)[:]
-            nc.gpsimd.tensor_tensor(new, picked[:, tiles, cols], first[:, tiles] if q == 0 else moved[:, tiles, cols], ALU.add)
+            new = slot[:, 0 : n * QUARTER].rearrange("p (e j) -> p e j", e=n)
+            nc.gpsimd.tensor_tensor(new, picked(tiles.start, tiles.stop, cols), first[:, tiles] if q == 0 else moved[:, tiles, cols], ALU.add)
             for e in reversed(range(n)):
                 nc.vector.tensor_copy(state[tiles.start + e][:].indirect(listed(q, q + 1)), new[:, e])
 
         def put_fused(lo, hi, i, values):
-            nc.vector.tensor_tensor(state[i][:].indirect(listed(lo, hi)), picked[:, i, QUARTER * lo : QUARTER * hi], values, ALU.add)
+            nc.vector.tensor_tensor(state[i][:].indirect(listed(lo, hi)), picked(i, i + 1, slice(QUARTER * lo, QUARTER * hi))[:, 0], values, ALU.add)
 
         def store(i):
             nc.sync.dma_start(out[P * i : P * (i + 1), :], state[i][:])
@@ -251,29 +259,36 @@ def tile_list_oven_tray_refresh_kernel(tc, tab_words, tab_scales, offs, gT, w1, 
         gather_words(2, 1, QUARTERS)
         for a in range(K_PASSES):
             quantise_w1(a, 1)
-        for i in range(N_TILES - 1, 0, -1):
-            nc.vector.tensor_copy(picked[:, i], state[i][:].indirect(offsets[:]))
+        def pick(i, lo=0, hi=QUARTERS):
+            nc.vector.tensor_copy(picked(i, i + 1, slice(QUARTER * lo, QUARTER * hi))[:, 0], state[i][:].indirect(listed(lo, hi)))
+
+        pick(3)
+        pick(2)
+        pick(1, 3, 4)
 
         modes(0, 0, 0)
         modes(1, 0, 1)
         modes(0, 1, 2)
+        pick(1, 0, 3)
         modes(2, 0, 0)
         modes(1, 1, 3)
-        nc.vector.tensor_copy(picked[:, 0], state[0][:].indirect(offsets[:]))
-        first = keep.tile([P, N_TILES, QUARTER], F32, name="first", tag="square", align_bytes=64)
+        pick(0)
+        both = keep.tile([P, 3 * HALF], F32, name="both", tag="square2", align_bytes=64)
+        first = both[:, 2 * HALF :].rearrange("p (i j) -> p i j", i=N_TILES)
         for i in range(N_TILES):
             moved_at[0, i] = first[:, i]
         drive(0, 1)
-        put_summed(0, slice(2, 4), S)
-        put_summed(0, slice(1, 2), S + 2 * QUARTER)
-        modes(2, 1, 1)
-        put_summed(0, slice(0, 1), "slotB")
-        drive(1, 1)
-        put_summed(1, slice(2, 4), 0)
-        put_summed(1, slice(0, 2), 2 * QUARTER)
-        modes(3, 0, 2)
+        put_summed(0, slice(2, 4), arena[:, S:])
+        put_summed(0, slice(1, 2), arena[:, S + 2 * QUARTER :])
+        modes(2, 1, 2)
+        after21 = keep.tile([P, 3 * QUARTER], F32, name="after21", tag="raw01", align_bytes=64)
+        put_summed(0, slice(0, 1), after21[:])
+        drive(1, 0)
+        put_summed(1, slice(2, 4), after21[:, QUARTER:])
+        put_summed(1, slice(0, 2), arena[:, Z2 + 2 * QUARTER :])
+        modes(3, 0, 1)
         modes(3, 1, 3)
-        late = keep.tile([P, (N_TILES + 1) * QUARTER], F32, name="late", tag="raw01", align_bytes=64)
+        late = keep.tile([P, (N_TILES + 1) * QUARTER], F32, name="late", tag="raw21", align_bytes=64)
         for i in range(N_TILES):
             moved_at[2, i] = late[:, QUARTER * (3 - i) : QUARTER * (4 - i)]
         moved_at[3, 0] = late[:, QUARTER * 4 : QUARTER * 5]

@@ -50,15 +50,19 @@ def tile_list_oven_tray_refresh_kernel(tc, tab_words, tab_scales, offs, gT, w1, 
         tab_w = [keep.tile([P, T], U32, name="tab_w%d" % a, align_bytes=64) for a in range(K_PASSES)]
         state = [keep.tile([P, T], F32, name="state%d" % i, align_bytes=64) for i in range(N_TILES)]
         w4_w = keep.tile([P, R_PASSES, 2 * N], U8, name="w4_w", align_bytes=64)
+        picks = keep.tile([P, 3 * S + PACK * PASS], F32, name="picks", align_bytes=64)
         w1_raw = {}
 
         def load_table(a):
             nc.sync.dma_start(tab_w[a][:].bitcast(I32), tab_words[a].rearrange("p t i -> p (t i)").bitcast(I32))
 
         def load_w1(a, b):
-            w1_raw[a, b] = keep.tile([P, PACK, PASS], F32, name="w1_raw%d%d" % (a, b), tag="raw%d%d" % (a, b), align_bytes=64)
+            if (a, b) == (K_PASSES - 1, R_PASSES - 1):
+                w1_raw[a, b] = picks[:, 3 * S : 3 * S + PACK * PASS].rearrange("p (j c) -> p j c", j=PACK)
+            else:
+                w1_raw[a, b] = keep.tile([P, PACK, PASS], F32, name="w1_raw%d%d" % (a, b), tag="raw%d%d" % (a, b), align_bytes=64)[:]
             rows = w1[PASS * a : PASS * (a + 1), PASS * b : PASS * (b + 1)]
-            nc.sync.dma_start(w1_raw[a, b][:], rows.rearrange("(p j) c -> p j c", j=PACK))
+            nc.sync.dma_start(w1_raw[a, b], rows.rearrange("(p j) c -> p j c", j=PACK))
 
         def load_cub(b):
             nc.sync.dma_start(cub_sb[b][:], cub[PASS * b : PASS * (b + 1)].rearrange("(p t) -> p t", t=PACK))
@@ -66,8 +70,8 @@ def tile_list_oven_tray_refresh_kernel(tc, tab_words, tab_scales, offs, gT, w1, 
         def load_state(i):
             nc.sync.dma_start(state[i][:], gT[P * i : P * (i + 1), :])
 
-        nc.sync.dma_start(offsets[:], offs)
         load_table(0)
+        nc.sync.dma_start(offsets[:], offs)
         load_w1(0, 0)
         for Q in range(P // QUADRANT):
             nc.sync.dma_start(
@@ -77,11 +81,6 @@ def tile_list_oven_tray_refresh_kernel(tc, tab_words, tab_scales, offs, gT, w1, 
         load_table(1)
         load_w1(1, 0)
         load_w1(2, 0)
-        for Q in range(P // QUADRANT):
-            nc.sync.dma_start(
-                w4_s[QUADRANT * Q : QUADRANT * Q + 4, :, :].bitcast(I32),
-                w4_scales[:, 4 * Q : 4 * Q + 4, :].rearrange("b s n -> s b n").bitcast(I32),
-            )
         load_cub(0)
         load_table(2)
         for a in range(K_PASSES):
@@ -89,27 +88,31 @@ def tile_list_oven_tray_refresh_kernel(tc, tab_words, tab_scales, offs, gT, w1, 
         load_state(3)
         load_state(2)
         load_cub(1)
+        load_state(1)
+        for Q in range(P // QUADRANT):
+            nc.sync.dma_start(
+                w4_s[QUADRANT * Q : QUADRANT * Q + 4, :, :].bitcast(I32),
+                w4_scales[:, 4 * Q : 4 * Q + 4, :].rearrange("b s n -> s b n").bitcast(I32),
+            )
         nc.sync.dma_start(w4_w[:].bitcast(I32), w4_words.rearrange("b p c -> p b c").bitcast(I32))
+        load_state(0)
         with nc.allow_non_contiguous_dma(reason="one step value a partition"):
             nc.sync.dma_start(step_sb[:], step.rearrange("(i p) -> p i", p=P))
-        load_state(1)
-        load_state(0)
 
         v_w = [keep.tile([P, S], U32, name="v_w%d" % a, align_bytes=64) for a in range(K_PASSES)]
         v_s = keep.tile([P, S], U8, name="v_s", align_bytes=64)
         ZH = 2 * QUARTER
-        Z1, Z2, Z0 = S - QUARTER, S - QUARTER + 2 * ZH, S - QUARTER + 3 * ZH
-        P1 = Z0 + ZH
-        arena = keep.tile([P, P1 + 3 * S], F32, name="arena", align_bytes=64)
-        lower = arena[:, 0 : 2 * P1].rearrange("p (i s) -> p i s", i=2)[:, :, 0:S]
-        upper = arena[:, P1 + S :].rearrange("p (i s) -> p i s", i=2)
+        arena = keep.tile([P, 4 * ZH], F32, name="arena", align_bytes=64)
+        z_start = {0: 2, 1: 0, 2: 1, 3: 1}
+        z_order = {0: (0, 1), 1: (1, 0), 2: (1, 0), 3: (1, 0)}
 
         def picked(lo, hi, cols):
-            return lower[:, lo:hi, cols] if lo < 2 else upper[:, lo - 2 : hi - 2, cols]
+            return picks[:, 0 : N_TILES * S].rearrange("p (i s) -> p i s", i=N_TILES)[:, lo:hi, cols]
 
-        w1_w, w1_s, z_bf, z_w, z_s = {}, {}, {}, {}, {}
+        w1_w, w1_s, z_w, z_s = {}, {}, {}, {}
+        z_bf = {q: arena[:, ZH * z_start[q] : ZH * (z_start[q] + 2)].bitcast(BF16) for q in range(QUARTERS)}
 
-        work_slot = {(0, 0): "raw00", (1, 0): "raw10", (2, 0): "raw20", (2, 1): "raw01", (3, 0): "raw11", (3, 1): "raw21"}
+        work_slot = {(0, 0): "raw00", (1, 0): "raw10", (2, 0): "raw20", (3, 0): "raw11", (3, 1): "work31"}
         HALF = PACK * QUARTER
 
         def listed(lo, hi):
@@ -120,11 +123,11 @@ def tile_list_oven_tray_refresh_kernel(tc, tab_words, tab_scales, offs, gT, w1, 
 
         def quantise_w1(a, b):
             if (a, b) == (K_PASSES - 1, R_PASSES - 1):
-                w1_bf = arena[:, Z2 - QUARTER : Z2 - QUARTER + S].bitcast(BF16)
+                w1_bf = arena[:, ZH : 3 * ZH].bitcast(BF16)
             else:
                 w1_bf = ring.tile([P, PACK * PASS], BF16, name="w1_bf", tag="w1_bf", align_bytes=64)[:]
             dst = w1_bf.rearrange("p (t m j) -> p m j t", t=PACK, j=PACK)
-            src = w1_raw[a, b][:].rearrange("p j (m t) -> p m j t", t=PACK)
+            src = w1_raw[a, b].rearrange("p j (m t) -> p m j t", t=PACK)
             if (a, b) == (K_PASSES - 1, 0):
                 nc.scalar.activation(dst[:, 0 : P // 2], src[:, 0 : P // 2], ACT.Copy)
                 nc.vector.tensor_copy(dst[:, P // 2 : P], src[:, P // 2 : P])
@@ -139,40 +142,15 @@ def tile_list_oven_tray_refresh_kernel(tc, tab_words, tab_scales, offs, gT, w1, 
         def by_line(ap):
             return ap.rearrange("p (c t i) -> p c t i", t=PACK, i=LINE)
 
-        z_order = {}
+        h_banks, h_sb, square, planes = {}, {}, {}, {}
 
-        def modes(q, b, pair):
-            on_vector = (q, b) in VECTOR_PRODUCTS
-            if on_vector:
-                if q == 0:
-                    square = keep.tile([P, PACK, QUARTER], F32, name="square", tag="square", align_bytes=64)[:]
-                else:
-                    square = keep.tile([P, PACK, QUARTER], F32, name="square11", tag="square2", align_bytes=64)[:]
-                planes = keep.tile([P, PACK, QUARTER], F32, name="factor%d" % q, tag="factor%d" % q, align_bytes=64)
-            else:
-                work = keep.tile([P, 2 * HALF], F32, name="work%d%d" % (q, b), tag=work_slot[q, b], align_bytes=64)
-                h_sb, factor = work[:, 0:HALF], work[:, HALF : 2 * HALF]
-                planes = by_line(factor).rearrange("p c t i -> p t c i")
-                square = planes
-                squares = factor
-                if (q, b) == (2, 0):
-                    factor = keep.tile([P, HALF], F32, name="factor20", tag="square", align_bytes=64)[:]
-                    squares = keep.tile([P, HALF], F32, name="square20", tag="square2", align_bytes=64)[:]
-                    planes = by_line(factor).rearrange("p c t i -> p t c i")
-                if (q, b) == (2, 1):
-                    h_sb, squares = both[:, 0:HALF], both[:, HALF : 2 * HALF]
-                square = by_line(squares).rearrange("p c t i -> p t c i")
-            h_banks = []
-            if (q, b) == (0, 0):
-                z_bf[0], z_order[0] = arena[:, Z0 : Z0 + S].bitcast(BF16), (0, 1)
-                z_bf[1], z_order[1] = arena[:, Z1 : Z1 + S].bitcast(BF16), (1, 0)
-            elif (q, b) == (2, 0):
-                z_bf[q], z_order[q] = arena[:, Z2 : Z2 + S].bitcast(BF16), (1, 0)
-            elif (q, b) == (3, 0):
-                z_bf[q], z_order[q] = arena[:, Z2 - ZH : Z2 + ZH].bitcast(BF16), (1, 0)
-            for u in range(2):
-                h_bank = psum.tile([P, PACK, P], F32, name="h_bank", tag="bank%d" % (2 * pair + u))
-                h_banks.append(h_bank)
+        chain = keep.tile([P, 3 * HALF], F32, name="chain", tag="raw01", align_bytes=64)
+        square_start = {0: HALF + P, 1: 3 * P}
+
+        def multiply(q, b, banks, halves=(0, 1)):
+            for u in halves:
+                h_bank = psum.tile([P, PACK, P], F32, name="h_bank", tag="bank%d" % banks[u])
+                h_banks[q, b, u] = h_bank
                 entries = slice(QUARTER * q + P * u, QUARTER * q + P * (u + 1))
                 for a in range(K_PASSES):
                     for t in range(PACK):
@@ -185,38 +163,79 @@ def tile_list_oven_tray_refresh_kernel(tc, tab_words, tab_scales, offs, gT, w1, 
                             start=(a == 0 and t == 0),
                             stop=(a == K_PASSES - 1 and t == PACK - 1),
                         )
-                if on_vector:
-                    nc.scalar.activation(square[:, :, P * u : P * (u + 1)], h_bank[:], ACT.Square)
-                    continue
-                h_lines = h_bank[:].rearrange("p t (c i) -> p c t i", i=LINE)
-                part = slice(PACK * P * u, PACK * P * (u + 1))
-                nc.scalar.activation(by_line(squares[:, part]), h_lines, ACT.Square)
-                nc.scalar.copy(by_line(h_sb[:, part]), h_lines)
-            for t in range(PACK):
-                nc.scalar.activation(planes[:, t], square[:, t], ACT.Copy, bias=1.0, scale=cub_sb[b][:, t : t + 1])
+            if (q, b) in square:
+                return
+            if (q, b) in VECTOR_PRODUCTS:
+                square[q, b] = chain[:, square_start[q] : square_start[q] + HALF]
+                planes[q, b] = picks[:, S * (1 - q) : S * (2 - q)]
+            else:
+                if (q, b) == (2, 1):
+                    work = chain
+                else:
+                    work = keep.tile([P, 2 * HALF], F32, name="work%d%d" % (q, b), tag=work_slot[q, b], align_bytes=64)
+                h_sb[q, b] = work[:, 0:HALF]
+                square[q, b] = planes[q, b] = work[:, HALF : 2 * HALF]
+                if (q, b) == (2, 0):
+                    planes[q, b] = chain[:, 2 * HALF : 3 * HALF]
+
+        def h_lines(q, b, u):
+            return h_banks[q, b, u][:].rearrange("p t (c i) -> p c t i", i=LINE)
+
+        def squares(q, b, banks=(0, 1)):
+            for u in banks:
+                if (q, b) in VECTOR_PRODUCTS:
+                    nc.scalar.activation(square[q, b].rearrange("p (t u j) -> p u t j", t=PACK, u=2)[:, u], h_banks[q, b, u][:], ACT.Square)
+                else:
+                    nc.scalar.activation(by_line(square[q, b][:, PACK * P * u : PACK * P * (u + 1)]), h_lines(q, b, u), ACT.Square)
+
+        def copy_h(q, b, banks=(0, 1)):
+            for u in banks:
+                nc.scalar.copy(by_line(h_sb[q, b][:, PACK * P * u : PACK * P * (u + 1)]), h_lines(q, b, u))
+
+        def factor(q, b, planes_now=(0, 3, 1, 2)):
+            if (q, b) in VECTOR_PRODUCTS:
+                src = square[q, b].rearrange("p (t u j) -> p t u j", u=2, t=PACK)
+                dst = planes[q, b].rearrange("p (u t j) -> p t u j", u=2, t=PACK)
+            else:
+                src, dst = [by_line(x).rearrange("p c t i -> p t c i") for x in (square[q, b], planes[q, b])]
+            for t in planes_now:
+                nc.scalar.activation(dst[:, t], src[:, t], ACT.Copy, bias=1.0, scale=cub_sb[b][:, t : t + 1])
+
+        def product(q, b):
             place = z_order[q][b]
             z_half = z_bf[q][:, HALF * place : HALF * (place + 1)]
-            if on_vector:
+            if (q, b) in VECTOR_PRODUCTS:
                 for u in range(2):
+                    part = slice(PACK * P * u, PACK * P * (u + 1))
                     nc.vector.tensor_tensor(
-                        z_half[:, PACK * P * u : PACK * P * (u + 1)].rearrange("p (c i t) -> p c t i", i=RUN, t=PACK),
-                        h_banks[u][:].rearrange("p t (c i) -> p c t i", i=RUN),
-                        planes[:, :, P * u : P * (u + 1)].rearrange("p t (c i) -> p c t i", i=RUN),
+                        z_half[:, part].rearrange("p (c i t) -> p c t i", i=RUN, t=PACK),
+                        h_banks[q, b, u][:].rearrange("p t (c i) -> p c t i", i=RUN),
+                        planes[q, b][:, part].rearrange("p (t c i) -> p c t i", t=PACK, i=RUN),
                         ALU.mult,
                     )
             else:
-                nc.gpsimd.tensor_tensor(z_half.rearrange("p (c i t) -> p c t i", i=LINE, t=PACK), by_line(h_sb), by_line(factor), ALU.mult)
-            if b == R_PASSES - 1:
-                z_w[q] = keep.tile([P, R_PASSES * QUARTER], U32, name="z_w%d" % q, align_bytes=64)
-                z_s[q] = keep.tile([P, R_PASSES * QUARTER], U8, name="z_s%d" % q, align_bytes=64)
-                nc.vector.quantize_mx(out=z_w[q][:].bitcast(FP8X4), scales=z_s[q][:], in_=z_bf[q])
+                nc.gpsimd.tensor_tensor(
+                    z_half.rearrange("p (c i t) -> p c t i", i=LINE, t=PACK), by_line(h_sb[q, b]), by_line(planes[q, b]), ALU.mult
+                )
 
-        moved = keep.tile([P, N_TILES, S], F32, name="moved", align_bytes=64)
-        moved_at = {(q, i): moved[:, i, QUARTER * q : QUARTER * (q + 1)] for q in range(QUARTERS) for i in range(N_TILES)}
+        def modes(q, b, banks):
+            multiply(q, b, banks)
+            squares(q, b)
+            if (q, b) not in VECTOR_PRODUCTS:
+                copy_h(q, b)
+            factor(q, b)
+            product(q, b)
 
-        def drive(q, pair):
+        def quantise_z(q, slot):
+            z_w[q] = keep.tile([P, R_PASSES * QUARTER], U32, name="z_w%d" % q, tag=slot, align_bytes=64)
+            z_s[q] = keep.tile([P, R_PASSES * QUARTER], U8, name="z_s%d" % q, align_bytes=64)
+            nc.vector.quantize_mx(out=z_w[q][:].bitcast(FP8X4), scales=z_s[q][:], in_=z_bf[q])
+
+        moved_at = {}
+
+        def drive(q, banks, after_first=None):
             for u in (1, 0):
-                y_bank = psum.tile([P, 2, QUARTER], F32, name="y_bank", tag="bank%d" % (2 * pair + u))
+                y_bank = psum.tile([P, 2, QUARTER], F32, name="y_bank", tag="bank%d" % banks[u])
                 for e in range(2):
                     i = 2 * u + e
                     for c in range(0, QUARTER, P):
@@ -234,14 +253,26 @@ def tile_list_oven_tray_refresh_kernel(tc, tab_words, tab_scales, offs, gT, w1, 
                 for e in (1, 0):
                     i = 2 * u + e
                     nc.scalar.activation(moved_at[q, i], y_bank[:, e, :], ACT.Copy, scale=step_sb[:, i : i + 1])
+                    if after_first and i == N_TILES - 1:
+                        after_first()
 
-        def put_summed(q, tiles, slot):
-            cols = slice(QUARTER * q, QUARTER * (q + 1))
-            n = tiles.stop - tiles.start
-            new = slot[:, 0 : n * QUARTER].rearrange("p (e j) -> p e j", e=n)
-            nc.gpsimd.tensor_tensor(new, picked(tiles.start, tiles.stop, cols), first[:, tiles] if q == 0 else moved[:, tiles, cols], ALU.add)
-            for e in reversed(range(n)):
-                nc.vector.tensor_copy(state[tiles.start + e][:].indirect(listed(q, q + 1)), new[:, e])
+        def moved_tile(q, lo, hi, slot):
+            tile = keep.tile([P, hi - lo, QUARTER], F32, name="moved%d%d" % (q, lo), tag=slot, align_bytes=64)
+            for i in range(lo, hi):
+                moved_at[q, i] = tile[:, i - lo]
+            return tile
+
+        new_at = {}
+
+        def add_up(q, lo, hi, moved, new=None):
+            old = picked(lo, hi, slice(QUARTER * q, QUARTER * (q + 1)))
+            new = old if new is None else new.rearrange("p (i j) -> p i j", j=QUARTER)
+            for i in range(lo, hi):
+                new_at[q, i] = new[:, i - lo]
+            nc.gpsimd.tensor_tensor(new, old, moved[:], ALU.add)
+
+        def put(q, i):
+            nc.vector.tensor_copy(state[i][:].indirect(listed(q, q + 1)), new_at[q, i])
 
         def put_fused(lo, hi, i, values):
             nc.vector.tensor_tensor(state[i][:].indirect(listed(lo, hi)), picked(i, i + 1, slice(QUARTER * lo, QUARTER * hi))[:, 0], values, ALU.add)
@@ -264,40 +295,82 @@ def tile_list_oven_tray_refresh_kernel(tc, tab_words, tab_scales, offs, gT, w1, 
 
         pick(3)
         pick(2)
-        pick(1, 3, 4)
 
-        modes(0, 0, 0)
-        modes(1, 0, 1)
-        modes(0, 1, 2)
-        pick(1, 0, 3)
-        modes(2, 0, 0)
-        modes(1, 1, 3)
-        pick(0)
-        both = keep.tile([P, 3 * HALF], F32, name="both", tag="square2", align_bytes=64)
-        first = both[:, 2 * HALF :].rearrange("p (i j) -> p i j", i=N_TILES)
-        for i in range(N_TILES):
-            moved_at[0, i] = first[:, i]
-        drive(0, 1)
-        put_summed(0, slice(2, 4), arena[:, S:])
-        put_summed(0, slice(1, 2), arena[:, S + 2 * QUARTER :])
-        modes(2, 1, 2)
-        after21 = keep.tile([P, 3 * QUARTER], F32, name="after21", tag="raw01", align_bytes=64)
-        put_summed(0, slice(0, 1), after21[:])
-        drive(1, 0)
-        put_summed(1, slice(2, 4), after21[:, QUARTER:])
-        put_summed(1, slice(0, 2), arena[:, Z2 + 2 * QUARTER :])
-        modes(3, 0, 1)
-        modes(3, 1, 3)
-        late = keep.tile([P, (N_TILES + 1) * QUARTER], F32, name="late", tag="raw21", align_bytes=64)
-        for i in range(N_TILES):
-            moved_at[2, i] = late[:, QUARTER * (3 - i) : QUARTER * (4 - i)]
-        moved_at[3, 0] = late[:, QUARTER * 4 : QUARTER * 5]
-        drive(2, 3)
-        for i in range(N_TILES - 1, 0, -1):
+        modes(0, 0, (0, 1))
+        modes(1, 0, (2, 3))
+        multiply(2, 0, (0, 1))
+        squares(2, 0)
+        copy_h(2, 0, (0,))
+        multiply(0, 1, (4, 5))
+        squares(0, 1)
+        copy_h(2, 0, (1,))
+        factor(0, 1)
+        product(0, 1)
+        pick(1, 0, 1)
+        quantise_z(0, "z0")
+        pick(1, 1, 4)
+        factor(2, 0, (0, 3, 1))
+        multiply(1, 1, (6, 7))
+        squares(1, 1)
+        factor(2, 0, (2,))
+        product(2, 0)
+        factor(1, 1)
+        product(1, 1)
+        pick(0, 0, 1)
+        pick(0, 1, 4)
+        upper = moved_tile(0, 1, 4, "upper")
+        lowest = moved_tile(0, 0, 1, "lowest")
+        multiply(2, 1, (4, 1), (0,))
+        drive(0, (0, 1))
+        multiply(2, 1, (4, 1), (1,))
+        add_up(0, 1, 4, upper)
+        quantise_z(1, "upper")
+        for i in (3, 2, 1):
+            put(0, i)
+        for u in range(2):
+            squares(2, 1, (u,))
+            copy_h(2, 1, (u,))
+        factor(2, 1)
+        product(2, 1)
+        add_up(0, 0, 1, lowest, arena[:, 0:QUARTER])
+        put(0, 0)
+        multiply(3, 0, (0, 5), (0,))
+        squares(3, 0, (0,))
+        copy_h(3, 0, (0,))
+        second = moved_tile(1, 0, 4, "second")
+        drive(1, (3, 5))
+        add_up(1, 0, 4, second)
+        quantise_z(2, "second")
+        for i in (3, 2, 1, 0):
+            put(1, i)
+        multiply(3, 0, (0, 5), (1,))
+        squares(3, 0, (1,))
+        copy_h(3, 0, (1,))
+        factor(3, 0)
+        product(3, 0)
+        multiply(3, 1, (3, 5))
+        squares(3, 1)
+        copy_h(3, 1)
+        factor(3, 1)
+
+        def last_product():
+            add_up(2, 3, 4, moved_at[2, 3].rearrange("p (i j) -> p i j", i=1))
+            put(2, 3)
+            product(3, 1)
+            quantise_z(3, "z0")
+
+        late = keep.tile([P, N_TILES * QUARTER], F32, name="late", tag="work31", align_bytes=64)
+        for i in range(N_TILES - 1):
+            moved_at[2, i] = late[:, QUARTER * (2 - i) : QUARTER * (3 - i)]
+        moved_at[2, 3] = arena[:, ZH : ZH + QUARTER]
+        moved_tile(3, 1, 4, "last")
+        moved_at[3, 0] = late[:, QUARTER * 3 : QUARTER * 4]
+        drive(2, (5, 3), after_first=last_product)
+        for i in range(N_TILES - 2, 0, -1):
             put_fused(2, 3, i, moved_at[2, i])
-        drive(3, 0)
+        drive(3, (2, 1))
         for i in range(N_TILES - 1, 0, -1):
             put_fused(3, 4, i, moved_at[3, i])
             store(i)
-        put_fused(2, 4, 0, late[:, QUARTER * 3 : QUARTER * 5])
+        put_fused(2, 4, 0, late[:, QUARTER * 2 : QUARTER * 4])
         store(0)

@@ -42,9 +42,9 @@ def tile_list_oven_tray_refresh_kernel(tc, tab_words, tab_scales, offs, gT, w1, 
 
         offsets = keep.tile([P, S // 16], U16, name="offsets")
         tab_s = keep.tile([P, T], U8, name="tab_s", align_bytes=64)
-        nc.gpsimd.memset(tab_s[:].bitcast(I32), 0)
+        nc.vector.memset(tab_s[:].bitcast(I32), 0)
         w4_s = keep.tile([P, R_PASSES, N], U8, name="w4_s", align_bytes=64)
-        nc.vector.memset(w4_s[:].rearrange("p b n -> p (b n)").bitcast(I32), 0)
+        nc.gpsimd.memset(w4_s[:].rearrange("p b n -> p (b n)").bitcast(I32), 0)
         cub_sb = [keep.tile([P, PACK], F32, name="cub_sb%d" % b) for b in range(R_PASSES)]
         step_sb = keep.tile([P, N_TILES], F32, name="step_sb")
         tab_w = [keep.tile([P, T], U32, name="tab_w%d" % a, align_bytes=64) for a in range(K_PASSES)]
@@ -72,13 +72,13 @@ def tile_list_oven_tray_refresh_kernel(tc, tab_words, tab_scales, offs, gT, w1, 
 
         load_table(0)
         nc.sync.dma_start(offsets[:], offs)
+        load_table(1)
         load_w1(0, 0)
         for Q in range(P // QUADRANT):
             nc.sync.dma_start(
                 tab_s[QUADRANT * Q : QUADRANT * Q + 4 * K_PASSES, :].bitcast(I32),
                 tab_scales[:, 4 * Q : 4 * Q + 4, :].bitcast(I32),
             )
-        load_table(1)
         load_w1(1, 0)
         load_w1(2, 0)
         load_cub(0)
@@ -112,7 +112,7 @@ def tile_list_oven_tray_refresh_kernel(tc, tab_words, tab_scales, offs, gT, w1, 
         w1_w, w1_s, z_w, z_s = {}, {}, {}, {}
         z_bf = {q: arena[:, ZH * z_start[q] : ZH * (z_start[q] + 2)].bitcast(BF16) for q in range(QUARTERS)}
 
-        work_slot = {(0, 0): "raw00", (1, 0): "raw10", (2, 0): "raw20", (3, 0): "raw11", (3, 1): "work31"}
+        work_slot = {(2, 0): "raw20", (3, 0): "raw11", (3, 1): "work31"}
         HALF = PACK * QUARTER
 
         def listed(lo, hi):
@@ -122,22 +122,27 @@ def tile_list_oven_tray_refresh_kernel(tc, tab_words, tab_scales, offs, gT, w1, 
             nc.vector.tensor_copy(v_w[a][:, QUARTER * lo : QUARTER * hi], tab_w[a][:].indirect(listed(lo, hi)))
 
         def quantise_w1(a, b):
-            if (a, b) == (K_PASSES - 1, R_PASSES - 1):
-                w1_bf = arena[:, ZH : 3 * ZH].bitcast(BF16)
-            else:
-                w1_bf = ring.tile([P, PACK * PASS], BF16, name="w1_bf", tag="w1_bf", align_bytes=64)[:]
-            dst = w1_bf.rearrange("p (t m j) -> p m j t", t=PACK, j=PACK)
-            src = w1_raw[a, b].rearrange("p j (m t) -> p m j t", t=PACK)
-            if (a, b) == (K_PASSES - 1, 0):
-                nc.scalar.activation(dst[:, 0 : P // 2], src[:, 0 : P // 2], ACT.Copy)
-                nc.vector.tensor_copy(dst[:, P // 2 : P], src[:, P // 2 : P])
-            elif b == 0:
-                nc.scalar.activation(dst, src, ACT.Copy)
-            else:
-                nc.vector.tensor_copy(dst, src)
+            w1_bf = ring.tile([P, PACK * PASS], BF16, name="w1_bf", tag="w1_bf", align_bytes=64)[:]
             w1_w[a, b] = keep.tile([P, PASS], U32, name="w1_w%d%d" % (a, b), align_bytes=64)
             w1_s[a, b] = keep.tile([P, PASS], U8, name="w1_s%d%d" % (a, b), align_bytes=64)
-            nc.vector.quantize_mx(out=w1_w[a, b][:].bitcast(FP8X4), scales=w1_s[a, b][:], in_=w1_bf)
+            src = w1_raw[a, b].rearrange("p j (m t) -> p m j t", t=PACK)
+            if b == 0:
+                dst = w1_bf.rearrange("p (t m j) -> p m j t", t=PACK, j=PACK)
+                if a == K_PASSES - 1:
+                    nc.scalar.activation(dst[:, 0 : P // 2], src[:, 0 : P // 2], ACT.Copy)
+                    nc.vector.tensor_copy(dst[:, P // 2 : P], src[:, P // 2 : P])
+                else:
+                    nc.scalar.activation(dst, src, ACT.Copy)
+                nc.vector.quantize_mx(out=w1_w[a, b][:].bitcast(FP8X4), scales=w1_s[a, b][:], in_=w1_bf)
+                return
+            pairs = [w1_bf[:, 0 : 2 * PASS], w1_bf[:, 2 * PASS :]]
+            if a == K_PASSES - 1:
+                pairs[1] = arena[:, ZH + QUARTER : 2 * ZH + QUARTER].bitcast(BF16)
+            for e in range(2):
+                nc.vector.tensor_copy(pairs[e].rearrange("p (t m j) -> p m j t", t=2, j=PACK), src[:, :, :, 2 * e : 2 * e + 2])
+            for e in range(2):
+                cols = slice(2 * P * e, 2 * P * (e + 1))
+                nc.vector.quantize_mx(out=w1_w[a, b][:, cols].bitcast(FP8X4), scales=w1_s[a, b][:, cols], in_=pairs[e])
 
         def by_line(ap):
             return ap.rearrange("p (c t i) -> p c t i", t=PACK, i=LINE)
@@ -145,6 +150,8 @@ def tile_list_oven_tray_refresh_kernel(tc, tab_words, tab_scales, offs, gT, w1, 
         h_banks, h_sb, square, planes = {}, {}, {}, {}
 
         chain = keep.tile([P, 3 * HALF], F32, name="chain", tag="raw01", align_bytes=64)
+        first_h = keep.tile([P, 2 * HALF], F32, name="first_h", tag="raw00", align_bytes=64)
+        first_factor = keep.tile([P, 2 * HALF], F32, name="first_factor", tag="raw10", align_bytes=64)
         square_start = {0: HALF + P, 1: 3 * P}
 
         def multiply(q, b, banks, halves=(0, 1)):
@@ -169,6 +176,11 @@ def tile_list_oven_tray_refresh_kernel(tc, tab_words, tab_scales, offs, gT, w1, 
                 square[q, b] = chain[:, square_start[q] : square_start[q] + HALF]
                 planes[q, b] = picks[:, S * (1 - q) : S * (2 - q)]
             else:
+                if b == 0 and q < 2:
+                    part = slice(HALF * (1 - q), HALF * (2 - q))
+                    h_sb[q, b] = first_h[:, part]
+                    square[q, b] = planes[q, b] = first_factor[:, part]
+                    return
                 if (q, b) == (2, 1):
                     work = chain
                 else:
@@ -218,14 +230,6 @@ def tile_list_oven_tray_refresh_kernel(tc, tab_words, tab_scales, offs, gT, w1, 
                     z_half.rearrange("p (c i t) -> p c t i", i=LINE, t=PACK), by_line(h_sb[q, b]), by_line(planes[q, b]), ALU.mult
                 )
 
-        def modes(q, b, banks):
-            multiply(q, b, banks)
-            squares(q, b)
-            if (q, b) not in VECTOR_PRODUCTS:
-                copy_h(q, b)
-            factor(q, b)
-            product(q, b)
-
         def quantise_z(q, slot):
             z_w[q] = keep.tile([P, R_PASSES * QUARTER], U32, name="z_w%d" % q, tag=slot, align_bytes=64)
             z_s[q] = keep.tile([P, R_PASSES * QUARTER], U8, name="z_s%d" % q, align_bytes=64)
@@ -233,28 +237,27 @@ def tile_list_oven_tray_refresh_kernel(tc, tab_words, tab_scales, offs, gT, w1, 
 
         moved_at = {}
 
-        def drive(q, banks, after_first=None):
-            for u in (1, 0):
-                y_bank = psum.tile([P, 2, QUARTER], F32, name="y_bank", tag="bank%d" % banks[u])
-                for e in range(2):
-                    i = 2 * u + e
-                    for c in range(0, QUARTER, P):
-                        for b in range(R_PASSES):
-                            z_cols = slice(QUARTER * z_order[q][b] + c, QUARTER * z_order[q][b] + c + P)
-                            nc.tensor.matmul_mx(
-                                out=y_bank[:, e, c : c + P],
-                                lhsT=w4_w[:, b, 2 * P * i : 2 * P * (i + 1)].bitcast(FP4X4),
-                                lhsT_scale=w4_s[:, b, P * i : P * (i + 1)],
-                                rhs=z_w[q][:, z_cols].bitcast(FP8X4),
-                                rhs_scale=z_s[q][:, z_cols],
-                                start=(b == 0),
-                                stop=(b == R_PASSES - 1),
-                            )
-                for e in (1, 0):
-                    i = 2 * u + e
-                    nc.scalar.activation(moved_at[q, i], y_bank[:, e, :], ACT.Copy, scale=step_sb[:, i : i + 1])
-                    if after_first and i == N_TILES - 1:
-                        after_first()
+        def drive_tiles(q, tiles, bank):
+            y_bank = psum.tile([P, len(tiles), QUARTER], F32, name="y_bank", tag="bank%d" % bank)
+            for e, i in enumerate(tiles):
+                for c in range(0, QUARTER, P):
+                    for b in range(R_PASSES):
+                        z_cols = slice(QUARTER * z_order[q][b] + c, QUARTER * z_order[q][b] + c + P)
+                        nc.tensor.matmul_mx(
+                            out=y_bank[:, e, c : c + P],
+                            lhsT=w4_w[:, b, 2 * P * i : 2 * P * (i + 1)].bitcast(FP4X4),
+                            lhsT_scale=w4_s[:, b, P * i : P * (i + 1)],
+                            rhs=z_w[q][:, z_cols].bitcast(FP8X4),
+                            rhs_scale=z_s[q][:, z_cols],
+                            start=(b == 0),
+                            stop=(b == R_PASSES - 1),
+                        )
+            for e, i in enumerate(tiles):
+                nc.scalar.activation(moved_at[q, i], y_bank[:, e, :], ACT.Copy, scale=step_sb[:, i : i + 1])
+
+        def drive(q, banks):
+            drive_tiles(q, (3, 2), banks[1])
+            drive_tiles(q, (1, 0), banks[0])
 
         def moved_tile(q, lo, hi, slot):
             tile = keep.tile([P, hi - lo, QUARTER], F32, name="moved%d%d" % (q, lo), tag=slot, align_bytes=64)
@@ -281,9 +284,9 @@ def tile_list_oven_tray_refresh_kernel(tc, tab_words, tab_scales, offs, gT, w1, 
             nc.sync.dma_start(out[P * i : P * (i + 1), :], state[i][:])
 
         gather_words(0, 0, QUARTERS)
+        gather_words(1, 0, QUARTERS)
         nc.vector.tensor_copy(v_s[:], tab_s[:].indirect(offsets[:]))
         quantise_w1(0, 0)
-        gather_words(1, 0, QUARTERS)
         quantise_w1(1, 0)
         quantise_w1(2, 0)
         gather_words(2, 0, 1)
@@ -296,8 +299,15 @@ def tile_list_oven_tray_refresh_kernel(tc, tab_words, tab_scales, offs, gT, w1, 
         pick(3)
         pick(2)
 
-        modes(0, 0, (0, 1))
-        modes(1, 0, (2, 3))
+        for q in range(2):
+            multiply(q, 0, (2 * q, 2 * q + 1))
+            squares(q, 0)
+            copy_h(q, 0)
+        in_planes = by_line(first_factor[:]).rearrange("p c t i -> p t c i")
+        for t in range(PACK):
+            nc.scalar.activation(in_planes[:, t], in_planes[:, t], ACT.Copy, bias=1.0, scale=cub_sb[0][:, t : t + 1])
+        for q in range(2):
+            product(q, 0)
         multiply(2, 0, (0, 1))
         squares(2, 0)
         copy_h(2, 0, (0,))
@@ -351,26 +361,28 @@ def tile_list_oven_tray_refresh_kernel(tc, tab_words, tab_scales, offs, gT, w1, 
         multiply(3, 1, (3, 5))
         squares(3, 1)
         copy_h(3, 1)
-        factor(3, 1)
-
-        def last_product():
-            add_up(2, 3, 4, moved_at[2, 3].rearrange("p (i j) -> p i j", i=1))
-            put(2, 3)
-            product(3, 1)
-            quantise_z(3, "z0")
-
-        late = keep.tile([P, N_TILES * QUARTER], F32, name="late", tag="work31", align_bytes=64)
-        for i in range(N_TILES - 1):
-            moved_at[2, i] = late[:, QUARTER * (2 - i) : QUARTER * (3 - i)]
         moved_at[2, 3] = arena[:, ZH : ZH + QUARTER]
-        moved_tile(3, 1, 4, "last")
-        moved_at[3, 0] = late[:, QUARTER * 3 : QUARTER * 4]
-        drive(2, (5, 3), after_first=last_product)
-        for i in range(N_TILES - 2, 0, -1):
-            put_fused(2, 3, i, moved_at[2, i])
-        drive(3, (2, 1))
-        for i in range(N_TILES - 1, 0, -1):
+        drive_tiles(2, (3,), 3)
+        factor(3, 1)
+        add_up(2, 3, 4, moved_at[2, 3].rearrange("p (i j) -> p i j", i=1))
+        put(2, 3)
+        product(3, 1)
+        quantise_z(3, "z0")
+        late = keep.tile([P, 5 * QUARTER], F32, name="late", tag="work31", align_bytes=64)
+        moved_at[2, 2] = late[:, 0:QUARTER]
+        for i in (1, 0):
+            for q in (2, 3):
+                moved_at[q, i] = late[:, QUARTER * (1 + 2 * i + q - 2) : QUARTER * (2 + 2 * i + q - 2)]
+        moved_tile(3, 2, 4, "last")
+        drive_tiles(2, (2,), 5)
+        put_fused(2, 3, 2, moved_at[2, 2])
+        drive_tiles(2, (1, 0), 3)
+        drive_tiles(3, (3,), 6)
+        drive_tiles(3, (2,), 2)
+        drive_tiles(3, (1, 0), 4)
+        for i in (3, 2):
             put_fused(3, 4, i, moved_at[3, i])
             store(i)
-        put_fused(2, 4, 0, late[:, QUARTER * 2 : QUARTER * 4])
-        store(0)
+        for i in (1, 0):
+            put_fused(2, 4, i, late[:, QUARTER * (1 + 2 * i) : QUARTER * (3 + 2 * i)])
+            store(i)

@@ -42,9 +42,9 @@ def tile_list_oven_tray_refresh_kernel(tc, tab_words, tab_scales, offs, gT, w1, 
 
         offsets = keep.tile([P, S // 16], U16, name="offsets")
         tab_s = keep.tile([P, T], U8, name="tab_s", align_bytes=64)
-        nc.vector.memset(tab_s[:].bitcast(I32), 0)
+        nc.gpsimd.memset(tab_s[:].bitcast(I32), 0)
         w4_s = keep.tile([P, R_PASSES, N], U8, name="w4_s", align_bytes=64)
-        nc.gpsimd.memset(w4_s[:].rearrange("p b n -> p (b n)").bitcast(I32), 0)
+        nc.vector.memset(w4_s[:].rearrange("p b n -> p (b n)").bitcast(I32), 0)
         cub_sb = [keep.tile([P, PACK], F32, name="cub_sb%d" % b) for b in range(R_PASSES)]
         step_sb = keep.tile([P, N_TILES], F32, name="step_sb")
         tab_w = [keep.tile([P, T], U32, name="tab_w%d" % a, align_bytes=64) for a in range(K_PASSES)]
@@ -72,13 +72,13 @@ def tile_list_oven_tray_refresh_kernel(tc, tab_words, tab_scales, offs, gT, w1, 
 
         load_table(0)
         nc.sync.dma_start(offsets[:], offs)
-        load_table(1)
         load_w1(0, 0)
         for Q in range(P // QUADRANT):
             nc.sync.dma_start(
                 tab_s[QUADRANT * Q : QUADRANT * Q + 4 * K_PASSES, :].bitcast(I32),
                 tab_scales[:, 4 * Q : 4 * Q + 4, :].bitcast(I32),
             )
+        load_table(1)
         load_w1(1, 0)
         load_w1(2, 0)
         load_cub(0)
@@ -284,9 +284,9 @@ def tile_list_oven_tray_refresh_kernel(tc, tab_words, tab_scales, offs, gT, w1, 
             nc.sync.dma_start(out[P * i : P * (i + 1), :], state[i][:])
 
         gather_words(0, 0, QUARTERS)
-        gather_words(1, 0, QUARTERS)
         nc.vector.tensor_copy(v_s[:], tab_s[:].indirect(offsets[:]))
         quantise_w1(0, 0)
+        gather_words(1, 0, QUARTERS)
         quantise_w1(1, 0)
         quantise_w1(2, 0)
         gather_words(2, 0, 1)

@@ -26,11 +26,15 @@ QUADRANT = 32
 QUARTERS = 4
 QUARTER = S // QUARTERS
 LIST_COLS = QUARTER // 16
+UNIT = PACK * QUARTER
+BANK = PACK * P
+PLACE = UNIT // 2
 RUN = 2
 LINE = 4
 RING = 3
-FACTOR_RING = 4
+SCALAR_COLS = 48
 VECTOR_PRODUCTS = ((0, 1), (1, 1))
+PLANE_ORDER = (0, 3, 1, 2)
 
 
 def tile_list_oven_tray_refresh_kernel(tc, tab_words, tab_scales, offs, gT, w1, cub, w4_words, w4_scales, step, out):
@@ -81,8 +85,8 @@ def tile_list_oven_tray_refresh_kernel(tc, tab_words, tab_scales, offs, gT, w1, 
         load_table(1)
         load_w1(1, 0)
         load_w1(2, 0)
-        load_cub(0)
         load_table(2)
+        load_cub(0)
         for a in range(K_PASSES):
             load_w1(a, 1)
         load_state(3)
@@ -101,25 +105,25 @@ def tile_list_oven_tray_refresh_kernel(tc, tab_words, tab_scales, offs, gT, w1, 
 
         v_w = [keep.tile([P, S], U32, name="v_w%d" % a, align_bytes=64) for a in range(K_PASSES)]
         v_s = keep.tile([P, S], U8, name="v_s", align_bytes=64)
-        ZH = 2 * QUARTER
-        arena = keep.tile([P, 4 * ZH], F32, name="arena", align_bytes=64)
+
+        z_places = keep.tile([P, 4 * PLACE], F32, name="z_places", align_bytes=64)
         z_start = {0: 2, 1: 0, 2: 1, 3: 1}
         z_order = {0: (0, 1), 1: (1, 0), 2: (1, 0), 3: (1, 0)}
-
-        def picked(lo, hi, cols):
-            return picks[:, 0 : N_TILES * S].rearrange("p (i s) -> p i s", i=N_TILES)[:, lo:hi, cols]
-
+        z_bf = {q: z_places[:, PLACE * z_start[q] : PLACE * (z_start[q] + 2)].bitcast(BF16) for q in range(QUARTERS)}
         w1_w, w1_s, z_w, z_s = {}, {}, {}, {}
-        z_bf = {q: arena[:, ZH * z_start[q] : ZH * (z_start[q] + 2)].bitcast(BF16) for q in range(QUARTERS)}
-
-        work_slot = {(2, 0): "raw20", (3, 0): "raw11", (3, 1): "work31"}
-        HALF = PACK * QUARTER
 
         def listed(lo, hi):
             return offsets[:, LIST_COLS * lo : LIST_COLS * hi]
 
+        def picked(tile_lo, tile_hi, lo, hi):
+            by_tile = picks[:, 0 : N_TILES * S].rearrange("p (i s) -> p i s", i=N_TILES)
+            return by_tile[:, tile_lo:tile_hi, QUARTER * lo : QUARTER * hi]
+
         def gather_words(a, lo, hi):
             nc.vector.tensor_copy(v_w[a][:, QUARTER * lo : QUARTER * hi], tab_w[a][:].indirect(listed(lo, hi)))
+
+        def pick(i, lo, hi):
+            nc.vector.tensor_copy(picked(i, i + 1, lo, hi)[:, 0], state[i][:].indirect(listed(lo, hi)))
 
         def quantise_w1(a, b):
             w1_bf = ring.tile([P, PACK * PASS], BF16, name="w1_bf", tag="w1_bf", align_bytes=64)[:]
@@ -128,16 +132,16 @@ def tile_list_oven_tray_refresh_kernel(tc, tab_words, tab_scales, offs, gT, w1, 
             src = w1_raw[a, b].rearrange("p j (m t) -> p m j t", t=PACK)
             if b == 0:
                 dst = w1_bf.rearrange("p (t m j) -> p m j t", t=PACK, j=PACK)
-                if a == K_PASSES - 1:
-                    nc.scalar.activation(dst[:, 0 : P // 2], src[:, 0 : P // 2], ACT.Copy)
-                    nc.vector.tensor_copy(dst[:, P // 2 : P], src[:, P // 2 : P])
+                if a > 0:
+                    nc.scalar.activation(dst[:, 0:SCALAR_COLS], src[:, 0:SCALAR_COLS], ACT.Copy)
+                    nc.vector.tensor_copy(dst[:, SCALAR_COLS:P], src[:, SCALAR_COLS:P])
                 else:
                     nc.scalar.activation(dst, src, ACT.Copy)
                 nc.vector.quantize_mx(out=w1_w[a, b][:].bitcast(FP8X4), scales=w1_s[a, b][:], in_=w1_bf)
                 return
             pairs = [w1_bf[:, 0 : 2 * PASS], w1_bf[:, 2 * PASS :]]
             if a == K_PASSES - 1:
-                pairs[1] = arena[:, ZH + QUARTER : 2 * ZH + QUARTER].bitcast(BF16)
+                pairs[1] = z_places[:, PLACE + PLACE // 2 : 2 * PLACE + PLACE // 2].bitcast(BF16)
             for e in range(2):
                 nc.vector.tensor_copy(pairs[e].rearrange("p (t m j) -> p m j t", t=2, j=PACK), src[:, :, :, 2 * e : 2 * e + 2])
             for e in range(2):
@@ -147,87 +151,98 @@ def tile_list_oven_tray_refresh_kernel(tc, tab_words, tab_scales, offs, gT, w1, 
         def by_line(ap):
             return ap.rearrange("p (c t i) -> p c t i", t=PACK, i=LINE)
 
-        h_banks, h_sb, square, planes = {}, {}, {}, {}
+        gather_words(0, 0, QUARTERS)
+        nc.vector.tensor_copy(v_s[:], tab_s[:].indirect(offsets[:]))
+        quantise_w1(0, 0)
+        gather_words(1, 0, QUARTERS)
+        quantise_w1(1, 0)
+        quantise_w1(2, 0)
+        gather_words(2, 0, 1)
+        gather_words(2, 1, QUARTERS)
+        for a in range(K_PASSES):
+            quantise_w1(a, 1)
+        pick(3, 0, QUARTERS)
+        pick(2, 0, QUARTERS)
 
-        chain = keep.tile([P, 3 * HALF], F32, name="chain", tag="raw01", align_bytes=64)
-        first_h = keep.tile([P, 2 * HALF], F32, name="first_h", tag="raw00", align_bytes=64)
-        first_factor = keep.tile([P, 2 * HALF], F32, name="first_factor", tag="raw10", align_bytes=64)
-        square_start = {0: HALF + P, 1: 3 * P}
+        chain = keep.tile([P, 3 * UNIT], F32, name="chain", tag="raw01", align_bytes=64)
+        first_h = keep.tile([P, 2 * UNIT], F32, name="first_h", tag="raw00", align_bytes=64)
+        first_factor = keep.tile([P, 2 * UNIT], F32, name="first_factor", tag="raw10", align_bytes=64)
+        work20 = keep.tile([P, 2 * UNIT], F32, name="work20", tag="raw20", align_bytes=64)
+        work30 = keep.tile([P, 2 * UNIT], F32, name="work30", tag="raw11", align_bytes=64)
+        h_sb = {(0, 0): first_h[:, UNIT:], (1, 0): first_h[:, 0:UNIT], (2, 0): work20[:, 0:UNIT], (2, 1): chain[:, 0:UNIT], (3, 0): work30[:, 0:UNIT]}
+        square = {
+            (0, 0): first_factor[:, UNIT:],
+            (1, 0): first_factor[:, 0:UNIT],
+            (2, 0): work20[:, UNIT:],
+            (0, 1): chain[:, UNIT + P : 2 * UNIT + P],
+            (1, 1): chain[:, 3 * P : UNIT + 3 * P],
+            (2, 1): chain[:, UNIT : 2 * UNIT],
+            (3, 0): work30[:, UNIT:],
+        }
+        factors = dict(square)
+        factors[2, 0] = chain[:, 2 * UNIT :]
+        factors[0, 1] = picks[:, S : 2 * S]
+        factors[1, 1] = picks[:, 0:S]
+        h_banks = {}
 
-        def multiply(q, b, banks, halves=(0, 1)):
-            for u in halves:
-                h_bank = psum.tile([P, PACK, P], F32, name="h_bank", tag="bank%d" % banks[u])
-                h_banks[q, b, u] = h_bank
-                entries = slice(QUARTER * q + P * u, QUARTER * q + P * (u + 1))
-                for a in range(K_PASSES):
-                    for t in range(PACK):
-                        nc.tensor.matmul_mx(
-                            out=h_bank[:, t, :],
-                            lhsT=w1_w[a, b][:, P * t : P * (t + 1)].bitcast(FP8X4),
-                            lhsT_scale=w1_s[a, b][:, P * t : P * (t + 1)],
-                            rhs=v_w[a][:, entries].bitcast(FP8X4),
-                            rhs_scale=v_s[4 * a : P, entries],
-                            start=(a == 0 and t == 0),
-                            stop=(a == K_PASSES - 1 and t == PACK - 1),
-                        )
-            if (q, b) in square:
-                return
-            if (q, b) in VECTOR_PRODUCTS:
-                square[q, b] = chain[:, square_start[q] : square_start[q] + HALF]
-                planes[q, b] = picks[:, S * (1 - q) : S * (2 - q)]
-            else:
-                if b == 0 and q < 2:
-                    part = slice(HALF * (1 - q), HALF * (2 - q))
-                    h_sb[q, b] = first_h[:, part]
-                    square[q, b] = planes[q, b] = first_factor[:, part]
-                    return
-                if (q, b) == (2, 1):
-                    work = chain
-                else:
-                    work = keep.tile([P, 2 * HALF], F32, name="work%d%d" % (q, b), tag=work_slot[q, b], align_bytes=64)
-                h_sb[q, b] = work[:, 0:HALF]
-                square[q, b] = planes[q, b] = work[:, HALF : 2 * HALF]
-                if (q, b) == (2, 0):
-                    planes[q, b] = chain[:, 2 * HALF : 3 * HALF]
+        def multiply(q, b, u, bank):
+            h_bank = psum.tile([P, PACK, P], F32, name="h_bank", tag="bank%d" % bank)
+            h_banks[q, b, u] = h_bank
+            entries = slice(QUARTER * q + P * u, QUARTER * q + P * (u + 1))
+            for a in range(K_PASSES):
+                for t in range(PACK):
+                    nc.tensor.matmul_mx(
+                        out=h_bank[:, t, :],
+                        lhsT=w1_w[a, b][:, P * t : P * (t + 1)].bitcast(FP8X4),
+                        lhsT_scale=w1_s[a, b][:, P * t : P * (t + 1)],
+                        rhs=v_w[a][:, entries].bitcast(FP8X4),
+                        rhs_scale=v_s[4 * a : P, entries],
+                        start=(a == 0 and t == 0),
+                        stop=(a == K_PASSES - 1 and t == PACK - 1),
+                    )
+
+        def multiply_both(q, b, banks):
+            for u in range(2):
+                multiply(q, b, u, banks[u])
 
         def h_lines(q, b, u):
             return h_banks[q, b, u][:].rearrange("p t (c i) -> p c t i", i=LINE)
 
-        def squares(q, b, banks=(0, 1)):
-            for u in banks:
-                if (q, b) in VECTOR_PRODUCTS:
-                    nc.scalar.activation(square[q, b].rearrange("p (t u j) -> p u t j", t=PACK, u=2)[:, u], h_banks[q, b, u][:], ACT.Square)
-                else:
-                    nc.scalar.activation(by_line(square[q, b][:, PACK * P * u : PACK * P * (u + 1)]), h_lines(q, b, u), ACT.Square)
-
-        def copy_h(q, b, banks=(0, 1)):
-            for u in banks:
-                nc.scalar.copy(by_line(h_sb[q, b][:, PACK * P * u : PACK * P * (u + 1)]), h_lines(q, b, u))
-
-        def factor(q, b, planes_now=(0, 3, 1, 2)):
+        def squares(q, b, u):
             if (q, b) in VECTOR_PRODUCTS:
-                src = square[q, b].rearrange("p (t u j) -> p t u j", u=2, t=PACK)
-                dst = planes[q, b].rearrange("p (u t j) -> p t u j", u=2, t=PACK)
+                nc.scalar.activation(square[q, b].rearrange("p (t u j) -> p u t j", t=PACK, u=2)[:, u], h_banks[q, b, u][:], ACT.Square)
             else:
-                src, dst = [by_line(x).rearrange("p c t i -> p t c i") for x in (square[q, b], planes[q, b])]
-            for t in planes_now:
+                nc.scalar.activation(by_line(square[q, b][:, BANK * u : BANK * (u + 1)]), h_lines(q, b, u), ACT.Square)
+
+        def copy_h(q, b, u):
+            nc.scalar.copy(by_line(h_sb[q, b][:, BANK * u : BANK * (u + 1)]), h_lines(q, b, u))
+
+        def scale_planes(dst, src, b, planes):
+            for t in planes:
                 nc.scalar.activation(dst[:, t], src[:, t], ACT.Copy, bias=1.0, scale=cub_sb[b][:, t : t + 1])
 
+        def factor(q, b, planes=PLANE_ORDER):
+            if (q, b) in VECTOR_PRODUCTS:
+                src = square[q, b].rearrange("p (t u j) -> p t u j", u=2, t=PACK)
+                dst = factors[q, b].rearrange("p (u t j) -> p t u j", u=2, t=PACK)
+            else:
+                src, dst = [by_line(x).rearrange("p c t i -> p t c i") for x in (square[q, b], factors[q, b])]
+            scale_planes(dst, src, b, planes)
+
         def product(q, b):
-            place = z_order[q][b]
-            z_half = z_bf[q][:, HALF * place : HALF * (place + 1)]
+            z_half = z_bf[q][:, UNIT * z_order[q][b] : UNIT * (z_order[q][b] + 1)]
             if (q, b) in VECTOR_PRODUCTS:
                 for u in range(2):
-                    part = slice(PACK * P * u, PACK * P * (u + 1))
+                    part = slice(BANK * u, BANK * (u + 1))
                     nc.vector.tensor_tensor(
                         z_half[:, part].rearrange("p (c i t) -> p c t i", i=RUN, t=PACK),
                         h_banks[q, b, u][:].rearrange("p t (c i) -> p c t i", i=RUN),
-                        planes[q, b][:, part].rearrange("p (t c i) -> p c t i", t=PACK, i=RUN),
+                        factors[q, b][:, part].rearrange("p (t c i) -> p c t i", t=PACK, i=RUN),
                         ALU.mult,
                     )
             else:
                 nc.gpsimd.tensor_tensor(
-                    z_half.rearrange("p (c i t) -> p c t i", i=LINE, t=PACK), by_line(h_sb[q, b]), by_line(planes[q, b]), ALU.mult
+                    z_half.rearrange("p (c i t) -> p c t i", i=LINE, t=PACK), by_line(h_sb[q, b]), by_line(factors[q, b]), ALU.mult
                 )
 
         def quantise_z(q, slot):
@@ -236,8 +251,9 @@ def tile_list_oven_tray_refresh_kernel(tc, tab_words, tab_scales, offs, gT, w1, 
             nc.vector.quantize_mx(out=z_w[q][:].bitcast(FP8X4), scales=z_s[q][:], in_=z_bf[q])
 
         moved_at = {}
+        new_at = {}
 
-        def drive_tiles(q, tiles, bank):
+        def drive(q, tiles, bank):
             y_bank = psum.tile([P, len(tiles), QUARTER], F32, name="y_bank", tag="bank%d" % bank)
             for e, i in enumerate(tiles):
                 for c in range(0, QUARTER, P):
@@ -255,134 +271,133 @@ def tile_list_oven_tray_refresh_kernel(tc, tab_words, tab_scales, offs, gT, w1, 
             for e, i in enumerate(tiles):
                 nc.scalar.activation(moved_at[q, i], y_bank[:, e, :], ACT.Copy, scale=step_sb[:, i : i + 1])
 
-        def drive(q, banks):
-            drive_tiles(q, (3, 2), banks[1])
-            drive_tiles(q, (1, 0), banks[0])
+        def moved_tile(q, tile_lo, tile_hi, slot):
+            tile = keep.tile([P, tile_hi - tile_lo, QUARTER], F32, name="moved%d%d" % (q, tile_lo), tag=slot, align_bytes=64)
+            for i in range(tile_lo, tile_hi):
+                moved_at[q, i] = tile[:, i - tile_lo]
+            return tile[:]
 
-        def moved_tile(q, lo, hi, slot):
-            tile = keep.tile([P, hi - lo, QUARTER], F32, name="moved%d%d" % (q, lo), tag=slot, align_bytes=64)
-            for i in range(lo, hi):
-                moved_at[q, i] = tile[:, i - lo]
-            return tile
+        def add_up(q, tile_lo, tile_hi, moved, new):
+            for i in range(tile_lo, tile_hi):
+                new_at[q, i] = new[:, i - tile_lo]
+            nc.gpsimd.tensor_tensor(new, picked(tile_lo, tile_hi, q, q + 1), moved, ALU.add)
 
-        new_at = {}
-
-        def add_up(q, lo, hi, moved, new=None):
-            old = picked(lo, hi, slice(QUARTER * q, QUARTER * (q + 1)))
-            new = old if new is None else new.rearrange("p (i j) -> p i j", j=QUARTER)
-            for i in range(lo, hi):
-                new_at[q, i] = new[:, i - lo]
-            nc.gpsimd.tensor_tensor(new, old, moved[:], ALU.add)
+        def add_in_place(q, tile_lo, tile_hi, moved):
+            add_up(q, tile_lo, tile_hi, moved, picked(tile_lo, tile_hi, q, q + 1))
 
         def put(q, i):
             nc.vector.tensor_copy(state[i][:].indirect(listed(q, q + 1)), new_at[q, i])
 
-        def put_fused(lo, hi, i, values):
-            nc.vector.tensor_tensor(state[i][:].indirect(listed(lo, hi)), picked(i, i + 1, slice(QUARTER * lo, QUARTER * hi))[:, 0], values, ALU.add)
+        def put_fused(lo, hi, i, moved):
+            nc.vector.tensor_tensor(state[i][:].indirect(listed(lo, hi)), picked(i, i + 1, lo, hi)[:, 0], moved, ALU.add)
 
         def store(i):
             nc.sync.dma_start(out[P * i : P * (i + 1), :], state[i][:])
 
-        gather_words(0, 0, QUARTERS)
-        nc.vector.tensor_copy(v_s[:], tab_s[:].indirect(offsets[:]))
-        quantise_w1(0, 0)
-        gather_words(1, 0, QUARTERS)
-        quantise_w1(1, 0)
-        quantise_w1(2, 0)
-        gather_words(2, 0, 1)
-        gather_words(2, 1, QUARTERS)
-        for a in range(K_PASSES):
-            quantise_w1(a, 1)
-        def pick(i, lo=0, hi=QUARTERS):
-            nc.vector.tensor_copy(picked(i, i + 1, slice(QUARTER * lo, QUARTER * hi))[:, 0], state[i][:].indirect(listed(lo, hi)))
-
-        pick(3)
-        pick(2)
+        def one_tile(ap):
+            return ap.rearrange("p (i j) -> p i j", i=1)
 
         for q in range(2):
-            multiply(q, 0, (2 * q, 2 * q + 1))
-            squares(q, 0)
-            copy_h(q, 0)
-        in_planes = by_line(first_factor[:]).rearrange("p c t i -> p t c i")
-        for t in range(PACK):
-            nc.scalar.activation(in_planes[:, t], in_planes[:, t], ACT.Copy, bias=1.0, scale=cub_sb[0][:, t : t + 1])
+            multiply_both(q, 0, (2 * q, 2 * q + 1))
+            for u in range(2):
+                squares(q, 0, u)
+            for u in range(2):
+                copy_h(q, 0, u)
+        first_planes = by_line(first_factor[:]).rearrange("p c t i -> p t c i")
+        scale_planes(first_planes, first_planes, 0, range(PACK))
         for q in range(2):
             product(q, 0)
-        multiply(2, 0, (0, 1))
-        squares(2, 0)
-        copy_h(2, 0, (0,))
-        multiply(0, 1, (4, 5))
-        squares(0, 1)
-        copy_h(2, 0, (1,))
+        multiply_both(2, 0, (0, 1))
+        for u in range(2):
+            squares(2, 0, u)
+        copy_h(2, 0, 0)
+
+        multiply_both(0, 1, (4, 5))
+        for u in range(2):
+            squares(0, 1, u)
+        copy_h(2, 0, 1)
         factor(0, 1)
         product(0, 1)
         pick(1, 0, 1)
         quantise_z(0, "z0")
-        pick(1, 1, 4)
-        factor(2, 0, (0, 3, 1))
-        multiply(1, 1, (6, 7))
-        squares(1, 1)
-        factor(2, 0, (2,))
+        pick(1, 1, QUARTERS)
+
+        factor(2, 0, PLANE_ORDER[:-1])
+        multiply_both(1, 1, (6, 7))
+        for u in range(2):
+            squares(1, 1, u)
+        factor(2, 0, PLANE_ORDER[-1:])
         product(2, 0)
         factor(1, 1)
         product(1, 1)
         pick(0, 0, 1)
-        pick(0, 1, 4)
-        upper = moved_tile(0, 1, 4, "upper")
+        pick(0, 1, QUARTERS)
+
+        upper = moved_tile(0, 1, N_TILES, "upper")
         lowest = moved_tile(0, 0, 1, "lowest")
-        multiply(2, 1, (4, 1), (0,))
-        drive(0, (0, 1))
-        multiply(2, 1, (4, 1), (1,))
-        add_up(0, 1, 4, upper)
+        multiply(2, 1, 0, 4)
+        drive(0, (3, 2), 1)
+        drive(0, (1, 0), 0)
+        multiply(2, 1, 1, 1)
+        add_in_place(0, 1, N_TILES, upper)
         quantise_z(1, "upper")
         for i in (3, 2, 1):
             put(0, i)
         for u in range(2):
-            squares(2, 1, (u,))
-            copy_h(2, 1, (u,))
+            squares(2, 1, u)
+            copy_h(2, 1, u)
         factor(2, 1)
         product(2, 1)
-        add_up(0, 0, 1, lowest, arena[:, 0:QUARTER])
+        add_up(0, 0, 1, lowest, one_tile(z_places[:, 0:QUARTER]))
         put(0, 0)
-        multiply(3, 0, (0, 5), (0,))
-        squares(3, 0, (0,))
-        copy_h(3, 0, (0,))
-        second = moved_tile(1, 0, 4, "second")
-        drive(1, (3, 5))
-        add_up(1, 0, 4, second)
+
+        multiply(3, 0, 0, 0)
+        squares(3, 0, 0)
+        copy_h(3, 0, 0)
+        second = moved_tile(1, 0, N_TILES, "second")
+        drive(1, (3, 2), 5)
+        drive(1, (1, 0), 3)
+        add_in_place(1, 0, N_TILES, second)
         quantise_z(2, "second")
         for i in (3, 2, 1, 0):
             put(1, i)
-        multiply(3, 0, (0, 5), (1,))
-        squares(3, 0, (1,))
-        copy_h(3, 0, (1,))
+        multiply(3, 0, 1, 5)
+        squares(3, 0, 1)
+        copy_h(3, 0, 1)
         factor(3, 0)
         product(3, 0)
-        multiply(3, 1, (3, 5))
-        squares(3, 1)
-        copy_h(3, 1)
-        moved_at[2, 3] = arena[:, ZH : ZH + QUARTER]
-        drive_tiles(2, (3,), 3)
+        multiply_both(3, 1, (3, 5))
+        work31 = keep.tile([P, 2 * UNIT], F32, name="work31", tag="work31", align_bytes=64)
+        h_sb[3, 1] = work31[:, 0:UNIT]
+        square[3, 1] = factors[3, 1] = work31[:, UNIT:]
+        for u in range(2):
+            squares(3, 1, u)
+        for u in range(2):
+            copy_h(3, 1, u)
+
+        moved_at[2, 3] = z_places[:, PLACE : PLACE + QUARTER]
+        drive(2, (3,), 3)
         factor(3, 1)
-        add_up(2, 3, 4, moved_at[2, 3].rearrange("p (i j) -> p i j", i=1))
+        add_in_place(2, 3, N_TILES, one_tile(moved_at[2, 3]))
         put(2, 3)
         product(3, 1)
         quantise_z(3, "z0")
+
         late = keep.tile([P, 5 * QUARTER], F32, name="late", tag="work31", align_bytes=64)
         moved_at[2, 2] = late[:, 0:QUARTER]
+        both = {i: late[:, QUARTER * (1 + 2 * i) : QUARTER * (3 + 2 * i)] for i in (1, 0)}
         for i in (1, 0):
-            for q in (2, 3):
-                moved_at[q, i] = late[:, QUARTER * (1 + 2 * i + q - 2) : QUARTER * (2 + 2 * i + q - 2)]
-        moved_tile(3, 2, 4, "last")
-        drive_tiles(2, (2,), 5)
+            moved_at[2, i], moved_at[3, i] = both[i][:, 0:QUARTER], both[i][:, QUARTER:]
+        moved_tile(3, 2, N_TILES, "last")
+        drive(2, (2,), 5)
         put_fused(2, 3, 2, moved_at[2, 2])
-        drive_tiles(2, (1, 0), 3)
-        drive_tiles(3, (3,), 6)
-        drive_tiles(3, (2,), 2)
-        drive_tiles(3, (1, 0), 4)
+        drive(2, (1, 0), 3)
+        drive(3, (3,), 6)
+        drive(3, (2,), 2)
+        drive(3, (1, 0), 4)
         for i in (3, 2):
             put_fused(3, 4, i, moved_at[3, i])
             store(i)
         for i in (1, 0):
-            put_fused(2, 4, i, late[:, QUARTER * (1 + 2 * i) : QUARTER * (3 + 2 * i)])
+            put_fused(2, 4, i, both[i])
             store(i)

@@ -33,8 +33,7 @@ RUN = 2
 LINE = 4
 RING = 3
 SCALAR_COLS = 48
-VECTOR_PRODUCTS = ((0, 1), (1, 1))
-PLANE_ORDER = (0, 3, 1, 2)
+KB = 256
 
 
 def tile_list_oven_tray_refresh_kernel(tc, tab_words, tab_scales, offs, gT, w1, cub, w4_words, w4_scales, step, out):
@@ -106,10 +105,15 @@ def tile_list_oven_tray_refresh_kernel(tc, tab_words, tab_scales, offs, gT, w1, 
         v_w = [keep.tile([P, S], U32, name="v_w%d" % a, align_bytes=64) for a in range(K_PASSES)]
         v_s = keep.tile([P, S], U8, name="v_s", align_bytes=64)
 
-        z_places = keep.tile([P, 4 * PLACE], F32, name="z_places", align_bytes=64)
-        z_start = {0: 2, 1: 0, 2: 1, 3: 1}
-        z_order = {0: (0, 1), 1: (1, 0), 2: (1, 0), 3: (1, 0)}
-        z_bf = {q: z_places[:, PLACE * z_start[q] : PLACE * (z_start[q] + 2)].bitcast(BF16) for q in range(QUARTERS)}
+        arena = keep.tile([P, 14 * KB], F32, name="arena", align_bytes=64)
+
+        def at(lo, hi):
+            return arena[:, KB * lo : KB * hi]
+
+        z_start = {0: 7, 1: 5, 2: 3, 3: 3}
+        z_order = {0: (1, 0), 1: (0, 1), 2: (0, 1), 3: (0, 1)}
+        z_bf = {q: at(z_start[q], z_start[q] + 4).bitcast(BF16) for q in range(QUARTERS)}
+        rounded_at = {0: (8, 10), 1: (0, 2), 2: (12, 4)}
         w1_w, w1_s, z_w, z_s = {}, {}, {}, {}
 
         def listed(lo, hi):
@@ -126,11 +130,11 @@ def tile_list_oven_tray_refresh_kernel(tc, tab_words, tab_scales, offs, gT, w1, 
             nc.vector.tensor_copy(picked(i, i + 1, lo, hi)[:, 0], state[i][:].indirect(listed(lo, hi)))
 
         def quantise_w1(a, b):
-            w1_bf = ring.tile([P, PACK * PASS], BF16, name="w1_bf", tag="w1_bf", align_bytes=64)[:]
             w1_w[a, b] = keep.tile([P, PASS], U32, name="w1_w%d%d" % (a, b), align_bytes=64)
             w1_s[a, b] = keep.tile([P, PASS], U8, name="w1_s%d%d" % (a, b), align_bytes=64)
             src = w1_raw[a, b].rearrange("p j (m t) -> p m j t", t=PACK)
             if b == 0:
+                w1_bf = ring.tile([P, PACK * PASS], BF16, name="w1_bf", tag="w1_bf", align_bytes=64)[:]
                 dst = w1_bf.rearrange("p (t m j) -> p m j t", t=PACK, j=PACK)
                 if a > 0:
                     nc.scalar.activation(dst[:, 0:SCALAR_COLS], src[:, 0:SCALAR_COLS], ACT.Copy)
@@ -139,9 +143,7 @@ def tile_list_oven_tray_refresh_kernel(tc, tab_words, tab_scales, offs, gT, w1, 
                     nc.scalar.activation(dst, src, ACT.Copy)
                 nc.vector.quantize_mx(out=w1_w[a, b][:].bitcast(FP8X4), scales=w1_s[a, b][:], in_=w1_bf)
                 return
-            pairs = [w1_bf[:, 0 : 2 * PASS], w1_bf[:, 2 * PASS :]]
-            if a == K_PASSES - 1:
-                pairs[1] = z_places[:, PLACE + PLACE // 2 : 2 * PLACE + PLACE // 2].bitcast(BF16)
+            pairs = [at(rounded_at[a][e], rounded_at[a][e] + 2).bitcast(BF16) for e in range(2)]
             for e in range(2):
                 nc.vector.tensor_copy(pairs[e].rearrange("p (t m j) -> p m j t", t=2, j=PACK), src[:, :, :, 2 * e : 2 * e + 2])
             for e in range(2):
@@ -151,45 +153,15 @@ def tile_list_oven_tray_refresh_kernel(tc, tab_words, tab_scales, offs, gT, w1, 
         def by_line(ap):
             return ap.rearrange("p (c t i) -> p c t i", t=PACK, i=LINE)
 
-        gather_words(0, 0, QUARTERS)
-        nc.vector.tensor_copy(v_s[:], tab_s[:].indirect(offsets[:]))
-        quantise_w1(0, 0)
-        gather_words(1, 0, QUARTERS)
-        quantise_w1(1, 0)
-        quantise_w1(2, 0)
-        gather_words(2, 0, 1)
-        gather_words(2, 1, QUARTERS)
-        for a in range(K_PASSES):
-            quantise_w1(a, 1)
-        pick(3, 0, QUARTERS)
-        pick(2, 0, QUARTERS)
-
-        chain = keep.tile([P, 3 * UNIT], F32, name="chain", tag="raw01", align_bytes=64)
-        first_h = keep.tile([P, 2 * UNIT], F32, name="first_h", tag="raw00", align_bytes=64)
-        first_factor = keep.tile([P, 2 * UNIT], F32, name="first_factor", tag="raw10", align_bytes=64)
-        work20 = keep.tile([P, 2 * UNIT], F32, name="work20", tag="raw20", align_bytes=64)
-        work30 = keep.tile([P, 2 * UNIT], F32, name="work30", tag="raw11", align_bytes=64)
-        h_sb = {(0, 0): first_h[:, UNIT:], (1, 0): first_h[:, 0:UNIT], (2, 0): work20[:, 0:UNIT], (2, 1): chain[:, 0:UNIT], (3, 0): work30[:, 0:UNIT]}
-        square = {
-            (0, 0): first_factor[:, UNIT:],
-            (1, 0): first_factor[:, 0:UNIT],
-            (2, 0): work20[:, UNIT:],
-            (0, 1): chain[:, UNIT + P : 2 * UNIT + P],
-            (1, 1): chain[:, 3 * P : UNIT + 3 * P],
-            (2, 1): chain[:, UNIT : 2 * UNIT],
-            (3, 0): work30[:, UNIT:],
-        }
-        factors = dict(square)
-        factors[2, 0] = chain[:, 2 * UNIT :]
-        factors[0, 1] = picks[:, S : 2 * S]
-        factors[1, 1] = picks[:, 0:S]
         h_banks = {}
+        h_sb, square, factors = {}, {}, {}
 
-        def multiply(q, b, u, bank):
-            h_bank = psum.tile([P, PACK, P], F32, name="h_bank", tag="bank%d" % bank)
-            h_banks[q, b, u] = h_bank
+        def multiply(q, b, u, bank, passes=range(K_PASSES)):
+            if 0 in passes:
+                h_banks[q, b, u] = psum.tile([P, PACK, P], F32, name="h_bank", tag="bank%d" % bank)
+            h_bank = h_banks[q, b, u]
             entries = slice(QUARTER * q + P * u, QUARTER * q + P * (u + 1))
-            for a in range(K_PASSES):
+            for a in passes:
                 for t in range(PACK):
                     nc.tensor.matmul_mx(
                         out=h_bank[:, t, :],
@@ -201,61 +173,60 @@ def tile_list_oven_tray_refresh_kernel(tc, tab_words, tab_scales, offs, gT, w1, 
                         stop=(a == K_PASSES - 1 and t == PACK - 1),
                     )
 
-        def multiply_both(q, b, banks):
+        def multiply_both(q, b, banks, passes=range(K_PASSES)):
             for u in range(2):
-                multiply(q, b, u, banks[u])
+                multiply(q, b, u, banks[u], passes)
 
         def h_lines(q, b, u):
             return h_banks[q, b, u][:].rearrange("p t (c i) -> p c t i", i=LINE)
 
-        def squares(q, b, u):
-            if (q, b) in VECTOR_PRODUCTS:
-                nc.scalar.activation(square[q, b].rearrange("p (t u j) -> p u t j", t=PACK, u=2)[:, u], h_banks[q, b, u][:], ACT.Square)
-            else:
-                nc.scalar.activation(by_line(square[q, b][:, BANK * u : BANK * (u + 1)]), h_lines(q, b, u), ACT.Square)
+        def half(ap, u):
+            return ap[:, BANK * u : BANK * (u + 1)]
 
-        def copy_h(q, b, u):
-            nc.scalar.copy(by_line(h_sb[q, b][:, BANK * u : BANK * (u + 1)]), h_lines(q, b, u))
+        def squares(q, b, u, dst):
+            nc.scalar.activation(by_line(dst), h_lines(q, b, u), ACT.Square)
 
-        def scale_planes(dst, src, b, planes):
+        def copy_h(q, b, u, dst):
+            nc.scalar.copy(by_line(dst), h_lines(q, b, u))
+
+        def scale_planes(dst, src, b, planes=range(PACK)):
             for t in planes:
                 nc.scalar.activation(dst[:, t], src[:, t], ACT.Copy, bias=1.0, scale=cub_sb[b][:, t : t + 1])
 
-        def factor(q, b, planes=PLANE_ORDER):
-            if (q, b) in VECTOR_PRODUCTS:
-                src = square[q, b].rearrange("p (t u j) -> p t u j", u=2, t=PACK)
-                dst = factors[q, b].rearrange("p (u t j) -> p t u j", u=2, t=PACK)
-            else:
-                src, dst = [by_line(x).rearrange("p c t i -> p t c i") for x in (square[q, b], factors[q, b])]
-            scale_planes(dst, src, b, planes)
+        def factor(dst, src, b):
+            scale_planes(by_line(dst).rearrange("p c t i -> p t c i"), by_line(src).rearrange("p c t i -> p t c i"), b)
 
-        def product(q, b):
-            z_half = z_bf[q][:, UNIT * z_order[q][b] : UNIT * (z_order[q][b] + 1)]
-            if (q, b) in VECTOR_PRODUCTS:
-                for u in range(2):
-                    part = slice(BANK * u, BANK * (u + 1))
-                    nc.vector.tensor_tensor(
-                        z_half[:, part].rearrange("p (c i t) -> p c t i", i=RUN, t=PACK),
-                        h_banks[q, b, u][:].rearrange("p t (c i) -> p c t i", i=RUN),
-                        factors[q, b][:, part].rearrange("p (t c i) -> p c t i", t=PACK, i=RUN),
-                        ALU.mult,
-                    )
-            else:
-                nc.gpsimd.tensor_tensor(
-                    z_half.rearrange("p (c i t) -> p c t i", i=LINE, t=PACK), by_line(h_sb[q, b]), by_line(factors[q, b]), ALU.mult
-                )
+        def z_part(q, b, lo, hi):
+            start = UNIT * z_order[q][b]
+            return z_bf[q][:, start + BANK * lo : start + BANK * hi]
 
-        def quantise_z(q, slot):
+        def product(q, b, lo, hi, h, f):
+            nc.gpsimd.tensor_tensor(z_part(q, b, lo, hi).rearrange("p (c i t) -> p c t i", i=LINE, t=PACK), by_line(h), by_line(f), ALU.mult)
+
+        def plane_squares(q, b, u, dst):
+            nc.scalar.activation(dst.rearrange("p (t j) -> p t j", t=PACK), h_banks[q, b, u][:], ACT.Square)
+
+        def vector_product(q, b, u, f):
+            nc.vector.tensor_tensor(
+                z_part(q, b, u, u + 1).rearrange("p (c i t) -> p c t i", i=RUN, t=PACK),
+                h_banks[q, b, u][:].rearrange("p t (c i) -> p c t i", i=RUN),
+                f.rearrange("p (t c i) -> p c t i", t=PACK, i=RUN),
+                ALU.mult,
+            )
+
+        def quantise_z(q, slot, scale_slot):
             z_w[q] = keep.tile([P, R_PASSES * QUARTER], U32, name="z_w%d" % q, tag=slot, align_bytes=64)
-            z_s[q] = keep.tile([P, R_PASSES * QUARTER], U8, name="z_s%d" % q, align_bytes=64)
+            z_s[q] = keep.tile([P, R_PASSES * QUARTER], U8, name="z_s%d" % q, tag=scale_slot, align_bytes=64)
             nc.vector.quantize_mx(out=z_w[q][:].bitcast(FP8X4), scales=z_s[q][:], in_=z_bf[q])
 
         moved_at = {}
         new_at = {}
+        y_banks = {}
 
         def drive(q, tiles, bank):
             y_bank = psum.tile([P, len(tiles), QUARTER], F32, name="y_bank", tag="bank%d" % bank)
             for e, i in enumerate(tiles):
+                y_banks[q, i] = y_bank[:, e, :]
                 for c in range(0, QUARTER, P):
                     for b in range(R_PASSES):
                         z_cols = slice(QUARTER * z_order[q][b] + c, QUARTER * z_order[q][b] + c + P)
@@ -268,25 +239,31 @@ def tile_list_oven_tray_refresh_kernel(tc, tab_words, tab_scales, offs, gT, w1, 
                             start=(b == 0),
                             stop=(b == R_PASSES - 1),
                         )
-            for e, i in enumerate(tiles):
-                nc.scalar.activation(moved_at[q, i], y_bank[:, e, :], ACT.Copy, scale=step_sb[:, i : i + 1])
+            for i in tiles:
+                nc.scalar.activation(moved_at[q, i], y_banks[q, i], ACT.Copy, scale=step_sb[:, i : i + 1])
+
+        def moved_in(q, tile_lo, tile_hi, ap):
+            rows = ap.rearrange("p (i j) -> p i j", j=QUARTER)
+            for i in range(tile_lo, tile_hi):
+                moved_at[q, i] = rows[:, i - tile_lo]
+            return rows
 
         def moved_tile(q, tile_lo, tile_hi, slot):
-            tile = keep.tile([P, tile_hi - tile_lo, QUARTER], F32, name="moved%d%d" % (q, tile_lo), tag=slot, align_bytes=64)
-            for i in range(tile_lo, tile_hi):
-                moved_at[q, i] = tile[:, i - tile_lo]
-            return tile[:]
+            tile = keep.tile([P, (tile_hi - tile_lo) * QUARTER], F32, name="moved%d%d" % (q, tile_lo), tag=slot, align_bytes=64)
+            return moved_in(q, tile_lo, tile_hi, tile[:])
 
-        def add_up(q, tile_lo, tile_hi, moved, new):
+        def add_in_place(q, tile_lo, tile_hi, moved):
+            new = picked(tile_lo, tile_hi, q, q + 1)
+            nc.gpsimd.tensor_tensor(new, new, moved, ALU.add)
+
+        def add_into(q, tile_lo, tile_hi, moved, ap):
+            new = ap.rearrange("p (i j) -> p i j", j=QUARTER)
             for i in range(tile_lo, tile_hi):
                 new_at[q, i] = new[:, i - tile_lo]
             nc.gpsimd.tensor_tensor(new, picked(tile_lo, tile_hi, q, q + 1), moved, ALU.add)
 
-        def add_in_place(q, tile_lo, tile_hi, moved):
-            add_up(q, tile_lo, tile_hi, moved, picked(tile_lo, tile_hi, q, q + 1))
-
         def put(q, i):
-            nc.vector.tensor_copy(state[i][:].indirect(listed(q, q + 1)), new_at[q, i])
+            nc.vector.tensor_copy(state[i][:].indirect(listed(q, q + 1)), new_at.get((q, i), picked(i, i + 1, q, q + 1)[:, 0]))
 
         def put_fused(lo, hi, i, moved):
             nc.vector.tensor_tensor(state[i][:].indirect(listed(lo, hi)), picked(i, i + 1, lo, hi)[:, 0], moved, ALU.add)
@@ -294,96 +271,135 @@ def tile_list_oven_tray_refresh_kernel(tc, tab_words, tab_scales, offs, gT, w1, 
         def store(i):
             nc.sync.dma_start(out[P * i : P * (i + 1), :], state[i][:])
 
-        def one_tile(ap):
-            return ap.rearrange("p (i j) -> p i j", i=1)
+        def work(name, slot, width):
+            return keep.tile([P, width], F32, name=name, tag=slot, align_bytes=64)[:]
 
-        for q in range(2):
-            multiply_both(q, 0, (2 * q, 2 * q + 1))
+        def pair(name, slot):
+            both_inputs = work(name, slot, UNIT)
+            return half(both_inputs, 0), half(both_inputs, 1)
+
+        gather_words(0, 0, QUARTERS)
+        nc.vector.tensor_copy(v_s[:], tab_s[:].indirect(offsets[:]))
+        quantise_w1(0, 0)
+        gather_words(1, 0, QUARTERS)
+        quantise_w1(1, 0)
+        quantise_w1(2, 0)
+        gather_words(2, 0, 1)
+        gather_words(2, 1, QUARTERS)
+        for a in range(K_PASSES):
+            for q in range(QUARTERS):
+                multiply_both(q, 0, (2 * q, 2 * q + 1), (a,))
+
+        def whole_unit(q, b, h, f):
             for u in range(2):
-                squares(q, 0, u)
+                squares(q, b, u, half(f, u))
             for u in range(2):
-                copy_h(q, 0, u)
-        first_planes = by_line(first_factor[:]).rearrange("p c t i -> p t c i")
-        scale_planes(first_planes, first_planes, 0, range(PACK))
-        for q in range(2):
-            product(q, 0)
-        multiply_both(2, 0, (0, 1))
-        for u in range(2):
-            squares(2, 0, u)
-        copy_h(2, 0, 0)
+                copy_h(q, b, u, half(h, u))
+            factor(f, f, b)
+            product(q, b, 0, 2, h, f)
 
-        multiply_both(0, 1, (4, 5))
-        for u in range(2):
-            squares(0, 1, u)
-        copy_h(2, 0, 1)
-        factor(0, 1)
-        product(0, 1)
-        pick(1, 0, 1)
-        quantise_z(0, "z0")
-        pick(1, 1, QUARTERS)
+        def unit_inputs(name, slot):
+            both_inputs = work(name, slot, 2 * UNIT)
+            return both_inputs[:, 0:UNIT], both_inputs[:, UNIT:]
 
-        factor(2, 0, PLANE_ORDER[:-1])
-        multiply_both(1, 1, (6, 7))
+        first = at(0, 4)
         for u in range(2):
-            squares(1, 1, u)
-        factor(2, 0, PLANE_ORDER[-1:])
-        product(2, 0)
-        factor(1, 1)
-        product(1, 1)
-        pick(0, 0, 1)
-        pick(0, 1, QUARTERS)
+            plane_squares(0, 0, u, half(first, u))
+        for u in range(2):
+            planes = half(first, u).rearrange("p (t j) -> p t j", t=PACK)
+            scale_planes(planes, planes, 0)
+        quantise_w1(0, 1)
+        for u in range(2):
+            vector_product(0, 0, u, half(first, u))
+        quantise_w1(1, 1)
+        quantise_w1(2, 1)
+        pick(3, 0, QUARTERS)
+        pick(2, 0, QUARTERS)
+        whole_unit(1, 0, *unit_inputs("work10", "raw00"))
+        whole_unit(2, 0, *unit_inputs("work20", "raw10"))
 
-        upper = moved_tile(0, 1, N_TILES, "upper")
-        lowest = moved_tile(0, 0, 1, "lowest")
-        multiply(2, 1, 0, 4)
-        drive(0, (3, 2), 1)
-        drive(0, (1, 0), 0)
-        multiply(2, 1, 1, 1)
-        add_in_place(0, 1, N_TILES, upper)
-        quantise_z(1, "upper")
-        for i in (3, 2, 1):
+        multiply_both(0, 1, (0, 1), (0, 1))
+        multiply_both(1, 1, (2, 3), (0, 1))
+        for u in (1, 0):
+            multiply(0, 1, u, u, (2,))
+        multiply_both(1, 1, (2, 3), (2,))
+        work11 = work("work11", "raw20", 2 * UNIT)
+        f11, h11, square01 = work11[:, 0:UNIT], work11[:, UNIT:], work11[:, 3 * KB : 7 * KB]
+        spread = picks[:, S - QUARTER : S + 5 * QUARTER].rearrange("p (u x) -> p u x", u=2)[:, :, 0:BANK]
+        for u in (1, 0):
+            plane_squares(0, 1, u, half(square01, u))
+        squares(1, 1, 0, half(f11, 0))
+        scale_planes(spread.rearrange("p u (t j) -> p t u j", t=PACK), square01.rearrange("p (u t j) -> p t u j", u=2, t=PACK), 1)
+        for u in (1, 0):
+            vector_product(0, 1, u, spread[:, u])
+        pick(1, 3, QUARTERS)
+        quantise_z(0, "z_w0", "z_s0")
+        pick(1, 0, 3)
+        pick(0, 0, QUARTERS)
+
+        squares(1, 1, 1, half(f11, 1))
+        for u in range(2):
+            copy_h(1, 1, u, half(h11, u))
+        factor(f11, f11, 1)
+        product(1, 1, 0, 2, h11, f11)
+        multiply(2, 1, 0, 2)
+        h21, f21 = unit_inputs("work21", "raw01")
+        squares(2, 1, 0, half(f21, 0))
+        copy_h(2, 1, 0, half(h21, 0))
+        top = moved_tile(0, 3, 4, "top0")
+        middle = moved_tile(0, 1, 3, "middle0")
+        lowest = moved_tile(0, 0, 1, "lowest0")
+        drive(0, (3,), 5)
+        drive(0, (2, 1), 0)
+        drive(0, (0,), 1)
+        add_in_place(0, 3, 4, top)
+        add_in_place(0, 1, 3, middle)
+        put(0, 3)
+        quantise_z(1, "middle0", "z_s1")
+        add_into(0, 0, 1, lowest, at(8, 9))
+        for i in (2, 1, 0):
             put(0, i)
-        for u in range(2):
-            squares(2, 1, u)
-            copy_h(2, 1, u)
-        factor(2, 1)
-        product(2, 1)
-        add_up(0, 0, 1, lowest, one_tile(z_places[:, 0:QUARTER]))
-        put(0, 0)
 
-        multiply(3, 0, 0, 0)
-        squares(3, 0, 0)
-        copy_h(3, 0, 0)
-        second = moved_tile(1, 0, N_TILES, "second")
-        drive(1, (3, 2), 5)
-        drive(1, (1, 0), 3)
-        add_in_place(1, 0, N_TILES, second)
-        quantise_z(2, "second")
-        for i in (3, 2, 1, 0):
+        multiply(2, 1, 1, 5)
+        squares(2, 1, 1, half(f21, 1))
+        copy_h(2, 1, 1, half(h21, 1))
+        factor(f21, f21, 1)
+        product(2, 1, 0, 2, h21, f21)
+        square30 = work("square30", "top0", UNIT)
+        for u in range(2):
+            squares(3, 0, u, half(square30, u))
+        top = moved_tile(1, 3, 4, "top1")
+        lower = moved_tile(1, 0, 3, "lower1")
+        drive(1, (3,), 0)
+        drive(1, (2, 1), 1)
+        drive(1, (0,), 2)
+        add_in_place(1, 3, 4, top)
+        add_in_place(1, 0, 3, lower)
+        put(1, 3)
+        quantise_z(2, "lower1", "z_s2")
+        for i in (2, 1, 0):
             put(1, i)
-        multiply(3, 0, 1, 5)
-        squares(3, 0, 1)
-        copy_h(3, 0, 1)
-        factor(3, 0)
-        product(3, 0)
-        multiply_both(3, 1, (3, 5))
-        work31 = keep.tile([P, 2 * UNIT], F32, name="work31", tag="work31", align_bytes=64)
-        h_sb[3, 1] = work31[:, 0:UNIT]
-        square[3, 1] = factors[3, 1] = work31[:, UNIT:]
-        for u in range(2):
-            squares(3, 1, u)
-        for u in range(2):
-            copy_h(3, 1, u)
 
-        moved_at[2, 3] = z_places[:, PLACE : PLACE + QUARTER]
+        h30, f30 = unit_inputs("work30", "raw01")
+        for u in range(2):
+            copy_h(3, 0, u, half(h30, u))
+        factor(f30, square30, 0)
+        product(3, 0, 0, 2, h30, f30)
+        multiply_both(3, 1, (1, 2))
+        h31, f31 = unit_inputs("work31", "top1")
+        for u in range(2):
+            squares(3, 1, u, half(f31, u))
+        for u in range(2):
+            copy_h(3, 1, u, half(h31, u))
+        top = moved_in(2, 3, 4, at(6, 7))
         drive(2, (3,), 3)
-        factor(3, 1)
-        add_in_place(2, 3, N_TILES, one_tile(moved_at[2, 3]))
+        factor(f31, f31, 1)
+        add_in_place(2, 3, 4, top)
         put(2, 3)
-        product(3, 1)
-        quantise_z(3, "z0")
+        product(3, 1, 0, 2, h31, f31)
+        quantise_z(3, "z3", "z_s3")
 
-        late = keep.tile([P, 5 * QUARTER], F32, name="late", tag="work31", align_bytes=64)
+        late = work("late", "top1", 5 * QUARTER)
         moved_at[2, 2] = late[:, 0:QUARTER]
         both = {i: late[:, QUARTER * (1 + 2 * i) : QUARTER * (3 + 2 * i)] for i in (1, 0)}
         for i in (1, 0):
@@ -393,7 +409,7 @@ def tile_list_oven_tray_refresh_kernel(tc, tab_words, tab_scales, offs, gT, w1, 
         put_fused(2, 3, 2, moved_at[2, 2])
         drive(2, (1, 0), 3)
         drive(3, (3,), 6)
-        drive(3, (2,), 2)
+        drive(3, (2,), 7)
         drive(3, (1, 0), 4)
         for i in (3, 2):
             put_fused(3, 4, i, moved_at[3, i])

@@ -33,6 +33,7 @@ RUN = 2
 LINE = 4
 RING = 3
 SCALAR_COLS = 48
+VECTOR_PRODUCTS = ((0, 0), (0, 1))
 KB = 256
 
 
@@ -157,20 +158,22 @@ def tile_list_oven_tray_refresh_kernel(tc, tab_words, tab_scales, offs, gT, w1, 
         h_sb, square, factors = {}, {}, {}
 
         def multiply(q, b, u, bank, passes=range(K_PASSES)):
+            if (q, b) in VECTOR_PRODUCTS:
+                planes, entries = range(PACK), slice(QUARTER * q + P * u, QUARTER * q + P * (u + 1))
+            else:
+                planes, entries = range(2 * u, 2 * u + 2), slice(QUARTER * q, QUARTER * (q + 1))
             if 0 in passes:
-                h_banks[q, b, u] = psum.tile([P, PACK, P], F32, name="h_bank", tag="bank%d" % bank)
-            h_bank = h_banks[q, b, u]
-            entries = slice(QUARTER * q + P * u, QUARTER * q + P * (u + 1))
+                h_banks[q, b, u] = psum.tile([P, len(planes), BANK // len(planes)], F32, name="h_bank", tag="bank%d" % bank)
             for a in passes:
-                for t in range(PACK):
+                for e, t in enumerate(planes):
                     nc.tensor.matmul_mx(
-                        out=h_bank[:, t, :],
+                        out=h_banks[q, b, u][:, e, :],
                         lhsT=w1_w[a, b][:, P * t : P * (t + 1)].bitcast(FP8X4),
                         lhsT_scale=w1_s[a, b][:, P * t : P * (t + 1)],
                         rhs=v_w[a][:, entries].bitcast(FP8X4),
                         rhs_scale=v_s[4 * a : P, entries],
-                        start=(a == 0 and t == 0),
-                        stop=(a == K_PASSES - 1 and t == PACK - 1),
+                        start=(a == 0 and e == 0),
+                        stop=(a == K_PASSES - 1 and e == len(planes) - 1),
                     )
 
         def multiply_both(q, b, banks, passes=range(K_PASSES)):
@@ -184,10 +187,10 @@ def tile_list_oven_tray_refresh_kernel(tc, tab_words, tab_scales, offs, gT, w1, 
             return ap[:, BANK * u : BANK * (u + 1)]
 
         def squares(q, b, u, dst):
-            nc.scalar.activation(by_line(dst), h_lines(q, b, u), ACT.Square)
+            nc.scalar.activation(by_line(dst)[:, :, 2 * u : 2 * u + 2], h_lines(q, b, u), ACT.Square)
 
         def copy_h(q, b, u, dst):
-            nc.scalar.copy(by_line(dst), h_lines(q, b, u))
+            nc.scalar.copy(by_line(dst)[:, :, 2 * u : 2 * u + 2], h_lines(q, b, u))
 
         def scale_planes(dst, src, b, planes=range(PACK)):
             for t in planes:
@@ -214,10 +217,13 @@ def tile_list_oven_tray_refresh_kernel(tc, tab_words, tab_scales, offs, gT, w1, 
                 ALU.mult,
             )
 
-        def quantise_z(q, slot, scale_slot):
-            z_w[q] = keep.tile([P, R_PASSES * QUARTER], U32, name="z_w%d" % q, tag=slot, align_bytes=64)
-            z_s[q] = keep.tile([P, R_PASSES * QUARTER], U8, name="z_s%d" % q, tag=scale_slot, align_bytes=64)
-            nc.vector.quantize_mx(out=z_w[q][:].bitcast(FP8X4), scales=z_s[q][:], in_=z_bf[q])
+        def quantise_z(q, slot, scale_slot, halves=range(R_PASSES)):
+            if q not in z_w:
+                z_w[q] = keep.tile([P, R_PASSES * QUARTER], U32, name="z_w%d" % q, tag=slot, align_bytes=64)
+                z_s[q] = keep.tile([P, R_PASSES * QUARTER], U8, name="z_s%d" % q, tag=scale_slot, align_bytes=64)
+            lo, hi = min(z_order[q][b] for b in halves), max(z_order[q][b] for b in halves) + 1
+            cols = slice(QUARTER * lo, QUARTER * hi)
+            nc.vector.quantize_mx(out=z_w[q][:, cols].bitcast(FP8X4), scales=z_s[q][:, cols], in_=z_bf[q][:, UNIT * lo : UNIT * hi])
 
         moved_at = {}
         new_at = {}
@@ -227,18 +233,17 @@ def tile_list_oven_tray_refresh_kernel(tc, tab_words, tab_scales, offs, gT, w1, 
             y_bank = psum.tile([P, len(tiles), QUARTER], F32, name="y_bank", tag="bank%d" % bank)
             for e, i in enumerate(tiles):
                 y_banks[q, i] = y_bank[:, e, :]
-                for c in range(0, QUARTER, P):
-                    for b in range(R_PASSES):
-                        z_cols = slice(QUARTER * z_order[q][b] + c, QUARTER * z_order[q][b] + c + P)
-                        nc.tensor.matmul_mx(
-                            out=y_bank[:, e, c : c + P],
-                            lhsT=w4_w[:, b, 2 * P * i : 2 * P * (i + 1)].bitcast(FP4X4),
-                            lhsT_scale=w4_s[:, b, P * i : P * (i + 1)],
-                            rhs=z_w[q][:, z_cols].bitcast(FP8X4),
-                            rhs_scale=z_s[q][:, z_cols],
-                            start=(b == 0),
-                            stop=(b == R_PASSES - 1),
-                        )
+                for b in range(R_PASSES):
+                    z_cols = slice(QUARTER * z_order[q][b], QUARTER * (z_order[q][b] + 1))
+                    nc.tensor.matmul_mx(
+                        out=y_bank[:, e, :],
+                        lhsT=w4_w[:, b, 2 * P * i : 2 * P * (i + 1)].bitcast(FP4X4),
+                        lhsT_scale=w4_s[:, b, P * i : P * (i + 1)],
+                        rhs=z_w[q][:, z_cols].bitcast(FP8X4),
+                        rhs_scale=z_s[q][:, z_cols],
+                        start=(b == 0),
+                        stop=(b == R_PASSES - 1),
+                    )
             for i in tiles:
                 nc.scalar.activation(moved_at[q, i], y_banks[q, i], ACT.Copy, scale=step_sb[:, i : i + 1])
 
@@ -292,9 +297,9 @@ def tile_list_oven_tray_refresh_kernel(tc, tab_words, tab_scales, offs, gT, w1, 
 
         def whole_unit(q, b, h, f):
             for u in range(2):
-                squares(q, b, u, half(f, u))
+                squares(q, b, u, f)
             for u in range(2):
-                copy_h(q, b, u, half(h, u))
+                copy_h(q, b, u, h)
             factor(f, f, b)
             product(q, b, 0, 2, h, f)
 
@@ -312,6 +317,7 @@ def tile_list_oven_tray_refresh_kernel(tc, tab_words, tab_scales, offs, gT, w1, 
         for u in range(2):
             vector_product(0, 0, u, half(first, u))
         quantise_w1(1, 1)
+        quantise_z(0, "z_w0", "z_s0", (0,))
         quantise_w1(2, 1)
         pick(3, 0, QUARTERS)
         pick(2, 0, QUARTERS)
@@ -324,28 +330,28 @@ def tile_list_oven_tray_refresh_kernel(tc, tab_words, tab_scales, offs, gT, w1, 
             multiply(0, 1, u, u, (2,))
         multiply_both(1, 1, (2, 3), (2,))
         work11 = work("work11", "raw20", 2 * UNIT)
-        f11, h11, square01 = work11[:, 0:UNIT], work11[:, UNIT:], work11[:, 3 * KB : 7 * KB]
+        f11, h11, square01 = work11[:, 0:UNIT], work11[:, UNIT:], work11[:, UNIT:]
         spread = picks[:, S - QUARTER : S + 5 * QUARTER].rearrange("p (u x) -> p u x", u=2)[:, :, 0:BANK]
         for u in (1, 0):
             plane_squares(0, 1, u, half(square01, u))
-        squares(1, 1, 0, half(f11, 0))
+        squares(1, 1, 0, f11)
         scale_planes(spread.rearrange("p u (t j) -> p t u j", t=PACK), square01.rearrange("p (u t j) -> p t u j", u=2, t=PACK), 1)
         for u in (1, 0):
             vector_product(0, 1, u, spread[:, u])
         pick(1, 3, QUARTERS)
-        quantise_z(0, "z_w0", "z_s0")
+        quantise_z(0, "z_w0", "z_s0", (1,))
         pick(1, 0, 3)
         pick(0, 0, QUARTERS)
 
-        squares(1, 1, 1, half(f11, 1))
+        squares(1, 1, 1, f11)
         for u in range(2):
-            copy_h(1, 1, u, half(h11, u))
+            copy_h(1, 1, u, h11)
         factor(f11, f11, 1)
         product(1, 1, 0, 2, h11, f11)
         multiply(2, 1, 0, 2)
         h21, f21 = unit_inputs("work21", "raw01")
-        squares(2, 1, 0, half(f21, 0))
-        copy_h(2, 1, 0, half(h21, 0))
+        squares(2, 1, 0, f21)
+        copy_h(2, 1, 0, h21)
         top = moved_tile(0, 3, 4, "top0")
         middle = moved_tile(0, 1, 3, "middle0")
         lowest = moved_tile(0, 0, 1, "lowest0")
@@ -361,13 +367,13 @@ def tile_list_oven_tray_refresh_kernel(tc, tab_words, tab_scales, offs, gT, w1, 
             put(0, i)
 
         multiply(2, 1, 1, 5)
-        squares(2, 1, 1, half(f21, 1))
-        copy_h(2, 1, 1, half(h21, 1))
+        squares(2, 1, 1, f21)
+        copy_h(2, 1, 1, h21)
         factor(f21, f21, 1)
         product(2, 1, 0, 2, h21, f21)
         square30 = work("square30", "top0", UNIT)
         for u in range(2):
-            squares(3, 0, u, half(square30, u))
+            squares(3, 0, u, square30)
         top = moved_tile(1, 3, 4, "top1")
         lower = moved_tile(1, 0, 3, "lower1")
         drive(1, (3,), 0)
@@ -382,15 +388,15 @@ def tile_list_oven_tray_refresh_kernel(tc, tab_words, tab_scales, offs, gT, w1, 
 
         h30, f30 = unit_inputs("work30", "raw01")
         for u in range(2):
-            copy_h(3, 0, u, half(h30, u))
+            copy_h(3, 0, u, h30)
         factor(f30, square30, 0)
         product(3, 0, 0, 2, h30, f30)
         multiply_both(3, 1, (1, 2))
         h31, f31 = unit_inputs("work31", "top1")
         for u in range(2):
-            squares(3, 1, u, half(f31, u))
+            squares(3, 1, u, f31)
         for u in range(2):
-            copy_h(3, 1, u, half(h31, u))
+            copy_h(3, 1, u, h31)
         top = moved_in(2, 3, 4, at(6, 7))
         drive(2, (3,), 3)
         factor(f31, f31, 1)

@@ -125,10 +125,15 @@ def tile_list_oven_tray_refresh_kernel(tc, tab_words, tab_scales, offs, gT, w1, 
             return by_tile[:, tile_lo:tile_hi, QUARTER * lo : QUARTER * hi]
 
         def gather_words(a, lo, hi):
-            nc.vector.tensor_copy(v_w[a][:, QUARTER * lo : QUARTER * hi], tab_w[a][:].indirect(listed(lo, hi)))
+            nc.vector.tensor_copy(v_w[a][:, lo:hi], tab_w[a][:].indirect(offsets[:, lo // 16 : hi // 16]))
 
         def pick(i, lo, hi):
             nc.vector.tensor_copy(picked(i, i + 1, lo, hi)[:, 0], state[i][:].indirect(listed(lo, hi)))
+
+        rounded = {}
+
+        def quantise_rounded(a):
+            nc.vector.quantize_mx(out=w1_w[a, 1][:].bitcast(FP8X4), scales=w1_s[a, 1][:], in_=rounded[a])
 
         def quantise_w1(a, b):
             w1_w[a, b] = keep.tile([P, PASS], U32, name="w1_w%d%d" % (a, b), align_bytes=64)
@@ -143,6 +148,10 @@ def tile_list_oven_tray_refresh_kernel(tc, tab_words, tab_scales, offs, gT, w1, 
                 else:
                     nc.scalar.activation(dst, src, ACT.Copy)
                 nc.vector.quantize_mx(out=w1_w[a, b][:].bitcast(FP8X4), scales=w1_s[a, b][:], in_=w1_bf)
+                return
+            if a == 1:
+                rounded[a] = at(0, 4).bitcast(BF16)
+                nc.vector.tensor_copy(rounded[a].rearrange("p (t m j) -> p m j t", t=PACK, j=PACK), src)
                 return
             pairs = [at(rounded_at[a][e], rounded_at[a][e] + 2).bitcast(BF16) for e in range(2)]
             for e in range(2):
@@ -271,7 +280,7 @@ def tile_list_oven_tray_refresh_kernel(tc, tab_words, tab_scales, offs, gT, w1, 
             nc.vector.tensor_copy(state[i][:].indirect(listed(q, q + 1)), new_at.get((q, i), picked(i, i + 1, q, q + 1)[:, 0]))
 
         def put_fused(lo, hi, i, moved):
-            nc.vector.tensor_tensor(state[i][:].indirect(listed(lo, hi)), picked(i, i + 1, lo, hi)[:, 0], moved, ALU.add)
+            nc.vector.tensor_tensor(state[i][:].indirect(offsets[:, lo // 16 : hi // 16]), picks[:, S * i + lo : S * i + hi], moved, ALU.add)
 
         def store(i):
             nc.sync.dma_start(out[P * i : P * (i + 1), :], state[i][:])
@@ -283,14 +292,15 @@ def tile_list_oven_tray_refresh_kernel(tc, tab_words, tab_scales, offs, gT, w1, 
             both_inputs = work(name, slot, UNIT)
             return half(both_inputs, 0), half(both_inputs, 1)
 
-        gather_words(0, 0, QUARTERS)
+        gather_words(0, 0, S)
         nc.vector.tensor_copy(v_s[:], tab_s[:].indirect(offsets[:]))
         quantise_w1(0, 0)
-        gather_words(1, 0, QUARTERS)
+        gather_words(1, 0, S)
         quantise_w1(1, 0)
         quantise_w1(2, 0)
-        gather_words(2, 0, 1)
-        gather_words(2, 1, QUARTERS)
+        gather_words(2, 0, P)
+        gather_words(2, P, QUARTER)
+        gather_words(2, QUARTER, S)
         for a in range(K_PASSES):
             for q in range(QUARTERS):
                 multiply_both(q, 0, (2 * q, 2 * q + 1), (a,))
@@ -307,7 +317,7 @@ def tile_list_oven_tray_refresh_kernel(tc, tab_words, tab_scales, offs, gT, w1, 
             both_inputs = work(name, slot, 2 * UNIT)
             return both_inputs[:, 0:UNIT], both_inputs[:, UNIT:]
 
-        first = at(0, 4)
+        first = at(2, 6)
         for u in range(2):
             plane_squares(0, 0, u, half(first, u))
         for u in range(2):
@@ -318,6 +328,7 @@ def tile_list_oven_tray_refresh_kernel(tc, tab_words, tab_scales, offs, gT, w1, 
             vector_product(0, 0, u, half(first, u))
         quantise_w1(1, 1)
         quantise_z(0, "z_w0", "z_s0", (0,))
+        quantise_rounded(1)
         quantise_w1(2, 1)
         pick(3, 0, QUARTERS)
         pick(2, 0, QUARTERS)
@@ -412,14 +423,16 @@ def tile_list_oven_tray_refresh_kernel(tc, tab_words, tab_scales, offs, gT, w1, 
             moved_at[2, i], moved_at[3, i] = both[i][:, 0:QUARTER], both[i][:, QUARTER:]
         moved_tile(3, 2, N_TILES, "last")
         drive(2, (2,), 5)
-        put_fused(2, 3, 2, moved_at[2, 2])
+        put_fused(2 * QUARTER, 3 * QUARTER, 2, moved_at[2, 2])
         drive(2, (1, 0), 3)
+        put_fused(2 * QUARTER, 2 * QUARTER + P, 1, both[1][:, 0:P])
         drive(3, (3,), 6)
         drive(3, (2,), 7)
         drive(3, (1, 0), 4)
         for i in (3, 2):
-            put_fused(3, 4, i, moved_at[3, i])
+            put_fused(3 * QUARTER, S, i, moved_at[3, i])
             store(i)
-        for i in (1, 0):
-            put_fused(2, 4, i, both[i])
-            store(i)
+        put_fused(2 * QUARTER + P, S, 1, both[1][:, P:])
+        store(1)
+        put_fused(2 * QUARTER, S, 0, both[0])
+        store(0)

@@ -35,6 +35,7 @@ RING = 3
 SCALAR_COLS = 48
 VECTOR_PRODUCTS = ((0, 0), (0, 1))
 KB = 256
+POOL_COLS = 32
 
 
 def tile_list_oven_tray_refresh_kernel(tc, tab_words, tab_scales, offs, gT, w1, cub, w4_words, w4_scales, step, out):
@@ -106,15 +107,16 @@ def tile_list_oven_tray_refresh_kernel(tc, tab_words, tab_scales, offs, gT, w1, 
         v_w = [keep.tile([P, S], U32, name="v_w%d" % a, align_bytes=64) for a in range(K_PASSES)]
         v_s = keep.tile([P, S], U8, name="v_s", align_bytes=64)
 
-        arena = keep.tile([P, 14 * KB], F32, name="arena", align_bytes=64)
+        arena = keep.tile([P, 23 * KB], F32, name="arena", align_bytes=64)
 
         def at(lo, hi):
             return arena[:, KB * lo : KB * hi]
 
-        z_start = {0: 7, 1: 5, 2: 3, 3: 3}
+        z_start = {1: 14, 2: 12, 3: 12}
         z_order = {0: (1, 0), 1: (0, 1), 2: (0, 1), 3: (0, 1)}
-        z_bf = {q: at(z_start[q], z_start[q] + 4).bitcast(BF16) for q in range(QUARTERS)}
-        rounded_at = {0: (8, 10), 1: (0, 2), 2: (12, 4)}
+        z_bf = {q: at(z_start[q], z_start[q] + 4).bitcast(BF16) for q in z_start}
+        z_first = (at(1, 3).bitcast(BF16), at(16, 18).bitcast(BF16))
+        rounded_at = {0: (2, 0), 2: (21, 13)}
         w1_w, w1_s, z_w, z_s = {}, {}, {}, {}
 
         def listed(lo, hi):
@@ -150,8 +152,12 @@ def tile_list_oven_tray_refresh_kernel(tc, tab_words, tab_scales, offs, gT, w1, 
                 nc.vector.quantize_mx(out=w1_w[a, b][:].bitcast(FP8X4), scales=w1_s[a, b][:], in_=w1_bf)
                 return
             if a == 1:
-                rounded[a] = at(0, 4).bitcast(BF16)
-                nc.vector.tensor_copy(rounded[a].rearrange("p (t m j) -> p m j t", t=PACK, j=PACK), src)
+                rounded[a] = arena[:, 15 * KB // 4 : 31 * KB // 4].bitcast(BF16)
+                dst = rounded[a].rearrange("p (t m j) -> p m j t", t=PACK, j=PACK)
+                nc.gpsimd.tensor_scalar(
+                    dst[:, 0:POOL_COLS].rearrange("p m j t -> p t m j"), src[:, 0:POOL_COLS].rearrange("p m j t -> p t m j"), 1.0, 0.0, ALU.mult, ALU.add
+                )
+                nc.vector.tensor_copy(dst[:, POOL_COLS:P], src[:, POOL_COLS:P])
                 return
             pairs = [at(rounded_at[a][e], rounded_at[a][e] + 2).bitcast(BF16) for e in range(2)]
             for e in range(2):
@@ -209,6 +215,8 @@ def tile_list_oven_tray_refresh_kernel(tc, tab_words, tab_scales, offs, gT, w1, 
             scale_planes(by_line(dst).rearrange("p c t i -> p t c i"), by_line(src).rearrange("p c t i -> p t c i"), b)
 
         def z_part(q, b, lo, hi):
+            if q == 0:
+                return z_first[b][:, BANK * lo : BANK * hi]
             start = UNIT * z_order[q][b]
             return z_bf[q][:, start + BANK * lo : start + BANK * hi]
 
@@ -232,7 +240,7 @@ def tile_list_oven_tray_refresh_kernel(tc, tab_words, tab_scales, offs, gT, w1, 
                 z_s[q] = keep.tile([P, R_PASSES * QUARTER], U8, name="z_s%d" % q, tag=scale_slot, align_bytes=64)
             lo, hi = min(z_order[q][b] for b in halves), max(z_order[q][b] for b in halves) + 1
             cols = slice(QUARTER * lo, QUARTER * hi)
-            nc.vector.quantize_mx(out=z_w[q][:, cols].bitcast(FP8X4), scales=z_s[q][:, cols], in_=z_bf[q][:, UNIT * lo : UNIT * hi])
+            nc.vector.quantize_mx(out=z_w[q][:, cols].bitcast(FP8X4), scales=z_s[q][:, cols], in_=z_first[halves[0]] if q == 0 else z_bf[q])
 
         moved_at = {}
         new_at = {}
@@ -298,12 +306,13 @@ def tile_list_oven_tray_refresh_kernel(tc, tab_words, tab_scales, offs, gT, w1, 
         gather_words(1, 0, S)
         quantise_w1(1, 0)
         quantise_w1(2, 0)
-        gather_words(2, 0, P)
         gather_words(2, P, QUARTER)
+        gather_words(2, 0, P)
         gather_words(2, QUARTER, S)
         for a in range(K_PASSES):
             for q in range(QUARTERS):
-                multiply_both(q, 0, (2 * q, 2 * q + 1), (a,))
+                for u in (1, 0):
+                    multiply(q, 0, u, 2 * q + u, (a,))
 
         def whole_unit(q, b, h, f):
             for u in range(2):
@@ -317,15 +326,15 @@ def tile_list_oven_tray_refresh_kernel(tc, tab_words, tab_scales, offs, gT, w1, 
             both_inputs = work(name, slot, 2 * UNIT)
             return both_inputs[:, 0:UNIT], both_inputs[:, UNIT:]
 
-        first = at(2, 6)
-        for u in range(2):
-            plane_squares(0, 0, u, half(first, u))
-        for u in range(2):
-            planes = half(first, u).rearrange("p (t j) -> p t j", t=PACK)
+        first = (arena[:, 37 * KB // 4 : 45 * KB // 4], arena[:, 29 * KB // 4 : 37 * KB // 4])
+        for u in (1, 0):
+            plane_squares(0, 0, u, first[u])
+        for u in (1, 0):
+            planes = first[u].rearrange("p (t j) -> p t j", t=PACK)
             scale_planes(planes, planes, 0)
         quantise_w1(0, 1)
-        for u in range(2):
-            vector_product(0, 0, u, half(first, u))
+        for u in (1, 0):
+            vector_product(0, 0, u, first[u])
         quantise_w1(1, 1)
         quantise_z(0, "z_w0", "z_s0", (0,))
         quantise_rounded(1)
@@ -373,7 +382,7 @@ def tile_list_oven_tray_refresh_kernel(tc, tab_words, tab_scales, offs, gT, w1, 
         add_in_place(0, 1, 3, middle)
         put(0, 3)
         quantise_z(1, "middle0", "z_s1")
-        add_into(0, 0, 1, lowest, at(8, 9))
+        add_into(0, 0, 1, lowest, at(17, 18))
         for i in (2, 1, 0):
             put(0, i)
 

@@ -34,6 +34,7 @@ LINE = 4
 RING = 3
 SCALAR_COLS = 48
 VECTOR_PRODUCTS = ((0, 0), (0, 1))
+ALIGN = 256
 KB = 256
 POOL_COLS = 32
 
@@ -46,16 +47,16 @@ def tile_list_oven_tray_refresh_kernel(tc, tab_words, tab_scales, offs, gT, w1, 
         psum = ctx.enter_context(tc.psum_pool(name="psum", bufs=1))
 
         offsets = keep.tile([P, S // 16], U16, name="offsets")
-        tab_s = keep.tile([P, T], U8, name="tab_s", align_bytes=64)
+        tab_s = keep.tile([P, T], U8, name="tab_s", align_bytes=ALIGN)
         nc.gpsimd.memset(tab_s[:].bitcast(I32), 0)
-        w4_s = keep.tile([P, R_PASSES, N], U8, name="w4_s", align_bytes=64)
+        w4_s = keep.tile([P, R_PASSES, N], U8, name="w4_s", align_bytes=ALIGN)
         nc.vector.memset(w4_s[:].rearrange("p b n -> p (b n)").bitcast(I32), 0)
         cub_sb = [keep.tile([P, PACK], F32, name="cub_sb%d" % b) for b in range(R_PASSES)]
         step_sb = keep.tile([P, N_TILES], F32, name="step_sb")
-        tab_w = [keep.tile([P, T], U32, name="tab_w%d" % a, align_bytes=64) for a in range(K_PASSES)]
-        state = [keep.tile([P, T], F32, name="state%d" % i, align_bytes=64) for i in range(N_TILES)]
-        w4_w = keep.tile([P, R_PASSES, 2 * N], U8, name="w4_w", align_bytes=64)
-        picks = keep.tile([P, 3 * S + PACK * PASS], F32, name="picks", align_bytes=64)
+        tab_w = [keep.tile([P, T], U32, name="tab_w%d" % a, align_bytes=ALIGN) for a in range(K_PASSES)]
+        state = [keep.tile([P, T], F32, name="state%d" % i, align_bytes=ALIGN) for i in range(N_TILES)]
+        w4_w = keep.tile([P, R_PASSES, 2 * N], U8, name="w4_w", align_bytes=ALIGN)
+        picks = keep.tile([P, 3 * S + PACK * PASS], F32, name="picks", align_bytes=ALIGN)
         w1_raw = {}
 
         def load_table(a):
@@ -65,7 +66,7 @@ def tile_list_oven_tray_refresh_kernel(tc, tab_words, tab_scales, offs, gT, w1, 
             if (a, b) == (K_PASSES - 1, R_PASSES - 1):
                 w1_raw[a, b] = picks[:, 3 * S : 3 * S + PACK * PASS].rearrange("p (j c) -> p j c", j=PACK)
             else:
-                w1_raw[a, b] = keep.tile([P, PACK, PASS], F32, name="w1_raw%d%d" % (a, b), tag="raw%d%d" % (a, b), align_bytes=64)[:]
+                w1_raw[a, b] = keep.tile([P, PACK, PASS], F32, name="w1_raw%d%d" % (a, b), tag="raw%d%d" % (a, b), align_bytes=ALIGN)[:]
             rows = w1[PASS * a : PASS * (a + 1), PASS * b : PASS * (b + 1)]
             nc.sync.dma_start(w1_raw[a, b], rows.rearrange("(p j) c -> p j c", j=PACK))
 
@@ -104,10 +105,10 @@ def tile_list_oven_tray_refresh_kernel(tc, tab_words, tab_scales, offs, gT, w1, 
         with nc.allow_non_contiguous_dma(reason="one step value a partition"):
             nc.sync.dma_start(step_sb[:], step.rearrange("(i p) -> p i", p=P))
 
-        v_w = [keep.tile([P, S], U32, name="v_w%d" % a, align_bytes=64) for a in range(K_PASSES)]
-        v_s = keep.tile([P, S], U8, name="v_s", align_bytes=64)
+        v_w = [keep.tile([P, S], U32, name="v_w%d" % a, align_bytes=ALIGN) for a in range(K_PASSES)]
+        v_s = keep.tile([P, S], U8, name="v_s", align_bytes=ALIGN)
 
-        arena = keep.tile([P, 23 * KB], F32, name="arena", align_bytes=64)
+        arena = keep.tile([P, 23 * KB], F32, name="arena", align_bytes=ALIGN)
 
         def at(lo, hi):
             return arena[:, KB * lo : KB * hi]
@@ -138,11 +139,11 @@ def tile_list_oven_tray_refresh_kernel(tc, tab_words, tab_scales, offs, gT, w1, 
             nc.vector.quantize_mx(out=w1_w[a, 1][:].bitcast(FP8X4), scales=w1_s[a, 1][:], in_=rounded[a])
 
         def quantise_w1(a, b):
-            w1_w[a, b] = keep.tile([P, PASS], U32, name="w1_w%d%d" % (a, b), align_bytes=64)
-            w1_s[a, b] = keep.tile([P, PASS], U8, name="w1_s%d%d" % (a, b), align_bytes=64)
+            w1_w[a, b] = keep.tile([P, PASS], U32, name="w1_w%d%d" % (a, b), align_bytes=ALIGN)
+            w1_s[a, b] = keep.tile([P, PASS], U8, name="w1_s%d%d" % (a, b), align_bytes=ALIGN)
             src = w1_raw[a, b].rearrange("p j (m t) -> p m j t", t=PACK)
             if b == 0:
-                w1_bf = ring.tile([P, PACK * PASS], BF16, name="w1_bf", tag="w1_bf", align_bytes=64)[:]
+                w1_bf = ring.tile([P, PACK * PASS], BF16, name="w1_bf", tag="w1_bf", align_bytes=ALIGN)[:]
                 dst = w1_bf.rearrange("p (t m j) -> p m j t", t=PACK, j=PACK)
                 if a > 0:
                     nc.scalar.activation(dst[:, 0:SCALAR_COLS], src[:, 0:SCALAR_COLS], ACT.Copy)
@@ -236,8 +237,8 @@ def tile_list_oven_tray_refresh_kernel(tc, tab_words, tab_scales, offs, gT, w1, 
 
         def quantise_z(q, slot, scale_slot, halves=range(R_PASSES)):
             if q not in z_w:
-                z_w[q] = keep.tile([P, R_PASSES * QUARTER], U32, name="z_w%d" % q, tag=slot, align_bytes=64)
-                z_s[q] = keep.tile([P, R_PASSES * QUARTER], U8, name="z_s%d" % q, tag=scale_slot, align_bytes=64)
+                z_w[q] = keep.tile([P, R_PASSES * QUARTER], U32, name="z_w%d" % q, tag=slot, align_bytes=ALIGN)
+                z_s[q] = keep.tile([P, R_PASSES * QUARTER], U8, name="z_s%d" % q, tag=scale_slot, align_bytes=ALIGN)
             lo, hi = min(z_order[q][b] for b in halves), max(z_order[q][b] for b in halves) + 1
             cols = slice(QUARTER * lo, QUARTER * hi)
             nc.vector.quantize_mx(out=z_w[q][:, cols].bitcast(FP8X4), scales=z_s[q][:, cols], in_=z_first[halves[0]] if q == 0 else z_bf[q])
@@ -271,7 +272,7 @@ def tile_list_oven_tray_refresh_kernel(tc, tab_words, tab_scales, offs, gT, w1, 
             return rows
 
         def moved_tile(q, tile_lo, tile_hi, slot):
-            tile = keep.tile([P, (tile_hi - tile_lo) * QUARTER], F32, name="moved%d%d" % (q, tile_lo), tag=slot, align_bytes=64)
+            tile = keep.tile([P, (tile_hi - tile_lo) * QUARTER], F32, name="moved%d%d" % (q, tile_lo), tag=slot, align_bytes=ALIGN)
             return moved_in(q, tile_lo, tile_hi, tile[:])
 
         def add_in_place(q, tile_lo, tile_hi, moved):
@@ -294,7 +295,7 @@ def tile_list_oven_tray_refresh_kernel(tc, tab_words, tab_scales, offs, gT, w1, 
             nc.sync.dma_start(out[P * i : P * (i + 1), :], state[i][:])
 
         def work(name, slot, width):
-            return keep.tile([P, width], F32, name=name, tag=slot, align_bytes=64)[:]
+            return keep.tile([P, width], F32, name=name, tag=slot, align_bytes=ALIGN)[:]
 
         def pair(name, slot):
             both_inputs = work(name, slot, UNIT)

@@ -32,7 +32,7 @@ PLACE = UNIT // 2
 RUN = 2
 LINE = 4
 RING = 3
-SCALAR_COLS = 48
+SCALAR_COLS = {1: 72, 2: 48}
 VECTOR_PRODUCTS = ((0, 0), (0, 1))
 ALIGN = 256
 KB = 256
@@ -47,8 +47,8 @@ def tile_list_oven_tray_refresh_kernel(tc, tab_words, tab_scales, offs, gT, w1, 
         psum = ctx.enter_context(tc.psum_pool(name="psum", bufs=1))
 
         offsets = keep.tile([P, S // 16], U16, name="offsets")
-        tab_s = keep.tile([P, T], U8, name="tab_s", align_bytes=ALIGN)
-        nc.gpsimd.memset(tab_s[:].bitcast(I32), 0)
+        tab_s = keep.tile([P, 2, T], U8, name="tab_s", align_bytes=ALIGN)
+        nc.gpsimd.memset(tab_s[:].rearrange("p e t -> p (e t)").bitcast(I32), 0)
         w4_s = keep.tile([P, R_PASSES, N], U8, name="w4_s", align_bytes=ALIGN)
         nc.vector.memset(w4_s[:].rearrange("p b n -> p (b n)").bitcast(I32), 0)
         cub_sb = [keep.tile([P, PACK], F32, name="cub_sb%d" % b) for b in range(R_PASSES)]
@@ -79,9 +79,9 @@ def tile_list_oven_tray_refresh_kernel(tc, tab_words, tab_scales, offs, gT, w1, 
         load_table(0)
         nc.sync.dma_start(offsets[:], offs)
         load_w1(0, 0)
-        for Q in range(P // QUADRANT):
+        for Q in (2, 3, 0, 1):
             nc.sync.dma_start(
-                tab_s[QUADRANT * Q : QUADRANT * Q + 4 * K_PASSES, :].bitcast(I32),
+                tab_s[QUADRANT * (Q % 2) : QUADRANT * (Q % 2) + 4 * K_PASSES, Q // 2, :].bitcast(I32),
                 tab_scales[:, 4 * Q : 4 * Q + 4, :].bitcast(I32),
             )
         load_table(1)
@@ -146,8 +146,8 @@ def tile_list_oven_tray_refresh_kernel(tc, tab_words, tab_scales, offs, gT, w1, 
                 w1_bf = ring.tile([P, PACK * PASS], BF16, name="w1_bf", tag="w1_bf", align_bytes=ALIGN)[:]
                 dst = w1_bf.rearrange("p (t m j) -> p m j t", t=PACK, j=PACK)
                 if a > 0:
-                    nc.scalar.activation(dst[:, 0:SCALAR_COLS], src[:, 0:SCALAR_COLS], ACT.Copy)
-                    nc.vector.tensor_copy(dst[:, SCALAR_COLS:P], src[:, SCALAR_COLS:P])
+                    nc.scalar.activation(dst[:, 0 : SCALAR_COLS[a]], src[:, 0 : SCALAR_COLS[a]], ACT.Copy)
+                    nc.vector.tensor_copy(dst[:, SCALAR_COLS[a] : P], src[:, SCALAR_COLS[a] : P])
                 else:
                     nc.scalar.activation(dst, src, ACT.Copy)
                 nc.vector.quantize_mx(out=w1_w[a, b][:].bitcast(FP8X4), scales=w1_s[a, b][:], in_=w1_bf)
@@ -302,7 +302,8 @@ def tile_list_oven_tray_refresh_kernel(tc, tab_words, tab_scales, offs, gT, w1, 
             return half(both_inputs, 0), half(both_inputs, 1)
 
         gather_words(0, 0, S)
-        nc.vector.tensor_copy(v_s[:], tab_s[:].indirect(offsets[:]))
+        nc.vector.tensor_copy(tab_s[P // 2 : P, 0, :].bitcast(I32), tab_s[0 : P // 2, 1, :].bitcast(I32))
+        nc.vector.tensor_copy(v_s[:], tab_s[:, 0, :].indirect(offsets[:]))
         quantise_w1(0, 0)
         gather_words(1, 0, S)
         quantise_w1(1, 0)

from contextlib import ExitStack

import concourse.mybir as mybir

K, H, N, T, S = 1536, 1024, 512, 2048, 1024
FLOPS = 2 * K * H * S + 2 * H * N * S

F32 = mybir.dt.float32
BF16 = mybir.dt.bfloat16
I32 = mybir.dt.int32
U32 = mybir.dt.uint32
U16 = mybir.dt.uint16
U8 = mybir.dt.uint8
FP8X4 = mybir.dt.float8_e4m3fn_x4
FP4X4 = mybir.dt.float4_e2m1fn_x4
ACT = mybir.ActivationFunctionType
ALU = mybir.AluOpType

P = 128
PACK = 4
PASS = P * PACK
K_PASSES = K // PASS
R_PASSES = H // PASS
N_TILES = N // P
QUADRANT = 32
QUARTERS = 4
QUARTER = S // QUARTERS
LIST_COLS = QUARTER // 16
UNIT = PACK * QUARTER
BANK = PACK * P
PLACE = UNIT // 2
RUN = 2
LINE = 4
RING = 3
SCALAR_COLS = {1: 72, 2: 48}
VECTOR_PRODUCTS = ((0, 0), (0, 1))
ALIGN = 256
KB = 256
POOL_COLS = 32


def tile_list_oven_tray_refresh_kernel(tc, tab_words, tab_scales, offs, gT, w1, cub, w4_words, w4_scales, step, out):
    nc = tc.nc
    with ExitStack() as ctx:
        keep = ctx.enter_context(tc.tile_pool(name="keep", bufs=1))
        ring = ctx.enter_context(tc.tile_pool(name="ring", bufs=RING))
        psum = ctx.enter_context(tc.psum_pool(name="psum", bufs=1))

        offsets = keep.tile([P, S // 16], U16, name="offsets")
        tab_s = keep.tile([P, 2, T], U8, name="tab_s", align_bytes=ALIGN)
        nc.gpsimd.memset(tab_s[:].rearrange("p e t -> p (e t)").bitcast(I32), 0)
        w4_s = keep.tile([P, R_PASSES, N], U8, name="w4_s", align_bytes=ALIGN)
        nc.vector.memset(w4_s[:].rearrange("p b n -> p (b n)").bitcast(I32), 0)
        cub_sb = [keep.tile([P, PACK], F32, name="cub_sb%d" % b) for b in range(R_PASSES)]
        step_sb = keep.tile([P, N_TILES], F32, name="step_sb")
        tab_w = [keep.tile([P, T], U32, name="tab_w%d" % a, align_bytes=ALIGN) for a in range(K_PASSES)]
        state = [keep.tile([P, T], F32, name="state%d" % i, align_bytes=ALIGN) for i in range(N_TILES)]
        w4_w = keep.tile([P, R_PASSES, 2 * N], U8, name="w4_w", align_bytes=ALIGN)
        picks = keep.tile([P, 3 * S + PACK * PASS], F32, name="picks", align_bytes=ALIGN)
        w1_raw = {}

        def load_table(a):
            nc.sync.dma_start(tab_w[a][:].bitcast(I32), tab_words[a].rearrange("p t i -> p (t i)").bitcast(I32))

        def load_w1(a, b):
            if (a, b) == (K_PASSES - 1, R_PASSES - 1):
                w1_raw[a, b] = picks[:, 3 * S : 3 * S + PACK * PASS].rearrange("p (j c) -> p j c", j=PACK)
            else:
                w1_raw[a, b] = keep.tile([P, PACK, PASS], F32, name="w1_raw%d%d" % (a, b), tag="raw%d%d" % (a, b), align_bytes=ALIGN)[:]
            rows = w1[PASS * a : PASS * (a + 1), PASS * b : PASS * (b + 1)]
            nc.sync.dma_start(w1_raw[a, b], rows.rearrange("(p j) c -> p j c", j=PACK))

        def load_cub(b):
            nc.sync.dma_start(cub_sb[b][:], cub[PASS * b : PASS * (b + 1)].rearrange("(p t) -> p t", t=PACK))

        def load_state(i):
            nc.sync.dma_start(state[i][:], gT[P * i : P * (i + 1), :])

        load_table(0)
        nc.sync.dma_start(offsets[:], offs)
        load_w1(0, 0)
        for Q in (2, 3, 0, 1):
            nc.sync.dma_start(
                tab_s[QUADRANT * (Q % 2) : QUADRANT * (Q % 2) + 4 * K_PASSES, Q // 2, :].bitcast(I32),
                tab_scales[:, 4 * Q : 4 * Q + 4, :].bitcast(I32),
            )
        load_table(1)
        load_w1(1, 0)
        load_w1(2, 0)
        load_table(2)
        load_cub(0)
        for a in range(K_PASSES):
            load_w1(a, 1)
        load_state(3)
        load_state(2)
        load_cub(1)
        load_state(1)
        for Q in range(P // QUADRANT):
            nc.sync.dma_start(
                w4_s[QUADRANT * Q : QUADRANT * Q + 4, :, :].bitcast(I32),
                w4_scales[:, 4 * Q : 4 * Q + 4, :].rearrange("b s n -> s b n").bitcast(I32),
            )
        nc.sync.dma_start(w4_w[:].bitcast(I32), w4_words.rearrange("b p c -> p b c").bitcast(I32))
        load_state(0)
        with nc.allow_non_contiguous_dma(reason="one step value a partition"):
            nc.sync.dma_start(step_sb[:], step.rearrange("(i p) -> p i", p=P))

        v_w = [keep.tile([P, S], U32, name="v_w%d" % a, align_bytes=ALIGN) for a in range(K_PASSES)]
        v_s = keep.tile([P, S], U8, name="v_s", align_bytes=ALIGN)

        arena = keep.tile([P, 23 * KB], F32, name="arena", align_bytes=ALIGN)

        def at(lo, hi):
            return arena[:, KB * lo : KB * hi]

        z_start = {1: 14, 2: 12, 3: 12}
        z_order = {0: (1, 0), 1: (0, 1), 2: (0, 1), 3: (0, 1)}
        z_bf = {q: at(z_start[q], z_start[q] + 4).bitcast(BF16) for q in z_start}
        z_first = (at(1, 3).bitcast(BF16), at(16, 18).bitcast(BF16))
        rounded_at = {0: (2, 0), 2: (21, 13)}
        w1_w, w1_s, z_w, z_s = {}, {}, {}, {}

        def listed(lo, hi):
            return offsets[:, LIST_COLS * lo : LIST_COLS * hi]

        def picked(tile_lo, tile_hi, lo, hi):
            by_tile = picks[:, 0 : N_TILES * S].rearrange("p (i s) -> p i s", i=N_TILES)
            return by_tile[:, tile_lo:tile_hi, QUARTER * lo : QUARTER * hi]

        def gather_words(a, lo, hi):
            nc.vector.tensor_copy(v_w[a][:, lo:hi], tab_w[a][:].indirect(offsets[:, lo // 16 : hi // 16]))

        def pick(i, lo, hi):
            nc.vector.tensor_copy(picked(i, i + 1, lo, hi)[:, 0], state[i][:].indirect(listed(lo, hi)))

        rounded = {}

        def quantise_rounded(a):
            nc.vector.quantize_mx(out=w1_w[a, 1][:].bitcast(FP8X4), scales=w1_s[a, 1][:], in_=rounded[a])

        def quantise_w1(a, b):
            w1_w[a, b] = keep.tile([P, PASS], U32, name="w1_w%d%d" % (a, b), align_bytes=ALIGN)
            w1_s[a, b] = keep.tile([P, PASS], U8, name="w1_s%d%d" % (a, b), align_bytes=ALIGN)
            src = w1_raw[a, b].rearrange("p j (m t) -> p m j t", t=PACK)
            if b == 0:
                w1_bf = ring.tile([P, PACK * PASS], BF16, name="w1_bf", tag="w1_bf", align_bytes=ALIGN)[:]
                dst = w1_bf.rearrange("p (t m j) -> p m j t", t=PACK, j=PACK)
                if a > 0:
                    nc.scalar.activation(dst[:, 0 : SCALAR_COLS[a]], src[:, 0 : SCALAR_COLS[a]], ACT.Copy)
                    nc.vector.tensor_copy(dst[:, SCALAR_COLS[a] : P], src[:, SCALAR_COLS[a] : P])
                else:
                    nc.scalar.activation(dst, src, ACT.Copy)
                nc.vector.quantize_mx(out=w1_w[a, b][:].bitcast(FP8X4), scales=w1_s[a, b][:], in_=w1_bf)
                return
            if a == 1:
                rounded[a] = arena[:, 15 * KB // 4 : 31 * KB // 4].bitcast(BF16)
                dst = rounded[a].rearrange("p (t m j) -> p m j t", t=PACK, j=PACK)
                nc.gpsimd.tensor_scalar(
                    dst[:, 0:POOL_COLS].rearrange("p m j t -> p t m j"), src[:, 0:POOL_COLS].rearrange("p m j t -> p t m j"), 1.0, 0.0, ALU.mult, ALU.add
                )
                nc.vector.tensor_copy(dst[:, POOL_COLS:P], src[:, POOL_COLS:P])
                return
            pairs = [at(rounded_at[a][e], rounded_at[a][e] + 2).bitcast(BF16) for e in range(2)]
            for e in range(2):
                nc.vector.tensor_copy(pairs[e].rearrange("p (t m j) -> p m j t", t=2, j=PACK), src[:, :, :, 2 * e : 2 * e + 2])
            for e in range(2):
                cols = slice(2 * P * e, 2 * P * (e + 1))
                nc.vector.quantize_mx(out=w1_w[a, b][:, cols].bitcast(FP8X4), scales=w1_s[a, b][:, cols], in_=pairs[e])

        def by_line(ap):
            return ap.rearrange("p (c t i) -> p c t i", t=PACK, i=LINE)

        h_banks = {}
        h_sb, square, factors = {}, {}, {}

        def multiply(q, b, u, bank, passes=range(K_PASSES)):
            if (q, b) in VECTOR_PRODUCTS:
                planes, entries = range(PACK), slice(QUARTER * q + P * u, QUARTER * q + P * (u + 1))
            else:
                planes, entries = range(2 * u, 2 * u + 2), slice(QUARTER * q, QUARTER * (q + 1))
            if 0 in passes:
                h_banks[q, b, u] = psum.tile([P, len(planes), BANK // len(planes)], F32, name="h_bank", tag="bank%d" % bank)
            for a in passes:
                for e, t in enumerate(planes):
                    nc.tensor.matmul_mx(
                        out=h_banks[q, b, u][:, e, :],
                        lhsT=w1_w[a, b][:, P * t : P * (t + 1)].bitcast(FP8X4),
                        lhsT_scale=w1_s[a, b][:, P * t : P * (t + 1)],
                        rhs=v_w[a][:, entries].bitcast(FP8X4),
                        rhs_scale=v_s[4 * a : P, entries],
                        start=(a == 0 and e == 0),
                        stop=(a == K_PASSES - 1 and e == len(planes) - 1),
                    )

        def multiply_both(q, b, banks, passes=range(K_PASSES)):
            for u in range(2):
                multiply(q, b, u, banks[u], passes)

        def h_lines(q, b, u):
            return h_banks[q, b, u][:].rearrange("p t (c i) -> p c t i", i=LINE)

        def half(ap, u):
            return ap[:, BANK * u : BANK * (u + 1)]

        def squares(q, b, u, dst):
            nc.scalar.activation(by_line(dst)[:, :, 2 * u : 2 * u + 2], h_lines(q, b, u), ACT.Square)

        def copy_h(q, b, u, dst):
            nc.scalar.copy(by_line(dst)[:, :, 2 * u : 2 * u + 2], h_lines(q, b, u))

        def scale_planes(dst, src, b, planes=range(PACK)):
            for t in planes:
                nc.scalar.activation(dst[:, t], src[:, t], ACT.Copy, bias=1.0, scale=cub_sb[b][:, t : t + 1])

        def factor(dst, src, b):
            scale_planes(by_line(dst).rearrange("p c t i -> p t c i"), by_line(src).rearrange("p c t i -> p t c i"), b)

        def z_part(q, b, lo, hi):
            if q == 0:
                return z_first[b][:, BANK * lo : BANK * hi]
            start = UNIT * z_order[q][b]
            return z_bf[q][:, start + BANK * lo : start + BANK * hi]

        def product(q, b, lo, hi, h, f):
            nc.gpsimd.tensor_tensor(z_part(q, b, lo, hi).rearrange("p (c i t) -> p c t i", i=LINE, t=PACK), by_line(h), by_line(f), ALU.mult)

        def plane_squares(q, b, u, dst):
            nc.scalar.activation(dst.rearrange("p (t j) -> p t j", t=PACK), h_banks[q, b, u][:], ACT.Square)

        def vector_product(q, b, u, f):
            nc.vector.tensor_tensor(
                z_part(q, b, u, u + 1).rearrange("p (c i t) -> p c t i", i=RUN, t=PACK),
                h_banks[q, b, u][:].rearrange("p t (c i) -> p c t i", i=RUN),
                f.rearrange("p (t c i) -> p c t i", t=PACK, i=RUN),
                ALU.mult,
            )

        def quantise_z(q, slot, scale_slot, halves=range(R_PASSES)):
            if q not in z_w:
                z_w[q] = keep.tile([P, R_PASSES * QUARTER], U32, name="z_w%d" % q, tag=slot, align_bytes=ALIGN)
                z_s[q] = keep.tile([P, R_PASSES * QUARTER], U8, name="z_s%d" % q, tag=scale_slot, align_bytes=ALIGN)
            lo, hi = min(z_order[q][b] for b in halves), max(z_order[q][b] for b in halves) + 1
            cols = slice(QUARTER * lo, QUARTER * hi)
            nc.vector.quantize_mx(out=z_w[q][:, cols].bitcast(FP8X4), scales=z_s[q][:, cols], in_=z_first[halves[0]] if q == 0 else z_bf[q])

        moved_at = {}
        new_at = {}
        y_banks = {}

        def drive(q, tiles, bank):
            y_bank = psum.tile([P, len(tiles), QUARTER], F32, name="y_bank", tag="bank%d" % bank)
            for e, i in enumerate(tiles):
                y_banks[q, i] = y_bank[:, e, :]
                for b in range(R_PASSES):
                    z_cols = slice(QUARTER * z_order[q][b], QUARTER * (z_order[q][b] + 1))
                    nc.tensor.matmul_mx(
                        out=y_bank[:, e, :],
                        lhsT=w4_w[:, b, 2 * P * i : 2 * P * (i + 1)].bitcast(FP4X4),
                        lhsT_scale=w4_s[:, b, P * i : P * (i + 1)],
                        rhs=z_w[q][:, z_cols].bitcast(FP8X4),
                        rhs_scale=z_s[q][:, z_cols],
                        start=(b == 0),
                        stop=(b == R_PASSES - 1),
                    )
            for i in tiles:
                nc.scalar.activation(moved_at[q, i], y_banks[q, i], ACT.Copy, scale=step_sb[:, i : i + 1])

        def moved_in(q, tile_lo, tile_hi, ap):
            rows = ap.rearrange("p (i j) -> p i j", j=QUARTER)
            for i in range(tile_lo, tile_hi):
                moved_at[q, i] = rows[:, i - tile_lo]
            return rows

        def moved_tile(q, tile_lo, tile_hi, slot):
            tile = keep.tile([P, (tile_hi - tile_lo) * QUARTER], F32, name="moved%d%d" % (q, tile_lo), tag=slot, align_bytes=ALIGN)
            return moved_in(q, tile_lo, tile_hi, tile[:])

        def add_in_place(q, tile_lo, tile_hi, moved):
            new = picked(tile_lo, tile_hi, q, q + 1)
            nc.gpsimd.tensor_tensor(new, new, moved, ALU.add)

        def add_into(q, tile_lo, tile_hi, moved, ap):
            new = ap.rearrange("p (i j) -> p i j", j=QUARTER)
            for i in range(tile_lo, tile_hi):
                new_at[q, i] = new[:, i - tile_lo]
            nc.gpsimd.tensor_tensor(new, picked(tile_lo, tile_hi, q, q + 1), moved, ALU.add)

        def put(q, i):
            nc.vector.tensor_copy(state[i][:].indirect(listed(q, q + 1)), new_at.get((q, i), picked(i, i + 1, q, q + 1)[:, 0]))

        def put_fused(lo, hi, i, moved):
            nc.vector.tensor_tensor(state[i][:].indirect(offsets[:, lo // 16 : hi // 16]), picks[:, S * i + lo : S * i + hi], moved, ALU.add)

        def store(i):
            nc.sync.dma_start(out[P * i : P * (i + 1), :], state[i][:])

        def work(name, slot, width):
            return keep.tile([P, width], F32, name=name, tag=slot, align_bytes=ALIGN)[:]

        def pair(name, slot):
            both_inputs = work(name, slot, UNIT)
            return half(both_inputs, 0), half(both_inputs, 1)

        gather_words(0, 0, S)
        nc.vector.tensor_copy(tab_s[P // 2 : P, 0, :].bitcast(I32), tab_s[0 : P // 2, 1, :].bitcast(I32))
        nc.vector.tensor_copy(v_s[:], tab_s[:, 0, :].indirect(offsets[:]))
        quantise_w1(0, 0)
        gather_words(1, 0, S)
        quantise_w1(1, 0)
        quantise_w1(2, 0)
        gather_words(2, P, QUARTER)
        gather_words(2, 0, P)
        gather_words(2, QUARTER, S)
        for a in range(K_PASSES):
            for q in range(QUARTERS):
                for u in (1, 0):
                    multiply(q, 0, u, 2 * q + u, (a,))

        def whole_unit(q, b, h, f):
            for u in range(2):
                squares(q, b, u, f)
            for u in range(2):
                copy_h(q, b, u, h)
            factor(f, f, b)
            product(q, b, 0, 2, h, f)

        def unit_inputs(name, slot):
            both_inputs = work(name, slot, 2 * UNIT)
            return both_inputs[:, 0:UNIT], both_inputs[:, UNIT:]

        first = (arena[:, 37 * KB // 4 : 45 * KB // 4], arena[:, 29 * KB // 4 : 37 * KB // 4])
        for u in (1, 0):
            plane_squares(0, 0, u, first[u])
        for u in (1, 0):
            planes = first[u].rearrange("p (t j) -> p t j", t=PACK)
            scale_planes(planes, planes, 0)
        quantise_w1(0, 1)
        for u in (1, 0):
            vector_product(0, 0, u, first[u])
        quantise_w1(1, 1)
        quantise_z(0, "z_w0", "z_s0", (0,))
        quantise_rounded(1)
        quantise_w1(2, 1)
        pick(3, 0, QUARTERS)
        pick(2, 0, QUARTERS)
        whole_unit(1, 0, *unit_inputs("work10", "raw00"))
        whole_unit(2, 0, *unit_inputs("work20", "raw10"))

        multiply_both(0, 1, (0, 1), (0, 1))
        multiply_both(1, 1, (2, 3), (0, 1))
        for u in (1, 0):
            multiply(0, 1, u, u, (2,))
        multiply_both(1, 1, (2, 3), (2,))
        work11 = work("work11", "raw20", 2 * UNIT)
        f11, h11, square01 = work11[:, 0:UNIT], work11[:, UNIT:], work11[:, UNIT:]
        spread = picks[:, S - QUARTER : S + 5 * QUARTER].rearrange("p (u x) -> p u x", u=2)[:, :, 0:BANK]
        for u in (1, 0):
            plane_squares(0, 1, u, half(square01, u))
        squares(1, 1, 0, f11)
        scale_planes(spread.rearrange("p u (t j) -> p t u j", t=PACK), square01.rearrange("p (u t j) -> p t u j", u=2, t=PACK), 1)
        for u in (1, 0):
            vector_product(0, 1, u, spread[:, u])
        pick(1, 3, QUARTERS)
        quantise_z(0, "z_w0", "z_s0", (1,))
        pick(1, 0, 3)
        pick(0, 0, QUARTERS)

        squares(1, 1, 1, f11)
        for u in range(2):
            copy_h(1, 1, u, h11)
        factor(f11, f11, 1)
        product(1, 1, 0, 2, h11, f11)
        multiply(2, 1, 0, 2)
        h21, f21 = unit_inputs("work21", "raw01")
        squares(2, 1, 0, f21)
        copy_h(2, 1, 0, h21)
        top = moved_tile(0, 3, 4, "top0")
        middle = moved_tile(0, 1, 3, "middle0")
        lowest = moved_tile(0, 0, 1, "lowest0")
        drive(0, (3,), 5)
        drive(0, (2, 1), 0)
        drive(0, (0,), 1)
        add_in_place(0, 3, 4, top)
        add_in_place(0, 1, 3, middle)
        put(0, 3)
        quantise_z(1, "middle0", "z_s1")
        add_into(0, 0, 1, lowest, at(17, 18))
        for i in (2, 1, 0):
            put(0, i)

        multiply(2, 1, 1, 5)
        squares(2, 1, 1, f21)
        copy_h(2, 1, 1, h21)
        factor(f21, f21, 1)
        product(2, 1, 0, 2, h21, f21)
        square30 = work("square30", "top0", UNIT)
        for u in range(2):
            squares(3, 0, u, square30)
        top = moved_tile(1, 3, 4, "top1")
        lower = moved_tile(1, 0, 3, "lower1")
        drive(1, (3,), 0)
        drive(1, (2, 1), 1)
        drive(1, (0,), 2)
        add_in_place(1, 3, 4, top)
        add_in_place(1, 0, 3, lower)
        put(1, 3)
        quantise_z(2, "lower1", "z_s2")
        for i in (2, 1, 0):
            put(1, i)

        h30, f30 = unit_inputs("work30", "raw01")
        for u in range(2):
            copy_h(3, 0, u, h30)
        factor(f30, square30, 0)
        product(3, 0, 0, 2, h30, f30)
        multiply_both(3, 1, (1, 2))
        h31, f31 = unit_inputs("work31", "top1")
        for u in range(2):
            squares(3, 1, u, f31)
        for u in range(2):
            copy_h(3, 1, u, h31)
        top = moved_in(2, 3, 4, at(6, 7))
        drive(2, (3,), 3)
        factor(f31, f31, 1)
        add_in_place(2, 3, 4, top)
        put(2, 3)
        product(3, 1, 0, 2, h31, f31)
        quantise_z(3, "z3", "z_s3")

        late = work("late", "top1", 5 * QUARTER)
        moved_at[2, 2] = late[:, 0:QUARTER]
        both = {i: late[:, QUARTER * (1 + 2 * i) : QUARTER * (3 + 2 * i)] for i in (1, 0)}
        for i in (1, 0):
            moved_at[2, i], moved_at[3, i] = both[i][:, 0:QUARTER], both[i][:, QUARTER:]
        moved_tile(3, 2, N_TILES, "last")
        drive(2, (2,), 5)
        put_fused(2 * QUARTER, 3 * QUARTER, 2, moved_at[2, 2])
        drive(2, (1, 0), 3)
        put_fused(2 * QUARTER, 2 * QUARTER + P, 1, both[1][:, 0:P])
        drive(3, (3,), 6)
        drive(3, (2,), 7)
        drive(3, (1, 0), 4)
        for i in (3, 2):
            put_fused(3 * QUARTER, S, i, moved_at[3, i])
            store(i)
        put_fused(2 * QUARTER + P, S, 1, both[1][:, P:])
        store(1)
        put_fused(2 * QUARTER, S, 0, both[0])
        store(0)
